import numpy as np
import ml_dtypes


def mxq(x, axis, fmt="e4m3"):
    dtype, down = {"e4m3": (ml_dtypes.float8_e4m3fn, 7), "e5m2": (ml_dtypes.float8_e5m2, 14)}[fmt]
    v = np.moveaxis(np.asarray(x, np.float32).astype(ml_dtypes.bfloat16).astype(np.float64), axis, -1)
    blocks = v.reshape(v.shape[:-1] + (-1, 32))
    amax = np.abs(blocks).max(-1, keepdims=True)
    byte = np.maximum(np.where(amax > 0, np.frexp(amax)[1] - 1 + 127, 0) - down, 1)
    scale = np.exp2(byte - 127.0)
    codes = (blocks / scale).astype(np.float32).astype(dtype).astype(np.float64)
    return np.moveaxis((codes * scale).reshape(v.shape), -1, axis)


WIDE = False


def mx_kscale(k):
    if not WIDE:
        return np.ones(k)
    levels = np.array([24, -24, 12, -12, 0])
    if k % 512:
        return np.exp2(np.random.permutation(np.resize(levels, k // 32))).repeat(32)
    a = np.empty((k // 512, 16))
    for p in range(k // 512):
        a[p, :8] = np.random.permutation(np.resize(levels, 8))
        for g in range(8):
            far = levels[np.abs(levels - a[p, g]) >= 10]
            a[p, g + 8] = far[np.random.randint(len(far))]
    return np.exp2(a.ravel()).repeat(32)


def f64(x):
    return np.asarray(x).astype(np.float64)


E2M1 = np.array([0.0, 0.5, 1.0, 1.5, 2.0, 3.0, 4.0, 6.0, -0.0, -0.5, -1.0, -1.5, -2.0, -3.0, -4.0, -6.0])


def pack_weight(w, fmt):
    k, n = w.shape
    w = f64(np.asarray(w, np.float32).astype(ml_dtypes.bfloat16)).reshape(k // 32, 32, n)
    amax = np.abs(w).max(1)
    if fmt == "e4m3":
        byte = np.frexp(amax)[1] - 1 + 127 - 7
    else:
        mant, ex = np.frexp(amax / 6.0)
        byte = np.where(mant > 0.5, ex, ex - 1) + 127
    byte = np.clip(np.where(amax > 0, byte, 1), 1, 254)
    scaled = (w * np.exp2(127.0 - byte)[:, None, :]).reshape(k, n).astype(np.float32)
    by_word = np.ascontiguousarray(scaled.reshape(k // 512, 128, 4, n).transpose(0, 1, 3, 2))
    if fmt == "e4m3":
        words = by_word.astype(ml_dtypes.float8_e4m3fn).view(np.uint8)
    else:
        c = by_word.astype(ml_dtypes.float4_e2m1fn).view(np.uint8) & 0xF
        words = (c[..., 0::2] | (c[..., 1::2] << 4)).reshape(k // 512, 128, 2 * n)
    return np.ascontiguousarray(words), np.ascontiguousarray(byte.astype(np.uint8).reshape(k // 512, 16, n))


def unpack_weight(words, scales, fmt):
    g, _, n = scales.shape
    words = np.ascontiguousarray(words).reshape(g, 128, n, -1)
    if fmt == "e4m3":
        vals = words.view(ml_dtypes.float8_e4m3fn).astype(np.float64)
    else:
        nib = np.empty((g, 128, n, 4), np.uint8)
        nib[..., 0::2] = words & 0xF
        nib[..., 1::2] = words >> 4
        vals = E2M1[nib]
    vals = vals * np.repeat(np.exp2(scales.astype(np.float64) - 127.0), 8, axis=1)[..., None]
    return vals.transpose(0, 1, 3, 2).reshape(g * 512, n)


K, J, N, T = 512, 1024, 512, 512


def setup_inputs():
    n = np.random.standard_normal
    u = mx_kscale(J)[:, None]
    s = mx_kscale(K)[:, None]
    w = n((K, J)) / np.sqrt(K) / s * 0.4
    w4 = pack_weight(w, "e2m1")
    rest = w - unpack_weight(*w4, "e2m1")
    p_r8 = pack_weight(rest, "e4m3")
    p_v8 = pack_weight(n((J, N)) / np.sqrt(J) / u, "e4m3")
    return {
        "x": (n((K, T)) * s).astype(np.float32),
        "w4_words": w4[0],
        "w4_scales": w4[1],
        "r8_words": p_r8[0],
        "r8_scales": p_r8[1],
        "cw": (np.random.uniform(0.5, 2.0, J) * u[:, 0]).astype(np.float32),
        "cb": (0.3 * n(J)).astype(np.float32),
        "v8_words": p_v8[0],
        "v8_scales": p_v8[1],
        "b": (0.3 * n(N)).astype(np.float32),
    }


def reference(x, w4_words, w4_scales, r8_words, r8_scales, cw, cb, v8_words, v8_scales, b):
    x_ = mxq(f64(x), 0, "e4m3")
    w4_ = unpack_weight(w4_words, w4_scales, "e2m1")
    r8_ = unpack_weight(r8_words, r8_scales, "e4m3")
    d = w4_.T @ x_ + r8_.T @ x_
    h = f64(cw)[:, None] * (d + f64(cb)[:, None]) ** 2
    h_ = mxq(h, 0, "e4m3")
    v8_ = unpack_weight(v8_words, v8_scales, "e4m3")
    y = v8_.T @ h_
    return y + f64(b)[:, None]

@@ -1,0 +1,303 @@
+from contextlib import ExitStack
+
+import concourse.mybir as mybir
+
+K, J, N, T = 512, 1024, 512, 512
+FLOPS = 2 * (2 * K * J * T + J * N * T)
+
+F32 = mybir.dt.float32
+BF16 = mybir.dt.bfloat16
+I32 = mybir.dt.int32
+U32 = mybir.dt.uint32
+U8 = mybir.dt.uint8
+FP8X4 = mybir.dt.float8_e4m3fn_x4
+FP4X4 = mybir.dt.float4_e2m1fn_x4
+ACT = mybir.ActivationFunctionType
+ALU = mybir.AluOpType
+
+P = 128
+PACK = 4
+PASS = P * PACK
+J_PASSES = J // PASS
+N_TILES = N // P
+CHUNKS = (128, 256, 128)
+W4_ROW, R8_ROW, V8_ROW = 0, 4, 8
+FP4_N = 128
+
+
+def tile_mix_kern_resid_poly2_bias_kernel(
+    tc, x, w4_words, w4_scales, r8_words, r8_scales, cw, cb, v8_words, v8_scales, b, out
+):
+    nc = tc.nc
+    starts = [sum(CHUNKS[:c]) for c in range(len(CHUNKS))]
+    units = [(c, a) for c in range(len(CHUNKS)) for a in range(J_PASSES)]
+
+    with ExitStack() as ctx:
+        sb = ctx.enter_context(tc.tile_pool(name="sb", bufs=1))
+        ps = ctx.enter_context(tc.psum_pool(name="ps", bufs=1))
+        ctx.enter_context(tc.manual_schedule())
+
+        def tiles(name, count, shape_of, dtype):
+            return [sb.tile(shape_of(n), dtype, name="%s%d" % (name, n), align_bytes=64) for n in range(count)]
+
+        n_chunks = len(CHUNKS)
+        scales_in = sb.tile([P, J], U8, name="scales_in", align_bytes=64)
+        scales_by_slot = tiles("scales_by_slot", J_PASSES, lambda a: [P, PASS], U8)
+        w4_in = sb.tile([P, 2 * J], U8, name="w4_in", align_bytes=64)
+        w4_by_slot = tiles("w4_by_slot", J_PASSES, lambda a: [P, 2 * PASS], U8)
+        r8_in = tiles("r8_in", J_PASSES, lambda a: [P, PASS], I32)
+        r8_by_slot = tiles("r8_by_slot", J_PASSES, lambda a: [P, PASS], I32)
+        v8_sb = sb.tile([P, J_PASSES * N], I32, name="v8_sb", align_bytes=64)
+        cw_sb = sb.tile([P, J_PASSES * PACK], F32, name="cw_sb", align_bytes=64)
+        cb_sb = sb.tile([P, J_PASSES * PACK], F32, name="cb_sb", align_bytes=64)
+        b_sb = sb.tile([P, N_TILES], F32, name="b_sb", align_bytes=64)
+        x_in = tiles("x_in", n_chunks, lambda c: [P, PACK, CHUNKS[c]], F32)
+        x_bf = tiles("x_bf", n_chunks, lambda c: [P, PACK * CHUNKS[c]], BF16)
+        x_codes = tiles("x_codes", n_chunks, lambda c: [P, CHUNKS[c]], U32)
+        x_scales = tiles("x_scales", n_chunks, lambda c: [P, CHUNKS[c]], U8)
+        n_units = len(units)
+        width_of = lambda u: CHUNKS[units[u][0]]
+        squares = tiles("squares", n_units, lambda u: [P, PACK, width_of(u)], F32)
+        h_bf = tiles("h_bf", n_units, lambda u: [P, PACK * width_of(u)], BF16)
+        h_codes = tiles("h_codes", n_units, lambda u: [P, width_of(u)], U32)
+        h_scales = tiles("h_scales", n_units, lambda u: [P, width_of(u)], U8)
+        y_sb = tiles("y_sb", 2 * n_chunks, lambda n: [P, 2, CHUNKS[n // 2]], F32)
+
+        def load_x(c):
+            cols = slice(starts[c], starts[c] + CHUNKS[c])
+            nc.sync.dma_start(out=x_in[c][:], in_=x[:, cols].rearrange("(p j) t -> p j t", j=PACK))
+
+        def load_scale_rows(rows, first_row, quadrant):
+            lo = 32 * quadrant + first_row
+            nc.sync.dma_start(
+                out=scales_in[lo : lo + 4, :].bitcast(I32),
+                in_=rows[4 * quadrant : 4 * quadrant + 4, :].bitcast(I32),
+            )
+
+        def load_v8_scale_rows(quadrant):
+            lo = 32 * quadrant + V8_ROW
+            nc.sync.dma_start(
+                out=scales_in[lo : lo + 4, :].bitcast(I32).rearrange("r (a n) -> r a n", a=J_PASSES),
+                in_=v8_scales[:, 4 * quadrant : 4 * quadrant + 4, :].bitcast(I32).rearrange("a r n -> r a n"),
+            )
+
+        def load_w4():
+            nc.sync.dma_start(out=w4_in[:].bitcast(I32), in_=w4_words[0].bitcast(I32))
+
+        def load_r8(a):
+            flat = r8_words[0].rearrange("p j i -> p (j i)")
+            nc.sync.dma_start(out=r8_in[a][:], in_=flat[:, 4 * PASS * a : 4 * PASS * (a + 1)].bitcast(I32))
+
+        def sort_w4(a):
+            nc.vector.tensor_copy(
+                out=w4_by_slot[a][:].rearrange("p (i m e) -> p i m e", i=PACK, e=2),
+                in_=w4_in[:, 2 * PASS * a : 2 * PASS * (a + 1)].rearrange("p (m i e) -> p i m e", i=PACK, e=2),
+            )
+
+        def sort_r8(a):
+            nc.vector.tensor_copy(
+                out=r8_by_slot[a][:].rearrange("p (i m e) -> p m i e", i=PACK, e=2),
+                in_=r8_in[a][:].rearrange("p (m e i) -> p m i e", i=PACK, e=2),
+            )
+
+        def sort_scales(a):
+            nc.vector.tensor_copy(
+                out=scales_by_slot[a][:].rearrange("p (i m) -> p i m", i=PACK),
+                in_=scales_in[:, PASS * a : PASS * (a + 1)].rearrange("p (m i) -> p i m", i=PACK),
+            )
+
+        def interleaved(dst):
+            return dst[:].rearrange("p (m e i) -> p m i e", i=PACK, e=2)
+
+        def by_rows(src):
+            return src[:].rearrange("p i (m e) -> p m i e", e=2)
+
+        def quantize(codes, scales, values):
+            nc.vector.quantize_mx(out=codes[:].bitcast(FP8X4), scales=scales[:], in_=values[:])
+
+        d_banks = {}
+
+        def first_product(u):
+            c, a = units[u]
+            width = CHUNKS[c]
+            for half in range(2):
+                bank = ps.tile([P, 2, width], F32, name="d%d" % (2 * u + half), tag="bank", bufs=8)
+                d_banks[u, half] = bank
+                for e in range(2):
+                    i = 2 * half + e
+                    for t0 in range(0, width, FP4_N):
+                        nc.tensor.matmul_mx(
+                            out=bank[:, e, t0 : t0 + FP4_N],
+                            lhsT=w4_by_slot[a][:, 2 * P * i : 2 * P * (i + 1)].bitcast(FP4X4),
+                            lhsT_scale=scales_by_slot[a][W4_ROW:, P * i : P * (i + 1)],
+                            rhs=x_codes[c][:, t0 : t0 + FP4_N].bitcast(FP8X4),
+                            rhs_scale=x_scales[c][:, t0 : t0 + FP4_N],
+                            start=(t0 == 0),
+                            stop=False,
+                        )
+                    nc.tensor.matmul_mx(
+                        out=bank[:, e, :],
+                        lhsT=r8_by_slot[a][:, P * i : P * (i + 1)].bitcast(FP8X4),
+                        lhsT_scale=scales_by_slot[a][R8_ROW:, P * i : P * (i + 1)],
+                        rhs=x_codes[c][:].bitcast(FP8X4),
+                        rhs_scale=x_scales[c][:],
+                        start=False,
+                        stop=True,
+                    )
+
+        def square(u):
+            c, a = units[u]
+            for i in range(PACK):
+                col = PACK * a + i
+                nc.scalar.activation(
+                    out=squares[u][:, i, :],
+                    in_=d_banks[u, i // 2][:, i % 2, :],
+                    func=ACT.Square,
+                    bias=cb_sb[:, col : col + 1],
+                )
+
+        def weigh(u):
+            c, a = units[u]
+            pairs = CHUNKS[c] // 2
+            weights = cw_sb[:, PACK * a : PACK * (a + 1)].unsqueeze(1).unsqueeze(3).to_broadcast([P, pairs, PACK, 2])
+            nc.vector.tensor_tensor(out=interleaved(h_bf[u]), in0=by_rows(squares[u]), in1=weights, op=ALU.mult)
+
+        y_banks = {}
+
+        def second_product(u):
+            c, a = units[u]
+            for half in range(2):
+                if a == 0:
+                    y_banks[c, half] = ps.tile([P, 2, CHUNKS[c]], F32, name="y%d" % (2 * c + half), tag="bank", bufs=8)
+                for e in range(2):
+                    cols = slice(N * a + P * (2 * half + e), N * a + P * (2 * half + e + 1))
+                    nc.tensor.matmul_mx(
+                        out=y_banks[c, half][:, e, :],
+                        lhsT=v8_sb[:, cols].bitcast(FP8X4),
+                        lhsT_scale=scales_in[V8_ROW:, cols],
+                        rhs=h_codes[u][:].bitcast(FP8X4),
+                        rhs_scale=h_scales[u][:],
+                        start=(a == 0 and e == 0),
+                        stop=(a == J_PASSES - 1 and e == 1),
+                    )
+
+        out_tiles = out.rearrange("(n p) t -> p n t", p=P)
+
+        def bias_on_scalar(c, half):
+            for e in range(2):
+                col = 2 * half + e
+                nc.scalar.activation(
+                    out=y_sb[2 * c + half][:, e, :],
+                    in_=y_banks[c, half][:, e, :],
+                    func=ACT.Identity,
+                    bias=b_sb[:, col : col + 1],
+                )
+
+        def bias_on_vector(c, half):
+            biases = b_sb[:, 2 * half : 2 * half + 2].unsqueeze(2).to_broadcast([P, 2, CHUNKS[c]])
+            nc.vector.tensor_tensor(out=y_sb[2 * c + half][:], in0=y_banks[c, half][:], in1=biases, op=ALU.add)
+
+        def store(queue, c, half):
+            queue.dma_start(
+                out=out_tiles[:, 2 * half : 2 * half + 2, starts[c] : starts[c] + CHUNKS[c]], in_=y_sb[2 * c + half][:]
+            )
+
+        def load_by_slot(dst, vec):
+            nc.sync.dma_start(
+                out=dst[:].rearrange("p (a i) -> p a i", i=PACK), in_=vec.rearrange("(a p i) -> p a i", p=P, i=PACK)
+            )
+
+        def quantize_x(c):
+            quantize(x_codes[c], x_scales[c], x_bf[c])
+
+        def quantize_h(u):
+            quantize(h_codes[u], h_scales[u], h_bf[u])
+
+        def cast_on_scalar(c):
+            nc.scalar.activation(out=interleaved(x_bf[c]), in_=by_rows(x_in[c]), func=ACT.Copy)
+
+        def cast_on_vector(c):
+            nc.vector.tensor_copy(out=interleaved(x_bf[c]), in_=by_rows(x_in[c]))
+
+        def load_v8():
+            nc.sync.dma_start(
+                out=v8_sb[:].rearrange("p (a n) -> p a n", a=J_PASSES),
+                in_=v8_words.rearrange("a p n i -> p a (n i)").bitcast(I32),
+            )
+
+        def load_b():
+            with nc.allow_non_contiguous_dma(reason="one bias value for each partition"):
+                nc.sync.dma_start(out=b_sb[:], in_=b.rearrange("(n p) -> p n", p=P))
+
+        def finish_on_scalar(c):
+            for half in range(2):
+                bias_on_scalar(c, half)
+                store(nc.sync, c, half)
+
+        nc.vector.memset(scales_in[:].bitcast(I32), 0)
+        load_x(0)
+        for q in range(4):
+            load_scale_rows(w4_scales[0], W4_ROW, q)
+        load_scale_rows(r8_scales[0], R8_ROW, 0)
+        load_w4()
+        load_r8(0)
+        for q in range(1, 4):
+            load_scale_rows(r8_scales[0], R8_ROW, q)
+        load_by_slot(cb_sb, cb)
+        load_r8(1)
+        load_x(1)
+        load_by_slot(cw_sb, cw)
+        load_x(2)
+        load_v8()
+
+        cast_on_scalar(0)
+        sort_w4(0)
+        quantize_x(0)
+        sort_r8(0)
+        sort_w4(1)
+        sort_scales(0)
+        first_product(0)
+        sort_scales(1)
+        sort_r8(1)
+        for q in range(4):
+            load_v8_scale_rows(q)
+        load_b()
+        first_product(1)
+        square(0)
+        cast_on_vector(1)
+        weigh(0)
+        quantize_x(1)
+        square(1)
+        first_product(2)
+        first_product(3)
+        cast_on_scalar(2)
+        weigh(1)
+        quantize_x(2)
+        quantize_h(0)
+        quantize_h(1)
+        square(2)
+        second_product(0)
+        second_product(1)
+        first_product(4)
+        square(3)
+        first_product(5)
+        finish_on_scalar(0)
+        weigh(2)
+        weigh(3)
+        quantize_h(2)
+        quantize_h(3)
+        square(4)
+        square(5)
+        second_product(2)
+        second_product(3)
+        finish_on_scalar(1)
+        weigh(4)
+        weigh(5)
+        quantize_h(4)
+        quantize_h(5)
+        second_product(4)
+        second_product(5)
+        bias_on_scalar(2, 0)
+        bias_on_vector(2, 1)
+        store(nc.scalar, 2, 0)
+        store(nc.sync, 2, 1)

@@ -20,73 +20,65 @@ PACK = 4
 PASS = P * PACK
 J_PASSES = J // PASS
 N_TILES = N // P
-CHUNKS = (128, 256, 128)
-W4_ROW, R8_ROW, V8_ROW = 0, 4, 8
-FP4_N = 128
+CHUNK = 128
+CHUNKS = T // CHUNK
+UNITS = CHUNKS * J_PASSES
+X_LOADS = ((0, 128), (128, 128), (256, 256))
+R8_ROW, V8_ROW = 0, 4
+PSUM_BANKS = 8
 
 
 def tile_mix_kern_resid_poly2_bias_kernel(
     tc, x, w4_words, w4_scales, r8_words, r8_scales, cw, cb, v8_words, v8_scales, b, out
 ):
     nc = tc.nc
-    starts = [sum(CHUNKS[:c]) for c in range(len(CHUNKS))]
-    units = [(c, a) for c in range(len(CHUNKS)) for a in range(J_PASSES)]
 
     with ExitStack() as ctx:
         sb = ctx.enter_context(tc.tile_pool(name="sb", bufs=1))
         ps = ctx.enter_context(tc.psum_pool(name="ps", bufs=1))
         ctx.enter_context(tc.manual_schedule())
 
-        def tiles(name, count, shape_of, dtype):
-            return [sb.tile(shape_of(n), dtype, name="%s%d" % (name, n), align_bytes=64) for n in range(count)]
+        def tiles(name, shapes, dtype):
+            return [sb.tile(shape, dtype, name="%s%d" % (name, n), align_bytes=64) for n, shape in enumerate(shapes)]
 
-        n_chunks = len(CHUNKS)
-        scales_in = sb.tile([P, J], U8, name="scales_in", align_bytes=64)
-        scales_by_slot = tiles("scales_by_slot", J_PASSES, lambda a: [P, PASS], U8)
+        w4_scales_in = sb.tile([P, J], U8, name="w4_scales_in", align_bytes=64)
+        e4m3_scales_in = sb.tile([P, J], U8, name="e4m3_scales_in", align_bytes=64)
+        w4_scales_by_slot = tiles("w4_scales_by_slot", [[P, PASS]] * J_PASSES, U8)
+        r8_scales_by_slot = tiles("r8_scales_by_slot", [[P, PASS]] * J_PASSES, U8)
         w4_in = sb.tile([P, 2 * J], U8, name="w4_in", align_bytes=64)
-        w4_by_slot = tiles("w4_by_slot", J_PASSES, lambda a: [P, 2 * PASS], U8)
-        r8_in = tiles("r8_in", J_PASSES, lambda a: [P, PASS], I32)
-        r8_by_slot = tiles("r8_by_slot", J_PASSES, lambda a: [P, PASS], I32)
+        w4_by_slot = tiles("w4_by_slot", [[P, 2 * PASS]] * J_PASSES, U8)
+        r8_in = sb.tile([P, J], I32, name="r8_in", align_bytes=64)
+        r8_by_slot = tiles("r8_by_slot", [[P, PASS]] * J_PASSES, I32)
         v8_sb = sb.tile([P, J_PASSES * N], I32, name="v8_sb", align_bytes=64)
         cw_sb = sb.tile([P, J_PASSES * PACK], F32, name="cw_sb", align_bytes=64)
         cb_sb = sb.tile([P, J_PASSES * PACK], F32, name="cb_sb", align_bytes=64)
         b_sb = sb.tile([P, N_TILES], F32, name="b_sb", align_bytes=64)
-        x_in = tiles("x_in", n_chunks, lambda c: [P, PACK, CHUNKS[c]], F32)
-        x_bf = tiles("x_bf", n_chunks, lambda c: [P, PACK * CHUNKS[c]], BF16)
-        x_codes = tiles("x_codes", n_chunks, lambda c: [P, CHUNKS[c]], U32)
-        x_scales = tiles("x_scales", n_chunks, lambda c: [P, CHUNKS[c]], U8)
-        n_units = len(units)
-        width_of = lambda u: CHUNKS[units[u][0]]
-        squares = tiles("squares", n_units, lambda u: [P, PACK, width_of(u)], F32)
-        h_bf = tiles("h_bf", n_units, lambda u: [P, PACK * width_of(u)], BF16)
-        h_codes = tiles("h_codes", n_units, lambda u: [P, width_of(u)], U32)
-        h_scales = tiles("h_scales", n_units, lambda u: [P, width_of(u)], U8)
-        y_sb = tiles("y_sb", 2 * n_chunks, lambda n: [P, 2, CHUNKS[n // 2]], F32)
+        x_in = tiles("x_in", [[P, PACK, w] for t0, w in X_LOADS], F32)
+        x_bf = tiles("x_bf", [[P, PACK * w] for t0, w in X_LOADS], BF16)
+        x_codes = sb.tile([P, T], U32, name="x_codes", align_bytes=64)
+        x_scales = sb.tile([P, T], U8, name="x_scales", align_bytes=64)
+        squares = tiles("squares", [[P, PACK, CHUNK]] * UNITS, F32)
+        h_bf = tiles("h_bf", [[P, PACK * CHUNK]] * UNITS, BF16)
+        h_codes = tiles("h_codes", [[P, CHUNK]] * UNITS, U32)
+        h_scales = tiles("h_scales", [[P, CHUNK]] * UNITS, U8)
+        y_sb = tiles("y_sb", [[P, 2, CHUNK]] * (2 * CHUNKS), F32)
 
-        def load_x(c):
-            cols = slice(starts[c], starts[c] + CHUNKS[c])
-            nc.sync.dma_start(out=x_in[c][:], in_=x[:, cols].rearrange("(p j) t -> p j t", j=PACK))
+        def load_x(n):
+            t0, w = X_LOADS[n]
+            nc.sync.dma_start(out=x_in[n][:], in_=x[:, t0 : t0 + w].rearrange("(p j) t -> p j t", j=PACK))
 
-        def load_scale_rows(rows, first_row, quadrant):
-            lo = 32 * quadrant + first_row
-            nc.sync.dma_start(
-                out=scales_in[lo : lo + 4, :].bitcast(I32),
-                in_=rows[4 * quadrant : 4 * quadrant + 4, :].bitcast(I32),
+        def load_scale_rows(plane, first_row, rows):
+            for q in range(4):
+                lo = 32 * q + first_row
+                nc.sync.dma_start(
+                    out=plane[lo : lo + 4, :].bitcast(I32).rearrange("r (a n) -> r a n", a=rows.shape[0]),
+                    in_=rows[:, 4 * q : 4 * q + 4, :].bitcast(I32).rearrange("a r n -> r a n"),
+                )
+
+        def load_by_slot(queue, dst, vec):
+            queue.dma_start(
+                out=dst[:].rearrange("p (a i) -> p a i", i=PACK), in_=vec.rearrange("(a p i) -> p a i", p=P, i=PACK)
             )
-
-        def load_v8_scale_rows(quadrant):
-            lo = 32 * quadrant + V8_ROW
-            nc.sync.dma_start(
-                out=scales_in[lo : lo + 4, :].bitcast(I32).rearrange("r (a n) -> r a n", a=J_PASSES),
-                in_=v8_scales[:, 4 * quadrant : 4 * quadrant + 4, :].bitcast(I32).rearrange("a r n -> r a n"),
-            )
-
-        def load_w4():
-            nc.sync.dma_start(out=w4_in[:].bitcast(I32), in_=w4_words[0].bitcast(I32))
-
-        def load_r8(a):
-            flat = r8_words[0].rearrange("p j i -> p (j i)")
-            nc.sync.dma_start(out=r8_in[a][:], in_=flat[:, 4 * PASS * a : 4 * PASS * (a + 1)].bitcast(I32))
 
         def sort_w4(a):
             nc.vector.tensor_copy(
@@ -96,14 +88,14 @@ def tile_mix_kern_resid_poly2_bias_kernel(
 
         def sort_r8(a):
             nc.vector.tensor_copy(
-                out=r8_by_slot[a][:].rearrange("p (i m e) -> p m i e", i=PACK, e=2),
-                in_=r8_in[a][:].rearrange("p (m e i) -> p m i e", i=PACK, e=2),
+                out=r8_by_slot[a][:].rearrange("p (i m e) -> p m i e", i=PACK, e=4),
+                in_=r8_in[:, PASS * a : PASS * (a + 1)].rearrange("p (m e i) -> p m i e", i=PACK, e=4),
             )
 
-        def sort_scales(a):
+        def sort_scales(dst, plane, a):
             nc.vector.tensor_copy(
-                out=scales_by_slot[a][:].rearrange("p (i m) -> p i m", i=PACK),
-                in_=scales_in[:, PASS * a : PASS * (a + 1)].rearrange("p (m i) -> p i m", i=PACK),
+                out=dst[a][:].rearrange("p (i m) -> p i m", i=PACK),
+                in_=plane[:, PASS * a : PASS * (a + 1)].rearrange("p (m i) -> p i m", i=PACK),
             )
 
         def interleaved(dst):
@@ -112,41 +104,53 @@ def tile_mix_kern_resid_poly2_bias_kernel(
         def by_rows(src):
             return src[:].rearrange("p i (m e) -> p m i e", e=2)
 
-        def quantize(codes, scales, values):
-            nc.vector.quantize_mx(out=codes[:].bitcast(FP8X4), scales=scales[:], in_=values[:])
+        def quantize_x(n):
+            t0, w = X_LOADS[n]
+            nc.vector.quantize_mx(
+                out=x_codes[:, t0 : t0 + w].bitcast(FP8X4), scales=x_scales[:, t0 : t0 + w], in_=x_bf[n][:]
+            )
+
+        def quantize_h(u):
+            nc.vector.quantize_mx(out=h_codes[u][:].bitcast(FP8X4), scales=h_scales[u][:], in_=h_bf[u][:])
 
         d_banks = {}
 
+        def w4_pass(u, i):
+            c, a = divmod(u, J_PASSES)
+            if i % 2 == 0:
+                d_banks[u, i // 2] = ps.tile(
+                    [P, 2, CHUNK], F32, name="d%d_%d" % (u, i // 2), tag="bank", bufs=PSUM_BANKS
+                )
+            nc.tensor.matmul_mx(
+                out=d_banks[u, i // 2][:, i % 2, :],
+                lhsT=w4_by_slot[a][:, 2 * P * i : 2 * P * (i + 1)].bitcast(FP4X4),
+                lhsT_scale=w4_scales_by_slot[a][:, P * i : P * (i + 1)],
+                rhs=x_codes[:, CHUNK * c : CHUNK * (c + 1)].bitcast(FP8X4),
+                rhs_scale=x_scales[:, CHUNK * c : CHUNK * (c + 1)],
+                start=(i % 2 == 0),
+                stop=False,
+            )
+
+        def r8_pass(u, i):
+            c, a = divmod(u, J_PASSES)
+            nc.tensor.matmul_mx(
+                out=d_banks[u, i // 2][:, i % 2, :],
+                lhsT=r8_by_slot[a][:, P * i : P * (i + 1)].bitcast(FP8X4),
+                lhsT_scale=r8_scales_by_slot[a][R8_ROW:, P * i : P * (i + 1)],
+                rhs=x_codes[:, CHUNK * c : CHUNK * (c + 1)].bitcast(FP8X4),
+                rhs_scale=x_scales[:, CHUNK * c : CHUNK * (c + 1)],
+                start=False,
+                stop=(i % 2 == 1),
+            )
+
         def first_product(u):
-            c, a = units[u]
-            width = CHUNKS[c]
             for half in range(2):
-                bank = ps.tile([P, 2, width], F32, name="d%d" % (2 * u + half), tag="bank", bufs=8)
-                d_banks[u, half] = bank
-                for e in range(2):
-                    i = 2 * half + e
-                    for t0 in range(0, width, FP4_N):
-                        nc.tensor.matmul_mx(
-                            out=bank[:, e, t0 : t0 + FP4_N],
-                            lhsT=w4_by_slot[a][:, 2 * P * i : 2 * P * (i + 1)].bitcast(FP4X4),
-                            lhsT_scale=scales_by_slot[a][W4_ROW:, P * i : P * (i + 1)],
-                            rhs=x_codes[c][:, t0 : t0 + FP4_N].bitcast(FP8X4),
-                            rhs_scale=x_scales[c][:, t0 : t0 + FP4_N],
-                            start=(t0 == 0),
-                            stop=False,
-                        )
-                    nc.tensor.matmul_mx(
-                        out=bank[:, e, :],
-                        lhsT=r8_by_slot[a][:, P * i : P * (i + 1)].bitcast(FP8X4),
-                        lhsT_scale=scales_by_slot[a][R8_ROW:, P * i : P * (i + 1)],
-                        rhs=x_codes[c][:].bitcast(FP8X4),
-                        rhs_scale=x_scales[c][:],
-                        start=False,
-                        stop=True,
-                    )
+                for one_pass in (w4_pass, r8_pass):
+                    for i in (2 * half, 2 * half + 1):
+                        one_pass(u, i)
 
         def square(u):
-            c, a = units[u]
+            a = u % J_PASSES
             for i in range(PACK):
                 col = PACK * a + i
                 nc.scalar.activation(
@@ -157,28 +161,32 @@ def tile_mix_kern_resid_poly2_bias_kernel(
                 )
 
         def weigh(u):
-            c, a = units[u]
-            pairs = CHUNKS[c] // 2
-            weights = cw_sb[:, PACK * a : PACK * (a + 1)].unsqueeze(1).unsqueeze(3).to_broadcast([P, pairs, PACK, 2])
-            nc.vector.tensor_tensor(out=interleaved(h_bf[u]), in0=by_rows(squares[u]), in1=weights, op=ALU.mult)
+            a = u % J_PASSES
+            weights = cw_sb[:, PACK * a : PACK * (a + 1)].unsqueeze(1).unsqueeze(3)
+            nc.vector.tensor_tensor(
+                out=interleaved(h_bf[u]),
+                in0=by_rows(squares[u]),
+                in1=weights.to_broadcast([P, CHUNK // 2, PACK, 2]),
+                op=ALU.mult,
+            )
 
         y_banks = {}
 
-        def second_product(u):
-            c, a = units[u]
+        def second_product(c):
             for half in range(2):
-                if a == 0:
-                    y_banks[c, half] = ps.tile([P, 2, CHUNKS[c]], F32, name="y%d" % (2 * c + half), tag="bank", bufs=8)
-                for e in range(2):
-                    cols = slice(N * a + P * (2 * half + e), N * a + P * (2 * half + e + 1))
+                y_banks[c, half] = ps.tile([P, 2, CHUNK], F32, name="y%d_%d" % (c, half), tag="bank", bufs=PSUM_BANKS)
+            for a in range(J_PASSES):
+                u = J_PASSES * c + a
+                for n in range(N_TILES):
+                    cols = slice(N * a + P * n, N * a + P * (n + 1))
                     nc.tensor.matmul_mx(
-                        out=y_banks[c, half][:, e, :],
+                        out=y_banks[c, n // 2][:, n % 2, :],
                         lhsT=v8_sb[:, cols].bitcast(FP8X4),
-                        lhsT_scale=scales_in[V8_ROW:, cols],
+                        lhsT_scale=e4m3_scales_in[V8_ROW:, cols],
                         rhs=h_codes[u][:].bitcast(FP8X4),
                         rhs_scale=h_scales[u][:],
-                        start=(a == 0 and e == 0),
-                        stop=(a == J_PASSES - 1 and e == 1),
+                        start=(a == 0 and n % 2 == 0),
+                        stop=(a == J_PASSES - 1 and n % 2 == 1),
                     )
 
         out_tiles = out.rearrange("(n p) t -> p n t", p=P)
@@ -194,110 +202,77 @@ def tile_mix_kern_resid_poly2_bias_kernel(
                 )
 
         def bias_on_vector(c, half):
-            biases = b_sb[:, 2 * half : 2 * half + 2].unsqueeze(2).to_broadcast([P, 2, CHUNKS[c]])
+            biases = b_sb[:, 2 * half : 2 * half + 2].unsqueeze(2).to_broadcast([P, 2, CHUNK])
             nc.vector.tensor_tensor(out=y_sb[2 * c + half][:], in0=y_banks[c, half][:], in1=biases, op=ALU.add)
 
         def store(queue, c, half):
             queue.dma_start(
-                out=out_tiles[:, 2 * half : 2 * half + 2, starts[c] : starts[c] + CHUNKS[c]], in_=y_sb[2 * c + half][:]
+                out=out_tiles[:, 2 * half : 2 * half + 2, CHUNK * c : CHUNK * (c + 1)], in_=y_sb[2 * c + half][:]
             )
-
-        def load_by_slot(dst, vec):
-            nc.sync.dma_start(
-                out=dst[:].rearrange("p (a i) -> p a i", i=PACK), in_=vec.rearrange("(a p i) -> p a i", p=P, i=PACK)
-            )
-
-        def quantize_x(c):
-            quantize(x_codes[c], x_scales[c], x_bf[c])
-
-        def quantize_h(u):
-            quantize(h_codes[u], h_scales[u], h_bf[u])
-
-        def cast_on_scalar(c):
-            nc.scalar.activation(out=interleaved(x_bf[c]), in_=by_rows(x_in[c]), func=ACT.Copy)
-
-        def cast_on_vector(c):
-            nc.vector.tensor_copy(out=interleaved(x_bf[c]), in_=by_rows(x_in[c]))
-
-        def load_v8():
-            nc.sync.dma_start(
-                out=v8_sb[:].rearrange("p (a n) -> p a n", a=J_PASSES),
-                in_=v8_words.rearrange("a p n i -> p a (n i)").bitcast(I32),
-            )
-
-        def load_b():
-            with nc.allow_non_contiguous_dma(reason="one bias value for each partition"):
-                nc.sync.dma_start(out=b_sb[:], in_=b.rearrange("(n p) -> p n", p=P))
 
         def finish_on_scalar(c):
             for half in range(2):
                 bias_on_scalar(c, half)
                 store(nc.sync, c, half)
 
-        nc.vector.memset(scales_in[:].bitcast(I32), 0)
+        nc.gpsimd.memset(w4_scales_in[:].bitcast(I32), 0)
+        nc.gpsimd.memset(e4m3_scales_in[:].bitcast(I32), 0)
+        load_by_slot(nc.gpsimd, cb_sb, cb)
+        nc.sync.dma_start(out=w4_in[:].bitcast(I32), in_=w4_words[0].bitcast(I32))
+        load_scale_rows(w4_scales_in, 0, w4_scales)
         load_x(0)
-        for q in range(4):
-            load_scale_rows(w4_scales[0], W4_ROW, q)
-        load_scale_rows(r8_scales[0], R8_ROW, 0)
-        load_w4()
-        load_r8(0)
-        for q in range(1, 4):
-            load_scale_rows(r8_scales[0], R8_ROW, q)
-        load_by_slot(cb_sb, cb)
-        load_r8(1)
+        nc.sync.dma_start(out=r8_in[:], in_=r8_words[0].rearrange("p j i -> p (j i)").bitcast(I32))
+        load_by_slot(nc.sync, cw_sb, cw)
+        load_scale_rows(e4m3_scales_in, R8_ROW, r8_scales)
         load_x(1)
-        load_by_slot(cw_sb, cw)
         load_x(2)
-        load_v8()
+        nc.sync.dma_start(
+            out=v8_sb[:].rearrange("p (a n) -> p a n", a=J_PASSES),
+            in_=v8_words.rearrange("a p n i -> p a (n i)").bitcast(I32),
+        )
 
-        cast_on_scalar(0)
-        sort_w4(0)
+        nc.scalar.activation(out=interleaved(x_bf[0]), in_=by_rows(x_in[0]), func=ACT.Copy)
+        for a in range(J_PASSES):
+            sort_w4(a)
+            sort_scales(w4_scales_by_slot, w4_scales_in, a)
         quantize_x(0)
+        for i in range(PACK):
+            w4_pass(0, i)
         sort_r8(0)
-        sort_w4(1)
-        sort_scales(0)
-        first_product(0)
-        sort_scales(1)
+        sort_scales(r8_scales_by_slot, e4m3_scales_in, 0)
+        for i in range(PACK):
+            r8_pass(0, i)
         sort_r8(1)
-        for q in range(4):
-            load_v8_scale_rows(q)
-        load_b()
+        sort_scales(r8_scales_by_slot, e4m3_scales_in, 1)
+        load_scale_rows(e4m3_scales_in, V8_ROW, v8_scales)
+        with nc.allow_non_contiguous_dma(reason="one bias value for each partition"):
+            nc.sync.dma_start(out=b_sb[:], in_=b.rearrange("(n p) -> p n", p=P))
         first_product(1)
+        nc.vector.tensor_copy(out=interleaved(x_bf[1]), in_=by_rows(x_in[1]))
         square(0)
-        cast_on_vector(1)
-        weigh(0)
         quantize_x(1)
-        square(1)
         first_product(2)
         first_product(3)
-        cast_on_scalar(2)
-        weigh(1)
-        quantize_x(2)
+        weigh(0)
+        nc.vector.tensor_copy(out=interleaved(x_bf[2]), in_=by_rows(x_in[2]))
         quantize_h(0)
-        quantize_h(1)
-        square(2)
-        second_product(0)
-        second_product(1)
-        first_product(4)
-        square(3)
-        first_product(5)
-        finish_on_scalar(0)
-        weigh(2)
-        weigh(3)
-        quantize_h(2)
-        quantize_h(3)
-        square(4)
-        square(5)
-        second_product(2)
-        second_product(3)
+        quantize_x(2)
+        for u in range(1, UNITS):
+            square(u)
+            if u + 3 < UNITS:
+                first_product(u + 3)
+            if u >= 3 and u % 2 == 1:
+                second_product((u - 3) // 2)
+            if u == UNITS - 2:
+                finish_on_scalar(0)
+            weigh(u)
+            if u >= 2:
+                quantize_h(u - 1)
+        quantize_h(UNITS - 1)
         finish_on_scalar(1)
-        weigh(4)
-        weigh(5)
-        quantize_h(4)
-        quantize_h(5)
-        second_product(4)
-        second_product(5)
-        bias_on_scalar(2, 0)
-        bias_on_vector(2, 1)
-        store(nc.scalar, 2, 0)
-        store(nc.sync, 2, 1)
+        second_product(CHUNKS - 1)
+        finish_on_scalar(2)
+        bias_on_scalar(CHUNKS - 1, 0)
+        bias_on_vector(CHUNKS - 1, 1)
+        store(nc.scalar, CHUNKS - 1, 0)
+        store(nc.sync, CHUNKS - 1, 1)

@@ -16,16 +16,17 @@ ACT = mybir.ActivationFunctionType
 ALU = mybir.AluOpType
 
 P = 128
-PACK = 4
-PASS = P * PACK
+SLOTS = 4
+PASS = P * SLOTS
 J_PASSES = J // PASS
-N_TILES = N // P
-CHUNK = 128
-CHUNKS = T // CHUNK
-UNITS = CHUNKS * J_PASSES
-X_LOADS = ((0, 128), (128, 128), (256, 256))
-R8_ROW, V8_ROW = 0, 4
+QUADRANTS = 4
 PSUM_BANKS = 8
+FP4_COLUMNS = 128
+R8_ROW, V8_ROW = 0, 4
+
+X_LOADS = ((0, 128), (128, 128), (256, 256))
+D_TILES = ((0, 0, 128), (0, 128, 128), (1, 0, 256), (0, 256, 256), (1, 256, 256))
+Y_RANGES = ((0, 256), (256, 128), (384, 128))
 
 
 def tile_mix_kern_resid_poly2_bias_kernel(
@@ -38,241 +39,265 @@ def tile_mix_kern_resid_poly2_bias_kernel(
         ps = ctx.enter_context(tc.psum_pool(name="ps", bufs=1))
         ctx.enter_context(tc.manual_schedule())
 
-        def tiles(name, shapes, dtype):
-            return [sb.tile(shape, dtype, name="%s%d" % (name, n), align_bytes=64) for n, shape in enumerate(shapes)]
+        def one_tile(name, shape, dtype):
+            return sb.tile(shape, dtype, name=name, align_bytes=64)
 
-        w4_scales_in = sb.tile([P, J], U8, name="w4_scales_in", align_bytes=64)
-        e4m3_scales_in = sb.tile([P, J], U8, name="e4m3_scales_in", align_bytes=64)
-        w4_scales_by_slot = tiles("w4_scales_by_slot", [[P, PASS]] * J_PASSES, U8)
-        r8_scales_by_slot = tiles("r8_scales_by_slot", [[P, PASS]] * J_PASSES, U8)
-        w4_in = sb.tile([P, 2 * J], U8, name="w4_in", align_bytes=64)
-        w4_by_slot = tiles("w4_by_slot", [[P, 2 * PASS]] * J_PASSES, U8)
-        r8_in = sb.tile([P, J], I32, name="r8_in", align_bytes=64)
-        r8_by_slot = tiles("r8_by_slot", [[P, PASS]] * J_PASSES, I32)
-        v8_sb = sb.tile([P, J_PASSES * N], I32, name="v8_sb", align_bytes=64)
-        cw_sb = sb.tile([P, J_PASSES * PACK], F32, name="cw_sb", align_bytes=64)
-        cb_sb = sb.tile([P, J_PASSES * PACK], F32, name="cb_sb", align_bytes=64)
-        b_sb = sb.tile([P, N_TILES], F32, name="b_sb", align_bytes=64)
-        x_in = tiles("x_in", [[P, PACK, w] for t0, w in X_LOADS], F32)
-        x_bf = tiles("x_bf", [[P, PACK * w] for t0, w in X_LOADS], BF16)
-        x_codes = sb.tile([P, T], U32, name="x_codes", align_bytes=64)
-        x_scales = sb.tile([P, T], U8, name="x_scales", align_bytes=64)
-        squares = tiles("squares", [[P, PACK, CHUNK]] * UNITS, F32)
-        h_bf = tiles("h_bf", [[P, PACK * CHUNK]] * UNITS, BF16)
-        h_codes = tiles("h_codes", [[P, CHUNK]] * UNITS, U32)
-        h_scales = tiles("h_scales", [[P, CHUNK]] * UNITS, U8)
-        y_sb = tiles("y_sb", [[P, 2, CHUNK]] * (2 * CHUNKS), F32)
+        def tiles(name, shapes, dtype):
+            return [one_tile("%s%d" % (name, n), shape, dtype) for n, shape in enumerate(shapes)]
+
+        def bank(name, shape):
+            return ps.tile(shape, F32, name=name, tag="bank", bufs=PSUM_BANKS)
+
+        w4_plane_in = one_tile("w4_plane_in", [P, J], U8)
+        e4m3_planes_in = one_tile("e4m3_planes_in", [P, J], U8)
+        w4_plane = one_tile("w4_plane", [P, J], U8)
+        r8_plane = tiles("r8_plane", [[P, PASS]] * J_PASSES, U8)
+        w4_in = one_tile("w4_in", [P, 2 * J], U8)
+        w4_sorted = one_tile("w4_sorted", [P, 2 * J], U8)
+        r8_in = tiles("r8_in", [[P, PASS]] * J_PASSES, I32)
+        r8_sorted = tiles("r8_sorted", [[P, PASS]] * J_PASSES, I32)
+        v8_sb = one_tile("v8_sb", [P, J_PASSES * N], I32)
+        cw_sb = one_tile("cw_sb", [P, J_PASSES * SLOTS], F32)
+        cb_sb = one_tile("cb_sb", [P, J_PASSES * SLOTS], F32)
+        b_sb = one_tile("b_sb", [P, N // P], F32)
+        x_in = tiles("x_in", [[P, SLOTS, width] for t0, width in X_LOADS], F32)
+        x_bf = tiles("x_bf", [[P, SLOTS * width] for t0, width in X_LOADS], BF16)
+        x_codes = one_tile("x_codes", [P, T], U32)
+        x_plane = one_tile("x_plane", [P, T], U8)
+        squares = tiles("squares", [[P, SLOTS, width] for a, t0, width in D_TILES], F32)
+        h_bf = tiles("h_bf", [[P, SLOTS * T]] * J_PASSES, BF16)
+        h_codes = tiles("h_codes", [[P, T]] * J_PASSES, U32)
+        h_plane = tiles("h_plane", [[P, T]] * J_PASSES, U8)
+        y_sb = tiles("y_sb", [[P, 2, width] for t0, width in Y_RANGES for half in range(2)], F32)
+        d_banks, y_banks = {}, {}
 
         def load_x(n):
-            t0, w = X_LOADS[n]
-            nc.sync.dma_start(out=x_in[n][:], in_=x[:, t0 : t0 + w].rearrange("(p j) t -> p j t", j=PACK))
+            t0, width = X_LOADS[n]
+            nc.sync.dma_start(out=x_in[n][:], in_=x[:, t0 : t0 + width].rearrange("(p i) t -> p i t", i=SLOTS))
 
-        def load_scale_rows(plane, first_row, rows):
-            for q in range(4):
-                lo = 32 * q + first_row
+        def load_planes(dst, first_row, scales):
+            for quadrant in range(QUADRANTS):
+                row = 32 * quadrant + first_row
                 nc.sync.dma_start(
-                    out=plane[lo : lo + 4, :].bitcast(I32).rearrange("r (a n) -> r a n", a=rows.shape[0]),
-                    in_=rows[:, 4 * q : 4 * q + 4, :].bitcast(I32).rearrange("a r n -> r a n"),
+                    out=dst[row : row + 4, :].bitcast(I32).rearrange("r (a n) -> r a n", a=scales.shape[0]),
+                    in_=scales[:, 4 * quadrant : 4 * quadrant + 4, :].bitcast(I32).rearrange("a r n -> r a n"),
                 )
+
+        def load_r8(a):
+            words = r8_words[0].rearrange("p j i -> p (j i)").bitcast(I32)
+            nc.sync.dma_start(out=r8_in[a][:], in_=words[:, PASS * a : PASS * (a + 1)])
 
         def load_by_slot(queue, dst, vec):
             queue.dma_start(
-                out=dst[:].rearrange("p (a i) -> p a i", i=PACK), in_=vec.rearrange("(a p i) -> p a i", p=P, i=PACK)
+                out=dst[:].rearrange("p (a i) -> p a i", i=SLOTS), in_=vec.rearrange("(a p i) -> p a i", p=P, i=SLOTS)
             )
 
-        def sort_w4(a):
+        def sort_w4():
             nc.vector.tensor_copy(
-                out=w4_by_slot[a][:].rearrange("p (i m e) -> p i m e", i=PACK, e=2),
-                in_=w4_in[:, 2 * PASS * a : 2 * PASS * (a + 1)].rearrange("p (m i e) -> p i m e", i=PACK, e=2),
+                out=w4_sorted[:].rearrange("p (a i m e) -> p a i m e", a=J_PASSES, i=SLOTS, e=2),
+                in_=w4_in[:].rearrange("p (a m i e) -> p a i m e", a=J_PASSES, i=SLOTS, e=2),
+            )
+            nc.vector.tensor_copy(
+                out=w4_plane[:].rearrange("p (a i m) -> p a i m", a=J_PASSES, i=SLOTS),
+                in_=w4_plane_in[:].rearrange("p (a m i) -> p a i m", a=J_PASSES, i=SLOTS),
             )
 
-        def sort_r8(a):
+        def sort_r8_words(a):
             nc.vector.tensor_copy(
-                out=r8_by_slot[a][:].rearrange("p (i m e) -> p m i e", i=PACK, e=4),
-                in_=r8_in[:, PASS * a : PASS * (a + 1)].rearrange("p (m e i) -> p m i e", i=PACK, e=4),
+                out=r8_sorted[a][:].rearrange("p (i m e) -> p m i e", i=SLOTS, e=4),
+                in_=r8_in[a][:].rearrange("p (m e i) -> p m i e", i=SLOTS, e=4),
             )
 
-        def sort_scales(dst, plane, a):
+        def sort_r8_plane(a):
             nc.vector.tensor_copy(
-                out=dst[a][:].rearrange("p (i m) -> p i m", i=PACK),
-                in_=plane[:, PASS * a : PASS * (a + 1)].rearrange("p (m i) -> p i m", i=PACK),
+                out=r8_plane[a][:].rearrange("p (i m) -> p i m", i=SLOTS),
+                in_=e4m3_planes_in[:, PASS * a : PASS * (a + 1)].rearrange("p (m i) -> p i m", i=SLOTS),
             )
 
         def interleaved(dst):
-            return dst[:].rearrange("p (m e i) -> p m i e", i=PACK, e=2)
+            return dst.rearrange("p (m e i) -> p m i e", i=SLOTS, e=2)
 
-        def by_rows(src):
-            return src[:].rearrange("p i (m e) -> p m i e", e=2)
+        def by_slot(src):
+            return src.rearrange("p i (m e) -> p m i e", e=2)
+
+        def round_x_on_scalar(n):
+            nc.scalar.activation(out=interleaved(x_bf[n][:]), in_=by_slot(x_in[n][:]), func=ACT.Copy)
+
+        def round_x_on_vector(n):
+            nc.vector.tensor_copy(out=interleaved(x_bf[n][:]), in_=by_slot(x_in[n][:]))
 
         def quantize_x(n):
-            t0, w = X_LOADS[n]
-            nc.vector.quantize_mx(
-                out=x_codes[:, t0 : t0 + w].bitcast(FP8X4), scales=x_scales[:, t0 : t0 + w], in_=x_bf[n][:]
-            )
+            t0, width = X_LOADS[n]
+            cols = slice(t0, t0 + width)
+            nc.vector.quantize_mx(out=x_codes[:, cols].bitcast(FP8X4), scales=x_plane[:, cols], in_=x_bf[n][:])
 
-        def quantize_h(u):
-            nc.vector.quantize_mx(out=h_codes[u][:].bitcast(FP8X4), scales=h_scales[u][:], in_=h_bf[u][:])
-
-        d_banks = {}
-
-        def w4_pass(u, i):
-            c, a = divmod(u, J_PASSES)
-            if i % 2 == 0:
-                d_banks[u, i // 2] = ps.tile(
-                    [P, 2, CHUNK], F32, name="d%d_%d" % (u, i // 2), tag="bank", bufs=PSUM_BANKS
+        def w4_passes(u, i):
+            a, t0, width = D_TILES[u]
+            d_banks[u, i] = bank("d%d_%d" % (u, i), [P, width])
+            first = PASS * a + P * i
+            for c0 in range(0, width, FP4_COLUMNS):
+                cols = slice(t0 + c0, t0 + c0 + FP4_COLUMNS)
+                nc.tensor.matmul_mx(
+                    out=d_banks[u, i][:, c0 : c0 + FP4_COLUMNS],
+                    lhsT=w4_sorted[:, 2 * first : 2 * (first + P)].bitcast(FP4X4),
+                    lhsT_scale=w4_plane[:, first : first + P],
+                    rhs=x_codes[:, cols].bitcast(FP8X4),
+                    rhs_scale=x_plane[:, cols],
+                    start=(c0 == 0),
+                    stop=False,
                 )
-            nc.tensor.matmul_mx(
-                out=d_banks[u, i // 2][:, i % 2, :],
-                lhsT=w4_by_slot[a][:, 2 * P * i : 2 * P * (i + 1)].bitcast(FP4X4),
-                lhsT_scale=w4_scales_by_slot[a][:, P * i : P * (i + 1)],
-                rhs=x_codes[:, CHUNK * c : CHUNK * (c + 1)].bitcast(FP8X4),
-                rhs_scale=x_scales[:, CHUNK * c : CHUNK * (c + 1)],
-                start=(i % 2 == 0),
-                stop=False,
-            )
 
         def r8_pass(u, i):
-            c, a = divmod(u, J_PASSES)
+            a, t0, width = D_TILES[u]
+            cols = slice(t0, t0 + width)
             nc.tensor.matmul_mx(
-                out=d_banks[u, i // 2][:, i % 2, :],
-                lhsT=r8_by_slot[a][:, P * i : P * (i + 1)].bitcast(FP8X4),
-                lhsT_scale=r8_scales_by_slot[a][R8_ROW:, P * i : P * (i + 1)],
-                rhs=x_codes[:, CHUNK * c : CHUNK * (c + 1)].bitcast(FP8X4),
-                rhs_scale=x_scales[:, CHUNK * c : CHUNK * (c + 1)],
+                out=d_banks[u, i][:],
+                lhsT=r8_sorted[a][:, P * i : P * (i + 1)].bitcast(FP8X4),
+                lhsT_scale=r8_plane[a][R8_ROW:, P * i : P * (i + 1)],
+                rhs=x_codes[:, cols].bitcast(FP8X4),
+                rhs_scale=x_plane[:, cols],
                 start=False,
-                stop=(i % 2 == 1),
+                stop=True,
             )
 
         def first_product(u):
-            for half in range(2):
-                for one_pass in (w4_pass, r8_pass):
-                    for i in (2 * half, 2 * half + 1):
-                        one_pass(u, i)
+            for i in range(SLOTS):
+                w4_passes(u, i)
+                r8_pass(u, i)
 
         def square(u):
-            a = u % J_PASSES
-            for i in range(PACK):
-                col = PACK * a + i
+            a = D_TILES[u][0]
+            for i in range(SLOTS):
+                col = SLOTS * a + i
                 nc.scalar.activation(
                     out=squares[u][:, i, :],
-                    in_=d_banks[u, i // 2][:, i % 2, :],
+                    in_=d_banks[u, i][:],
                     func=ACT.Square,
                     bias=cb_sb[:, col : col + 1],
                 )
 
-        def weigh(u):
-            a = u % J_PASSES
-            weights = cw_sb[:, PACK * a : PACK * (a + 1)].unsqueeze(1).unsqueeze(3)
+        def weigh(u, t0, width):
+            a, tile_t0 = D_TILES[u][:2]
+            weights = cw_sb[:, SLOTS * a : SLOTS * (a + 1)].unsqueeze(1).unsqueeze(3)
             nc.vector.tensor_tensor(
-                out=interleaved(h_bf[u]),
-                in0=by_rows(squares[u]),
-                in1=weights.to_broadcast([P, CHUNK // 2, PACK, 2]),
+                out=interleaved(h_bf[a][:, SLOTS * t0 : SLOTS * (t0 + width)]),
+                in0=by_slot(squares[u][:, :, t0 - tile_t0 : t0 - tile_t0 + width]),
+                in1=weights.to_broadcast([P, width // 2, SLOTS, 2]),
                 op=ALU.mult,
             )
 
-        y_banks = {}
+        def quantize_h(a, t0, width):
+            cols = slice(t0, t0 + width)
+            nc.vector.quantize_mx(
+                out=h_codes[a][:, cols].bitcast(FP8X4),
+                scales=h_plane[a][:, cols],
+                in_=h_bf[a][:, SLOTS * t0 : SLOTS * (t0 + width)],
+            )
 
-        def second_product(c):
-            for half in range(2):
-                y_banks[c, half] = ps.tile([P, 2, CHUNK], F32, name="y%d_%d" % (c, half), tag="bank", bufs=PSUM_BANKS)
-            for a in range(J_PASSES):
-                u = J_PASSES * c + a
-                for n in range(N_TILES):
-                    cols = slice(N * a + P * n, N * a + P * (n + 1))
-                    nc.tensor.matmul_mx(
-                        out=y_banks[c, n // 2][:, n % 2, :],
-                        lhsT=v8_sb[:, cols].bitcast(FP8X4),
-                        lhsT_scale=e4m3_scales_in[V8_ROW:, cols],
-                        rhs=h_codes[u][:].bitcast(FP8X4),
-                        rhs_scale=h_scales[u][:],
-                        start=(a == 0 and n % 2 == 0),
-                        stop=(a == J_PASSES - 1 and n % 2 == 1),
-                    )
+        def second_product(r, a):
+            t0, width = Y_RANGES[r]
+            cols = slice(t0, t0 + width)
+            if a == 0:
+                y_banks[r] = [bank("y%d_%d" % (r, half), [P, 2, width]) for half in range(2)]
+            for n in range(N // P):
+                first = N * a + P * n
+                nc.tensor.matmul_mx(
+                    out=y_banks[r][n // 2][:, n % 2, :],
+                    lhsT=v8_sb[:, first : first + P].bitcast(FP8X4),
+                    lhsT_scale=e4m3_planes_in[V8_ROW:, first : first + P],
+                    rhs=h_codes[a][:, cols].bitcast(FP8X4),
+                    rhs_scale=h_plane[a][:, cols],
+                    start=(a == 0 and n % 2 == 0),
+                    stop=(a == J_PASSES - 1 and n % 2 == 1),
+                )
 
-        out_tiles = out.rearrange("(n p) t -> p n t", p=P)
+        def store(queue, r, half):
+            t0, width = Y_RANGES[r]
+            rows = out.rearrange("(n p) t -> p n t", p=P)
+            queue.dma_start(out=rows[:, 2 * half : 2 * half + 2, t0 : t0 + width], in_=y_sb[2 * r + half][:])
 
-        def bias_on_scalar(c, half):
+        def finish_on_scalar(queue, r, half):
             for e in range(2):
                 col = 2 * half + e
                 nc.scalar.activation(
-                    out=y_sb[2 * c + half][:, e, :],
-                    in_=y_banks[c, half][:, e, :],
+                    out=y_sb[2 * r + half][:, e, :],
+                    in_=y_banks[r][half][:, e, :],
                     func=ACT.Identity,
                     bias=b_sb[:, col : col + 1],
                 )
+            store(queue, r, half)
 
-        def bias_on_vector(c, half):
-            biases = b_sb[:, 2 * half : 2 * half + 2].unsqueeze(2).to_broadcast([P, 2, CHUNK])
-            nc.vector.tensor_tensor(out=y_sb[2 * c + half][:], in0=y_banks[c, half][:], in1=biases, op=ALU.add)
+        def finish_on_vector(r, half):
+            biases = b_sb[:, 2 * half : 2 * half + 2].unsqueeze(2).to_broadcast([P, 2, Y_RANGES[r][1]])
+            nc.vector.tensor_tensor(out=y_sb[2 * r + half][:], in0=y_banks[r][half][:], in1=biases, op=ALU.add)
+            store(nc.sync, r, half)
 
-        def store(queue, c, half):
-            queue.dma_start(
-                out=out_tiles[:, 2 * half : 2 * half + 2, CHUNK * c : CHUNK * (c + 1)], in_=y_sb[2 * c + half][:]
-            )
-
-        def finish_on_scalar(c):
-            for half in range(2):
-                bias_on_scalar(c, half)
-                store(nc.sync, c, half)
-
-        nc.gpsimd.memset(w4_scales_in[:].bitcast(I32), 0)
-        nc.gpsimd.memset(e4m3_scales_in[:].bitcast(I32), 0)
+        nc.gpsimd.memset(w4_plane_in[:].bitcast(I32), 0)
+        nc.gpsimd.memset(e4m3_planes_in[:].bitcast(I32), 0)
         load_by_slot(nc.gpsimd, cb_sb, cb)
+
         nc.sync.dma_start(out=w4_in[:].bitcast(I32), in_=w4_words[0].bitcast(I32))
-        load_scale_rows(w4_scales_in, 0, w4_scales)
+        load_planes(w4_plane_in, 0, w4_scales)
         load_x(0)
-        nc.sync.dma_start(out=r8_in[:], in_=r8_words[0].rearrange("p j i -> p (j i)").bitcast(I32))
-        load_by_slot(nc.sync, cw_sb, cw)
-        load_scale_rows(e4m3_scales_in, R8_ROW, r8_scales)
+        load_r8(0)
         load_x(1)
+        load_planes(e4m3_planes_in, R8_ROW, r8_scales)
+        load_r8(1)
         load_x(2)
+        load_by_slot(nc.sync, cw_sb, cw)
         nc.sync.dma_start(
             out=v8_sb[:].rearrange("p (a n) -> p a n", a=J_PASSES),
             in_=v8_words.rearrange("a p n i -> p a (n i)").bitcast(I32),
         )
 
-        nc.scalar.activation(out=interleaved(x_bf[0]), in_=by_rows(x_in[0]), func=ACT.Copy)
-        for a in range(J_PASSES):
-            sort_w4(a)
-            sort_scales(w4_scales_by_slot, w4_scales_in, a)
+        round_x_on_scalar(0)
+        round_x_on_scalar(1)
+        sort_w4()
         quantize_x(0)
-        for i in range(PACK):
-            w4_pass(0, i)
-        sort_r8(0)
-        sort_scales(r8_scales_by_slot, e4m3_scales_in, 0)
-        for i in range(PACK):
+        for i in range(SLOTS):
+            w4_passes(0, i)
+        sort_r8_words(0)
+        sort_r8_plane(0)
+        for i in range(SLOTS):
             r8_pass(0, i)
-        sort_r8(1)
-        sort_scales(r8_scales_by_slot, e4m3_scales_in, 1)
-        load_scale_rows(e4m3_scales_in, V8_ROW, v8_scales)
+        quantize_x(1)
+        first_product(1)
+        sort_r8_plane(1)
+        sort_r8_words(1)
+        load_planes(e4m3_planes_in, V8_ROW, v8_scales)
         with nc.allow_non_contiguous_dma(reason="one bias value for each partition"):
             nc.sync.dma_start(out=b_sb[:], in_=b.rearrange("(n p) -> p n", p=P))
-        first_product(1)
-        nc.vector.tensor_copy(out=interleaved(x_bf[1]), in_=by_rows(x_in[1]))
+
         square(0)
-        quantize_x(1)
         first_product(2)
-        first_product(3)
-        weigh(0)
-        nc.vector.tensor_copy(out=interleaved(x_bf[2]), in_=by_rows(x_in[2]))
-        quantize_h(0)
+        square(1)
+        round_x_on_vector(2)
+        weigh(0, 0, 128)
         quantize_x(2)
-        for u in range(1, UNITS):
-            square(u)
-            if u + 3 < UNITS:
-                first_product(u + 3)
-            if u >= 3 and u % 2 == 1:
-                second_product((u - 3) // 2)
-            if u == UNITS - 2:
-                finish_on_scalar(0)
-            weigh(u)
-            if u >= 2:
-                quantize_h(u - 1)
-        quantize_h(UNITS - 1)
-        finish_on_scalar(1)
-        second_product(CHUNKS - 1)
-        finish_on_scalar(2)
-        bias_on_scalar(CHUNKS - 1, 0)
-        bias_on_vector(CHUNKS - 1, 1)
-        store(nc.scalar, CHUNKS - 1, 0)
-        store(nc.sync, CHUNKS - 1, 1)
+        first_product(3)
+        weigh(1, 128, 128)
+        square(2)
+        first_product(4)
+        weigh(2, 0, 256)
+        quantize_h(0, 0, 256)
+        quantize_h(1, 0, 256)
+        square(3)
+        square(4)
+        second_product(0, 0)
+        second_product(0, 1)
+        weigh(3, 256, 256)
+        weigh(4, 256, 128)
+        quantize_h(0, 256, 256)
+        quantize_h(1, 256, 128)
+        weigh(4, 384, 128)
+        quantize_h(1, 384, 128)
+        for r in (1, 2):
+            second_product(r, 0)
+            second_product(r, 1)
+
+        finish_on_scalar(nc.sync, 0, 0)
+        finish_on_scalar(nc.sync, 0, 1)
+        finish_on_scalar(nc.sync, 1, 0)
+        finish_on_vector(1, 1)
+        finish_on_scalar(nc.scalar, 2, 0)
+        finish_on_vector(2, 1)

@@ -87,8 +87,8 @@ def tile_mix_kern_resid_poly2_bias_kernel(
             words = r8_words[0].rearrange("p j i -> p (j i)").bitcast(I32)
             nc.sync.dma_start(out=r8_in[a][:], in_=words[:, PASS * a : PASS * (a + 1)])
 
-        def load_by_slot(queue, dst, vec):
-            queue.dma_start(
+        def load_by_slot(dst, vec):
+            nc.sync.dma_start(
                 out=dst[:].rearrange("p (a i) -> p a i", i=SLOTS), in_=vec.rearrange("(a p i) -> p a i", p=P, i=SLOTS)
             )
 
@@ -234,7 +234,6 @@ def tile_mix_kern_resid_poly2_bias_kernel(
 
         nc.gpsimd.memset(w4_plane_in[:].bitcast(I32), 0)
         nc.gpsimd.memset(e4m3_planes_in[:].bitcast(I32), 0)
-        load_by_slot(nc.gpsimd, cb_sb, cb)
 
         nc.sync.dma_start(out=w4_in[:].bitcast(I32), in_=w4_words[0].bitcast(I32))
         load_planes(w4_plane_in, 0, w4_scales)
@@ -242,9 +241,10 @@ def tile_mix_kern_resid_poly2_bias_kernel(
         load_r8(0)
         load_x(1)
         load_planes(e4m3_planes_in, R8_ROW, r8_scales)
+        load_by_slot(cb_sb, cb)
         load_r8(1)
         load_x(2)
-        load_by_slot(nc.sync, cw_sb, cw)
+        load_by_slot(cw_sb, cw)
         nc.sync.dma_start(
             out=v8_sb[:].rearrange("p (a n) -> p a n", a=J_PASSES),
             in_=v8_words.rearrange("a p n i -> p a (n i)").bitcast(I32),

@@ -9,6 +9,7 @@ F32 = mybir.dt.float32
 BF16 = mybir.dt.bfloat16
 I32 = mybir.dt.int32
 U32 = mybir.dt.uint32
+U16 = mybir.dt.uint16
 U8 = mybir.dt.uint8
 FP8X4 = mybir.dt.float8_e4m3fn_x4
 FP4X4 = mybir.dt.float4_e2m1fn_x4
@@ -20,12 +21,9 @@ SLOTS = 4
 PASS = P * SLOTS
 J_PASSES = J // PASS
 QUADRANTS = 4
-PSUM_BANKS = 8
 FP4_COLUMNS = 128
-R8_ROW, V8_ROW = 0, 4
-
-X_LOADS = ((0, 128), (128, 128), (256, 256))
-D_TILES = ((0, 0, 128), (0, 128, 128), (1, 0, 256), (0, 256, 256), (1, 256, 256))
+X_LOADS = ((0, 128), (128, 128), (256, 128), (384, 128))
+D_TILES = ((0, 0, 128), (0, 128, 128), (1, 0, 128), (1, 128, 128), (0, 256, 128), (1, 256, 128), (0, 384, 128), (1, 384, 128))
 Y_RANGES = ((0, 256), (256, 128), (384, 128))
 
 
@@ -45,15 +43,16 @@ def tile_mix_kern_resid_poly2_bias_kernel(
         def tiles(name, shapes, dtype):
             return [one_tile("%s%d" % (name, n), shape, dtype) for n, shape in enumerate(shapes)]
 
-        def bank(name, shape):
-            return ps.tile(shape, F32, name=name, tag="bank", bufs=PSUM_BANKS)
+        def bank(name, number):
+            return ps.tile([P, PASS], F32, name=name, tag="bank%d" % number, bufs=1)
 
         w4_plane_in = one_tile("w4_plane_in", [P, J], U8)
-        e4m3_planes_in = one_tile("e4m3_planes_in", [P, J], U8)
-        w4_plane = one_tile("w4_plane", [P, J], U8)
+        r8_plane_in = one_tile("r8_plane_in", [P, J], U8)
+        w4_plane = tiles("w4_plane", [[P, PASS]] * J_PASSES, U8)
         r8_plane = tiles("r8_plane", [[P, PASS]] * J_PASSES, U8)
+        v8_plane = one_tile("v8_plane", [P, J_PASSES * N], U8)
         w4_in = one_tile("w4_in", [P, 2 * J], U8)
-        w4_sorted = one_tile("w4_sorted", [P, 2 * J], U8)
+        w4_sorted = tiles("w4_sorted", [[P, 2 * PASS]] * J_PASSES, U8)
         r8_in = tiles("r8_in", [[P, PASS]] * J_PASSES, I32)
         r8_sorted = tiles("r8_sorted", [[P, PASS]] * J_PASSES, I32)
         v8_sb = one_tile("v8_sb", [P, J_PASSES * N], I32)
@@ -61,7 +60,7 @@ def tile_mix_kern_resid_poly2_bias_kernel(
         cb_sb = one_tile("cb_sb", [P, J_PASSES * SLOTS], F32)
         b_sb = one_tile("b_sb", [P, N // P], F32)
         x_in = tiles("x_in", [[P, SLOTS, width] for t0, width in X_LOADS], F32)
-        x_bf = tiles("x_bf", [[P, SLOTS * width] for t0, width in X_LOADS], BF16)
+        x_bf = one_tile("x_bf", [P, SLOTS * T], BF16)
         x_codes = one_tile("x_codes", [P, T], U32)
         x_plane = one_tile("x_plane", [P, T], U8)
         squares = tiles("squares", [[P, SLOTS, width] for a, t0, width in D_TILES], F32)
@@ -69,49 +68,58 @@ def tile_mix_kern_resid_poly2_bias_kernel(
         h_codes = tiles("h_codes", [[P, T]] * J_PASSES, U32)
         h_plane = tiles("h_plane", [[P, T]] * J_PASSES, U8)
         y_sb = tiles("y_sb", [[P, 2, width] for t0, width in Y_RANGES for half in range(2)], F32)
-        d_banks, y_banks = {}, {}
+        d_out, y_out = {}, {}
 
-        def load_x(n):
+        def load_x(queue, n):
             t0, width = X_LOADS[n]
-            nc.sync.dma_start(out=x_in[n][:], in_=x[:, t0 : t0 + width].rearrange("(p i) t -> p i t", i=SLOTS))
+            queue.dma_start(out=x_in[n][:], in_=x[:, t0 : t0 + width].rearrange("(p i) t -> p i t", i=SLOTS))
 
-        def load_planes(dst, first_row, scales):
+        def load_plane(dst, scales):
             for quadrant in range(QUADRANTS):
-                row = 32 * quadrant + first_row
+                row = 32 * quadrant
                 nc.sync.dma_start(
                     out=dst[row : row + 4, :].bitcast(I32).rearrange("r (a n) -> r a n", a=scales.shape[0]),
                     in_=scales[:, 4 * quadrant : 4 * quadrant + 4, :].bitcast(I32).rearrange("a r n -> r a n"),
                 )
 
-        def load_r8(a):
+        def load_w4(queue):
+            queue.dma_start(out=w4_in[:].bitcast(I32), in_=w4_words[0].bitcast(I32))
+
+        def load_r8(queue, a):
             words = r8_words[0].rearrange("p j i -> p (j i)").bitcast(I32)
-            nc.sync.dma_start(out=r8_in[a][:], in_=words[:, PASS * a : PASS * (a + 1)])
+            queue.dma_start(out=r8_in[a][:], in_=words[:, PASS * a : PASS * (a + 1)])
 
         def load_by_slot(dst, vec):
             nc.sync.dma_start(
                 out=dst[:].rearrange("p (a i) -> p a i", i=SLOTS), in_=vec.rearrange("(a p i) -> p a i", p=P, i=SLOTS)
             )
 
-        def sort_w4():
-            nc.vector.tensor_copy(
-                out=w4_sorted[:].rearrange("p (a i m e) -> p a i m e", a=J_PASSES, i=SLOTS, e=2),
-                in_=w4_in[:].rearrange("p (a m i e) -> p a i m e", a=J_PASSES, i=SLOTS, e=2),
-            )
-            nc.vector.tensor_copy(
-                out=w4_plane[:].rearrange("p (a i m) -> p a i m", a=J_PASSES, i=SLOTS),
-                in_=w4_plane_in[:].rearrange("p (a m i) -> p a i m", a=J_PASSES, i=SLOTS),
+        def load_v8():
+            nc.sync.dma_start(
+                out=v8_sb[:].rearrange("p (a n) -> p a n", a=J_PASSES),
+                in_=v8_words.rearrange("a p n i -> p a (n i)").bitcast(I32),
             )
 
-        def sort_r8_words(a):
+        def load_b():
+            with nc.allow_non_contiguous_dma(reason="one bias value for each partition"):
+                nc.sync.dma_start(out=b_sb[:], in_=b.rearrange("(n p) -> p n", p=P))
+
+        def sort_w4(a):
+            nc.vector.tensor_copy(
+                out=w4_sorted[a][:].bitcast(U16).rearrange("p (i m) -> p i m", i=SLOTS),
+                in_=w4_in[:, 2 * PASS * a : 2 * PASS * (a + 1)].bitcast(U16).rearrange("p (m i) -> p i m", i=SLOTS),
+            )
+
+        def sort_r8(a):
             nc.vector.tensor_copy(
                 out=r8_sorted[a][:].rearrange("p (i m e) -> p m i e", i=SLOTS, e=4),
                 in_=r8_in[a][:].rearrange("p (m e i) -> p m i e", i=SLOTS, e=4),
             )
 
-        def sort_r8_plane(a):
+        def sort_plane(dst, src, a):
             nc.vector.tensor_copy(
-                out=r8_plane[a][:].rearrange("p (i m) -> p i m", i=SLOTS),
-                in_=e4m3_planes_in[:, PASS * a : PASS * (a + 1)].rearrange("p (m i) -> p i m", i=SLOTS),
+                out=dst[a][:].rearrange("p (i m) -> p i m", i=SLOTS),
+                in_=src[:, PASS * a : PASS * (a + 1)].rearrange("p (m i) -> p i m", i=SLOTS),
             )
 
         def interleaved(dst):
@@ -120,58 +128,86 @@ def tile_mix_kern_resid_poly2_bias_kernel(
         def by_slot(src):
             return src.rearrange("p i (m e) -> p m i e", e=2)
 
-        def round_x_on_scalar(n):
-            nc.scalar.activation(out=interleaved(x_bf[n][:]), in_=by_slot(x_in[n][:]), func=ACT.Copy)
+        def x_views(n, t0, width):
+            c0 = t0 - X_LOADS[n][0]
+            return interleaved(x_bf[:, SLOTS * t0 : SLOTS * (t0 + width)]), by_slot(x_in[n][:, :, c0 : c0 + width])
 
-        def round_x_on_vector(n):
-            nc.vector.tensor_copy(out=interleaved(x_bf[n][:]), in_=by_slot(x_in[n][:]))
+        def round_x_on_scalar(n, t0, width):
+            dst, src = x_views(n, t0, width)
+            nc.scalar.activation(out=dst, in_=src, func=ACT.Copy)
 
-        def quantize_x(n):
-            t0, width = X_LOADS[n]
+        def round_x_on_vector(n, t0, width):
+            dst, src = x_views(n, t0, width)
+            nc.vector.tensor_copy(out=dst, in_=src)
+
+        def quantize_x(t0, width):
             cols = slice(t0, t0 + width)
-            nc.vector.quantize_mx(out=x_codes[:, cols].bitcast(FP8X4), scales=x_plane[:, cols], in_=x_bf[n][:])
+            nc.vector.quantize_mx(
+                out=x_codes[:, cols].bitcast(FP8X4),
+                scales=x_plane[:, cols],
+                in_=x_bf[:, SLOTS * t0 : SLOTS * (t0 + width)],
+            )
 
-        def w4_passes(u, i):
+        def w4_passes(u, banks):
             a, t0, width = D_TILES[u]
-            d_banks[u, i] = bank("d%d_%d" % (u, i), [P, width])
-            first = PASS * a + P * i
-            for c0 in range(0, width, FP4_COLUMNS):
-                cols = slice(t0 + c0, t0 + c0 + FP4_COLUMNS)
+            per_bank = SLOTS // len(banks)
+            for n, number in enumerate(banks):
+                acc = bank("d%d_%d" % (u, n), number)
+                for s in range(per_bank):
+                    d_out[u, per_bank * n + s] = acc[:, width * s : width * (s + 1)]
+                    w4_slot(u, per_bank * n + s, s == 0)
+
+        def w4_slot(u, i, opens):
+            a, t0, width = D_TILES[u]
+            step = width if width == PASS else FP4_COLUMNS
+            for c0 in range(0, width, step):
+                cols = slice(t0 + c0, t0 + c0 + step)
                 nc.tensor.matmul_mx(
-                    out=d_banks[u, i][:, c0 : c0 + FP4_COLUMNS],
-                    lhsT=w4_sorted[:, 2 * first : 2 * (first + P)].bitcast(FP4X4),
-                    lhsT_scale=w4_plane[:, first : first + P],
+                    out=d_out[u, i][:, c0 : c0 + step],
+                    lhsT=w4_sorted[a][:, 2 * P * i : 2 * P * (i + 1)].bitcast(FP4X4),
+                    lhsT_scale=w4_plane[a][:, P * i : P * (i + 1)],
                     rhs=x_codes[:, cols].bitcast(FP8X4),
                     rhs_scale=x_plane[:, cols],
-                    start=(c0 == 0),
+                    start=(opens and c0 == 0),
                     stop=False,
                 )
 
-        def r8_pass(u, i):
+        def r8_slot(u, i, closes):
             a, t0, width = D_TILES[u]
             cols = slice(t0, t0 + width)
             nc.tensor.matmul_mx(
-                out=d_banks[u, i][:],
+                out=d_out[u, i],
                 lhsT=r8_sorted[a][:, P * i : P * (i + 1)].bitcast(FP8X4),
-                lhsT_scale=r8_plane[a][R8_ROW:, P * i : P * (i + 1)],
+                lhsT_scale=r8_plane[a][:, P * i : P * (i + 1)],
                 rhs=x_codes[:, cols].bitcast(FP8X4),
                 rhs_scale=x_plane[:, cols],
                 start=False,
-                stop=True,
+                stop=closes,
             )
 
-        def first_product(u):
+        def r8_passes(u, bank_count):
+            per_bank = SLOTS // bank_count
             for i in range(SLOTS):
-                w4_passes(u, i)
-                r8_pass(u, i)
+                r8_slot(u, i, i % per_bank == per_bank - 1)
 
-        def square(u):
-            a = D_TILES[u][0]
+        def first_product(u, banks):
+            a, t0, width = D_TILES[u]
+            per_bank = SLOTS // len(banks)
+            for n, number in enumerate(banks):
+                acc = bank("d%d_%d" % (u, n), number)
+                for s in range(per_bank):
+                    i = per_bank * n + s
+                    d_out[u, i] = acc[:, width * s : width * (s + 1)]
+                    w4_slot(u, i, s == 0)
+                    r8_slot(u, i, s == per_bank - 1)
+
+        def square(u, t0, width):
+            a, tile_t0 = D_TILES[u][:2]
             for i in range(SLOTS):
                 col = SLOTS * a + i
                 nc.scalar.activation(
-                    out=squares[u][:, i, :],
-                    in_=d_banks[u, i][:],
+                    out=squares[u][:, i, t0 - tile_t0 : t0 - tile_t0 + width],
+                    in_=d_out[u, i][:, t0 - tile_t0 : t0 - tile_t0 + width],
                     func=ACT.Square,
                     bias=cb_sb[:, col : col + 1],
                 )
@@ -194,21 +230,22 @@ def tile_mix_kern_resid_poly2_bias_kernel(
                 in_=h_bf[a][:, SLOTS * t0 : SLOTS * (t0 + width)],
             )
 
-        def second_product(r, a):
+        def second_product(r, a, banks=None):
             t0, width = Y_RANGES[r]
             cols = slice(t0, t0 + width)
             if a == 0:
-                y_banks[r] = [bank("y%d_%d" % (r, half), [P, 2, width]) for half in range(2)]
+                y_out[r] = [bank("y%d_%d" % (r, half), number) for half, number in enumerate(banks)]
             for n in range(N // P):
                 first = N * a + P * n
+                half, s = divmod(n, 2)
                 nc.tensor.matmul_mx(
-                    out=y_banks[r][n // 2][:, n % 2, :],
+                    out=y_out[r][half][:, width * s : width * (s + 1)],
                     lhsT=v8_sb[:, first : first + P].bitcast(FP8X4),
-                    lhsT_scale=e4m3_planes_in[V8_ROW:, first : first + P],
+                    lhsT_scale=v8_plane[:, first : first + P],
                     rhs=h_codes[a][:, cols].bitcast(FP8X4),
                     rhs_scale=h_plane[a][:, cols],
-                    start=(a == 0 and n % 2 == 0),
-                    stop=(a == J_PASSES - 1 and n % 2 == 1),
+                    start=(a == 0 and s == 0),
+                    stop=(a == J_PASSES - 1 and s == 1),
                 )
 
         def store(queue, r, half):
@@ -217,87 +254,100 @@ def tile_mix_kern_resid_poly2_bias_kernel(
             queue.dma_start(out=rows[:, 2 * half : 2 * half + 2, t0 : t0 + width], in_=y_sb[2 * r + half][:])
 
         def finish_on_scalar(queue, r, half):
-            for e in range(2):
-                col = 2 * half + e
+            width = Y_RANGES[r][1]
+            for s in range(2):
+                n = 2 * half + s
                 nc.scalar.activation(
-                    out=y_sb[2 * r + half][:, e, :],
-                    in_=y_banks[r][half][:, e, :],
+                    out=y_sb[2 * r + half][:, s, :],
+                    in_=y_out[r][half][:, width * s : width * (s + 1)],
                     func=ACT.Identity,
-                    bias=b_sb[:, col : col + 1],
+                    bias=b_sb[:, n : n + 1],
                 )
             store(queue, r, half)
 
         def finish_on_vector(r, half):
-            biases = b_sb[:, 2 * half : 2 * half + 2].unsqueeze(2).to_broadcast([P, 2, Y_RANGES[r][1]])
-            nc.vector.tensor_tensor(out=y_sb[2 * r + half][:], in0=y_banks[r][half][:], in1=biases, op=ALU.add)
+            width = Y_RANGES[r][1]
+            sums = y_out[r][half][:, : 2 * width].rearrange("p (n t) -> p n t", n=2)
+            biases = b_sb[:, 2 * half : 2 * half + 2].unsqueeze(2).to_broadcast([P, 2, width])
+            nc.vector.tensor_tensor(out=y_sb[2 * r + half][:], in0=sums, in1=biases, op=ALU.add)
             store(nc.sync, r, half)
 
-        nc.gpsimd.memset(w4_plane_in[:].bitcast(I32), 0)
-        nc.gpsimd.memset(e4m3_planes_in[:].bitcast(I32), 0)
+        nc.vector.memset(w4_plane_in[:].bitcast(I32), 0)
+        nc.gpsimd.memset(r8_plane_in[:].bitcast(I32), 0)
+        nc.gpsimd.memset(v8_plane[:].bitcast(I32), 0)
 
-        nc.sync.dma_start(out=w4_in[:].bitcast(I32), in_=w4_words[0].bitcast(I32))
-        load_planes(w4_plane_in, 0, w4_scales)
-        load_x(0)
-        load_r8(0)
-        load_x(1)
-        load_planes(e4m3_planes_in, R8_ROW, r8_scales)
+        load_x(nc.sync, 0)
+        load_w4(nc.sync)
+        load_plane(w4_plane_in, w4_scales)
+        load_r8(nc.sync, 0)
+        load_x(nc.sync, 1)
+        load_plane(r8_plane_in, r8_scales)
+        load_r8(nc.sync, 1)
         load_by_slot(cb_sb, cb)
-        load_r8(1)
-        load_x(2)
+        load_x(nc.sync, 2)
         load_by_slot(cw_sb, cw)
-        nc.sync.dma_start(
-            out=v8_sb[:].rearrange("p (a n) -> p a n", a=J_PASSES),
-            in_=v8_words.rearrange("a p n i -> p a (n i)").bitcast(I32),
-        )
+        load_x(nc.sync, 3)
+        load_v8()
+        load_plane(v8_plane, v8_scales)
+        load_b()
 
-        round_x_on_scalar(0)
-        round_x_on_scalar(1)
-        sort_w4()
-        quantize_x(0)
-        for i in range(SLOTS):
-            w4_passes(0, i)
-        sort_r8_words(0)
-        sort_r8_plane(0)
-        for i in range(SLOTS):
-            r8_pass(0, i)
-        quantize_x(1)
-        first_product(1)
-        sort_r8_plane(1)
-        sort_r8_words(1)
-        load_planes(e4m3_planes_in, V8_ROW, v8_scales)
-        with nc.allow_non_contiguous_dma(reason="one bias value for each partition"):
-            nc.sync.dma_start(out=b_sb[:], in_=b.rearrange("(n p) -> p n", p=P))
-
-        square(0)
-        first_product(2)
-        square(1)
-        round_x_on_vector(2)
+        round_x_on_scalar(0, 0, 128)
+        round_x_on_scalar(1, 128, 128)
+        sort_w4(0)
+        sort_plane(w4_plane, w4_plane_in, 0)
+        quantize_x(0, 128)
+        w4_passes(0, (0, 1))
+        sort_w4(1)
+        sort_plane(w4_plane, w4_plane_in, 1)
+        w4_passes(2, (4, 5))
+        sort_r8(0)
+        sort_plane(r8_plane, r8_plane_in, 0)
+        r8_passes(0, 2)
+        quantize_x(128, 128)
+        first_product(1, (2, 3))
+        sort_plane(r8_plane, r8_plane_in, 1)
+        sort_r8(1)
+        r8_passes(2, 2)
+        first_product(3, (6, 7))
+        square(0, 0, 128)
+        round_x_on_vector(2, 256, 128)
         weigh(0, 0, 128)
-        quantize_x(2)
-        first_product(3)
+        quantize_x(256, 128)
+        square(1, 128, 128)
+        first_product(4, (0, 1))
+        round_x_on_vector(3, 384, 128)
         weigh(1, 128, 128)
-        square(2)
-        first_product(4)
-        weigh(2, 0, 256)
+        quantize_x(384, 128)
+        first_product(5, (2, 3))
+        square(2, 0, 128)
+        first_product(6, (4, 5))
+        weigh(2, 0, 128)
         quantize_h(0, 0, 256)
-        quantize_h(1, 0, 256)
-        square(3)
-        square(4)
-        second_product(0, 0)
-        second_product(0, 1)
-        weigh(3, 256, 256)
+        square(3, 128, 128)
+        first_product(7, (6, 7))
+        weigh(3, 128, 128)
+        square(4, 256, 128)
         weigh(4, 256, 128)
-        quantize_h(0, 256, 256)
+        quantize_h(1, 0, 256)
+        square(5, 256, 128)
+        second_product(0, 0, (0, 1))
+        second_product(0, 1)
+        weigh(5, 256, 128)
+        quantize_h(0, 256, 128)
+        square(6, 384, 128)
+        square(7, 384, 128)
+        weigh(6, 384, 128)
         quantize_h(1, 256, 128)
-        weigh(4, 384, 128)
+        second_product(1, 0, (2, 3))
+        second_product(1, 1)
+        quantize_h(0, 384, 128)
+        second_product(2, 0, (4, 5))
+        weigh(7, 384, 128)
         quantize_h(1, 384, 128)
-        for r in (1, 2):
-            second_product(r, 0)
-            second_product(r, 1)
-
+        second_product(2, 1)
         finish_on_scalar(nc.sync, 0, 0)
         finish_on_scalar(nc.sync, 0, 1)
-        finish_on_scalar(nc.sync, 1, 0)
-        finish_on_vector(1, 1)
+        finish_on_vector(1, 0)
+        finish_on_scalar(nc.sync, 1, 1)
         finish_on_scalar(nc.scalar, 2, 0)
         finish_on_vector(2, 1)

@@ -23,7 +23,7 @@ J_PASSES = J // PASS
 QUADRANTS = 4
 FP4_COLUMNS = 128
 X_LOADS = ((0, 128), (128, 128), (256, 128), (384, 128))
-D_TILES = ((0, 0, 128), (0, 128, 128), (1, 0, 128), (1, 128, 128), (0, 256, 128), (1, 256, 128), (0, 384, 128), (1, 384, 128))
+D_TILES = tuple((u % 2, 128 * (u // 2), 128) for u in range(8))
 Y_RANGES = ((0, 256), (256, 128), (384, 128))
 
 
@@ -53,7 +53,7 @@ def tile_mix_kern_resid_poly2_bias_kernel(
         v8_plane = one_tile("v8_plane", [P, J_PASSES * N], U8)
         w4_in = one_tile("w4_in", [P, 2 * J], U8)
         w4_sorted = tiles("w4_sorted", [[P, 2 * PASS]] * J_PASSES, U8)
-        r8_in = tiles("r8_in", [[P, PASS]] * J_PASSES, I32)
+        r8_in = one_tile("r8_in", [P, J], I32)
         r8_sorted = tiles("r8_sorted", [[P, PASS]] * J_PASSES, I32)
         v8_sb = one_tile("v8_sb", [P, J_PASSES * N], I32)
         cw_sb = one_tile("cw_sb", [P, J_PASSES * SLOTS], F32)
@@ -74,10 +74,10 @@ def tile_mix_kern_resid_poly2_bias_kernel(
             t0, width = X_LOADS[n]
             queue.dma_start(out=x_in[n][:], in_=x[:, t0 : t0 + width].rearrange("(p i) t -> p i t", i=SLOTS))
 
-        def load_plane(dst, scales):
-            for quadrant in range(QUADRANTS):
+        def load_plane(queue, dst, scales, quadrants=range(QUADRANTS)):
+            for quadrant in quadrants:
                 row = 32 * quadrant
-                nc.sync.dma_start(
+                queue.dma_start(
                     out=dst[row : row + 4, :].bitcast(I32).rearrange("r (a n) -> r a n", a=scales.shape[0]),
                     in_=scales[:, 4 * quadrant : 4 * quadrant + 4, :].bitcast(I32).rearrange("a r n -> r a n"),
                 )
@@ -85,9 +85,8 @@ def tile_mix_kern_resid_poly2_bias_kernel(
         def load_w4(queue):
             queue.dma_start(out=w4_in[:].bitcast(I32), in_=w4_words[0].bitcast(I32))
 
-        def load_r8(queue, a):
-            words = r8_words[0].rearrange("p j i -> p (j i)").bitcast(I32)
-            queue.dma_start(out=r8_in[a][:], in_=words[:, PASS * a : PASS * (a + 1)])
+        def load_r8(queue):
+            queue.dma_start(out=r8_in[:], in_=r8_words[0].rearrange("p j i -> p (j i)").bitcast(I32))
 
         def load_by_slot(dst, vec):
             nc.sync.dma_start(
@@ -113,7 +112,7 @@ def tile_mix_kern_resid_poly2_bias_kernel(
         def sort_r8(a):
             nc.vector.tensor_copy(
                 out=r8_sorted[a][:].rearrange("p (i m e) -> p m i e", i=SLOTS, e=4),
-                in_=r8_in[a][:].rearrange("p (m e i) -> p m i e", i=SLOTS, e=4),
+                in_=r8_in[:, PASS * a : PASS * (a + 1)].rearrange("p (m e i) -> p m i e", i=SLOTS, e=4),
             )
 
         def sort_plane(dst, src, a):
@@ -201,9 +200,9 @@ def tile_mix_kern_resid_poly2_bias_kernel(
                     w4_slot(u, i, s == 0)
                     r8_slot(u, i, s == per_bank - 1)
 
-        def square(u, t0, width):
+        def square(u, t0, width, slots=range(SLOTS)):
             a, tile_t0 = D_TILES[u][:2]
-            for i in range(SLOTS):
+            for i in slots:
                 col = SLOTS * a + i
                 nc.scalar.activation(
                     out=squares[u][:, i, t0 - tile_t0 : t0 - tile_t0 + width],
@@ -230,12 +229,12 @@ def tile_mix_kern_resid_poly2_bias_kernel(
                 in_=h_bf[a][:, SLOTS * t0 : SLOTS * (t0 + width)],
             )
 
-        def second_product(r, a, banks=None):
+        def second_product(r, a, banks=None, halves=(0, 1)):
             t0, width = Y_RANGES[r]
             cols = slice(t0, t0 + width)
-            if a == 0:
+            if banks:
                 y_out[r] = [bank("y%d_%d" % (r, half), number) for half, number in enumerate(banks)]
-            for n in range(N // P):
+            for n in range(2 * halves[0], 2 * halves[-1] + 2):
                 first = N * a + P * n
                 half, s = divmod(n, 2)
                 nc.tensor.matmul_mx(
@@ -248,12 +247,15 @@ def tile_mix_kern_resid_poly2_bias_kernel(
                     stop=(a == J_PASSES - 1 and s == 1),
                 )
 
-        def store(queue, r, half):
+        def store(queue, r, half, s0=0, count=2):
             t0, width = Y_RANGES[r]
             rows = out.rearrange("(n p) t -> p n t", p=P)
-            queue.dma_start(out=rows[:, 2 * half : 2 * half + 2, t0 : t0 + width], in_=y_sb[2 * r + half][:])
+            n0 = 2 * half + s0
+            queue.dma_start(
+                out=rows[:, n0 : n0 + count, t0 : t0 + width], in_=y_sb[2 * r + half][:, s0 : s0 + count, :]
+            )
 
-        def finish_on_scalar(queue, r, half):
+        def finish_on_scalar(queue, r, half, singly=False):
             width = Y_RANGES[r][1]
             for s in range(2):
                 n = 2 * half + s
@@ -263,7 +265,10 @@ def tile_mix_kern_resid_poly2_bias_kernel(
                     func=ACT.Identity,
                     bias=b_sb[:, n : n + 1],
                 )
-            store(queue, r, half)
+                if singly:
+                    store(queue, r, half, s, 1)
+            if not singly:
+                store(queue, r, half)
 
         def finish_on_vector(r, half):
             width = Y_RANGES[r][1]
@@ -278,17 +283,16 @@ def tile_mix_kern_resid_poly2_bias_kernel(
 
         load_x(nc.sync, 0)
         load_w4(nc.sync)
-        load_plane(w4_plane_in, w4_scales)
-        load_r8(nc.sync, 0)
+        load_plane(nc.sync, w4_plane_in, w4_scales)
+        load_r8(nc.sync)
         load_x(nc.sync, 1)
-        load_plane(r8_plane_in, r8_scales)
-        load_r8(nc.sync, 1)
+        load_plane(nc.sync, r8_plane_in, r8_scales)
         load_by_slot(cb_sb, cb)
         load_x(nc.sync, 2)
-        load_by_slot(cw_sb, cw)
         load_x(nc.sync, 3)
+        load_by_slot(cw_sb, cw)
         load_v8()
-        load_plane(v8_plane, v8_scales)
+        load_plane(nc.sync, v8_plane, v8_scales)
         load_b()
 
         round_x_on_scalar(0, 0, 128)
@@ -296,58 +300,62 @@ def tile_mix_kern_resid_poly2_bias_kernel(
         sort_w4(0)
         sort_plane(w4_plane, w4_plane_in, 0)
         quantize_x(0, 128)
-        w4_passes(0, (0, 1))
+        w4_passes(0, (0, 1, 2, 3))
         sort_w4(1)
         sort_plane(w4_plane, w4_plane_in, 1)
-        w4_passes(2, (4, 5))
+        w4_passes(1, (4, 5))
         sort_r8(0)
-        sort_plane(r8_plane, r8_plane_in, 0)
-        r8_passes(0, 2)
-        quantize_x(128, 128)
-        first_product(1, (2, 3))
-        sort_plane(r8_plane, r8_plane_in, 1)
         sort_r8(1)
-        r8_passes(2, 2)
-        first_product(3, (6, 7))
-        square(0, 0, 128)
+        sort_plane(r8_plane, r8_plane_in, 0)
+        r8_passes(0, 4)
+        sort_plane(r8_plane, r8_plane_in, 1)
+        r8_passes(1, 2)
+        quantize_x(128, 128)
+        first_product(2, (6, 7))
         round_x_on_vector(2, 256, 128)
-        weigh(0, 0, 128)
         quantize_x(256, 128)
-        square(1, 128, 128)
-        first_product(4, (0, 1))
+        square(0, 0, 128)
+        first_product(3, (0, 1))
         round_x_on_vector(3, 384, 128)
-        weigh(1, 128, 128)
+        weigh(0, 0, 128)
         quantize_x(384, 128)
-        first_product(5, (2, 3))
-        square(2, 0, 128)
-        first_product(6, (4, 5))
-        weigh(2, 0, 128)
-        quantize_h(0, 0, 256)
+        first_product(4, (2, 3))
+        square(1, 0, 128)
+        first_product(5, (4, 5))
+        weigh(1, 0, 128)
+        quantize_h(0, 0, 128)
+        square(2, 128, 128)
+        first_product(6, (6, 7))
+        weigh(2, 128, 128)
+        quantize_h(1, 0, 128)
         square(3, 128, 128)
-        first_product(7, (6, 7))
+        first_product(7, (0, 1))
         weigh(3, 128, 128)
+        quantize_h(0, 128, 128)
         square(4, 256, 128)
         weigh(4, 256, 128)
-        quantize_h(1, 0, 256)
+        quantize_h(1, 128, 128)
+        second_product(0, 0, (2, 3), (0,))
+        second_product(0, 1, None, (0,))
+        second_product(0, 0, None, (1,))
+        second_product(0, 1, None, (1,))
         square(5, 256, 128)
-        second_product(0, 0, (0, 1))
-        second_product(0, 1)
         weigh(5, 256, 128)
         quantize_h(0, 256, 128)
+        second_product(1, 0, (4, 5))
         square(6, 384, 128)
         square(7, 384, 128)
         weigh(6, 384, 128)
         quantize_h(1, 256, 128)
-        second_product(1, 0, (2, 3))
         second_product(1, 1)
-        quantize_h(0, 384, 128)
-        second_product(2, 0, (4, 5))
         weigh(7, 384, 128)
+        quantize_h(0, 384, 128)
+        second_product(2, 0, (6, 7))
         quantize_h(1, 384, 128)
         second_product(2, 1)
-        finish_on_scalar(nc.sync, 0, 0)
+        finish_on_scalar(nc.sync, 0, 0, True)
         finish_on_scalar(nc.sync, 0, 1)
-        finish_on_vector(1, 0)
-        finish_on_scalar(nc.sync, 1, 1)
+        finish_on_scalar(nc.sync, 1, 0)
+        finish_on_vector(1, 1)
         finish_on_scalar(nc.scalar, 2, 0)
         finish_on_vector(2, 1)

@@ -21,10 +21,18 @@ SLOTS = 4
 PASS = P * SLOTS
 J_PASSES = J // PASS
 QUADRANTS = 4
-FP4_COLUMNS = 128
-X_LOADS = ((0, 128), (128, 128), (256, 128), (384, 128))
-D_TILES = tuple((u % 2, 128 * (u // 2), 128) for u in range(8))
-Y_RANGES = ((0, 256), (256, 128), (384, 128))
+BANK_COLUMNS = 512
+PSUM_BANKS = 8
+CHUNK = 128
+CHUNKS = T // CHUNK
+D_TILES = J_PASSES * CHUNKS
+D_BANKS = (4, 2, 2, 2, 1, 1, 1, 1)
+LEAD = 3
+RUN = 2
+
+Y_RANGES = ((0, 2 * CHUNK), (2 * CHUNK, CHUNK), (3 * CHUNK, CHUNK))
+FIRST_RANGE_TILES = J_PASSES * Y_RANGES[0][1] // CHUNK
+HALF_ROWS = 2
 
 
 def tile_mix_kern_resid_poly2_bias_kernel(
@@ -43,8 +51,13 @@ def tile_mix_kern_resid_poly2_bias_kernel(
         def tiles(name, shapes, dtype):
             return [one_tile("%s%d" % (name, n), shape, dtype) for n, shape in enumerate(shapes)]
 
-        def bank(name, number):
-            return ps.tile([P, PASS], F32, name=name, tag="bank%d" % number, bufs=1)
+        def next_banks(name, count):
+            first = len(banks_given)
+            banks_given.extend(
+                ps.tile([P, BANK_COLUMNS], F32, name="%s_%d" % (name, n), tag="bank%d" % ((first + n) % PSUM_BANKS), bufs=1)
+                for n in range(count)
+            )
+            return banks_given[first:]
 
         w4_plane_in = one_tile("w4_plane_in", [P, J], U8)
         r8_plane_in = one_tile("r8_plane_in", [P, J], U8)
@@ -59,49 +72,35 @@ def tile_mix_kern_resid_poly2_bias_kernel(
         cw_sb = one_tile("cw_sb", [P, J_PASSES * SLOTS], F32)
         cb_sb = one_tile("cb_sb", [P, J_PASSES * SLOTS], F32)
         b_sb = one_tile("b_sb", [P, N // P], F32)
-        x_in = tiles("x_in", [[P, SLOTS, width] for t0, width in X_LOADS], F32)
+        x_in = tiles("x_in", [[P, SLOTS, CHUNK]] * CHUNKS, F32)
         x_bf = one_tile("x_bf", [P, SLOTS * T], BF16)
         x_codes = one_tile("x_codes", [P, T], U32)
         x_plane = one_tile("x_plane", [P, T], U8)
-        squares = tiles("squares", [[P, SLOTS, width] for a, t0, width in D_TILES], F32)
+        squares = tiles("squares", [[P, SLOTS, CHUNK]] * D_TILES, F32)
         h_bf = tiles("h_bf", [[P, SLOTS * T]] * J_PASSES, BF16)
         h_codes = tiles("h_codes", [[P, T]] * J_PASSES, U32)
         h_plane = tiles("h_plane", [[P, T]] * J_PASSES, U8)
-        y_sb = tiles("y_sb", [[P, 2, width] for t0, width in Y_RANGES for half in range(2)], F32)
-        d_out, y_out = {}, {}
+        y_sb = tiles("y_sb", [[P, HALF_ROWS, width] for t0, width in Y_RANGES for half in range(2)], F32)
+        banks_given, d_sums, y_banks = [], {}, {}
 
-        def load_x(queue, n):
-            t0, width = X_LOADS[n]
-            queue.dma_start(out=x_in[n][:], in_=x[:, t0 : t0 + width].rearrange("(p i) t -> p i t", i=SLOTS))
+        def chunk_columns(c, per_column=1):
+            return slice(per_column * CHUNK * c, per_column * CHUNK * (c + 1))
 
-        def load_plane(queue, dst, scales, quadrants=range(QUADRANTS)):
-            for quadrant in quadrants:
+        def load_x(c):
+            nc.sync.dma_start(out=x_in[c][:], in_=x[:, chunk_columns(c)].rearrange("(p i) t -> p i t", i=SLOTS))
+
+        def load_plane(dst, scales):
+            for quadrant in range(QUADRANTS):
                 row = 32 * quadrant
-                queue.dma_start(
+                nc.sync.dma_start(
                     out=dst[row : row + 4, :].bitcast(I32).rearrange("r (a n) -> r a n", a=scales.shape[0]),
                     in_=scales[:, 4 * quadrant : 4 * quadrant + 4, :].bitcast(I32).rearrange("a r n -> r a n"),
                 )
-
-        def load_w4(queue):
-            queue.dma_start(out=w4_in[:].bitcast(I32), in_=w4_words[0].bitcast(I32))
-
-        def load_r8(queue):
-            queue.dma_start(out=r8_in[:], in_=r8_words[0].rearrange("p j i -> p (j i)").bitcast(I32))
 
         def load_by_slot(dst, vec):
             nc.sync.dma_start(
                 out=dst[:].rearrange("p (a i) -> p a i", i=SLOTS), in_=vec.rearrange("(a p i) -> p a i", p=P, i=SLOTS)
             )
-
-        def load_v8():
-            nc.sync.dma_start(
-                out=v8_sb[:].rearrange("p (a n) -> p a n", a=J_PASSES),
-                in_=v8_words.rearrange("a p n i -> p a (n i)").bitcast(I32),
-            )
-
-        def load_b():
-            with nc.allow_non_contiguous_dma(reason="one bias value for each partition"):
-                nc.sync.dma_start(out=b_sb[:], in_=b.rearrange("(n p) -> p n", p=P))
 
         def sort_w4(a):
             nc.vector.tensor_copy(
@@ -115,247 +114,218 @@ def tile_mix_kern_resid_poly2_bias_kernel(
                 in_=r8_in[:, PASS * a : PASS * (a + 1)].rearrange("p (m e i) -> p m i e", i=SLOTS, e=4),
             )
 
-        def sort_plane(dst, src, a):
+        def sort_plane(dst, src, a, slots=slice(0, SLOTS)):
             nc.vector.tensor_copy(
-                out=dst[a][:].rearrange("p (i m) -> p i m", i=SLOTS),
-                in_=src[:, PASS * a : PASS * (a + 1)].rearrange("p (m i) -> p i m", i=SLOTS),
+                out=dst[a][:].rearrange("p (i m) -> p i m", i=SLOTS)[:, slots, :],
+                in_=src[:, PASS * a : PASS * (a + 1)].rearrange("p (m i) -> p i m", i=SLOTS)[:, slots, :],
             )
 
         def interleaved(dst):
-            return dst.rearrange("p (m e i) -> p m i e", i=SLOTS, e=2)
+            return dst.rearrange("p (m e i) -> p m i e", i=SLOTS, e=RUN)
 
         def by_slot(src):
-            return src.rearrange("p i (m e) -> p m i e", e=2)
+            return src.rearrange("p i (m e) -> p m i e", e=RUN)
 
-        def x_views(n, t0, width):
-            c0 = t0 - X_LOADS[n][0]
-            return interleaved(x_bf[:, SLOTS * t0 : SLOTS * (t0 + width)]), by_slot(x_in[n][:, :, c0 : c0 + width])
+        def round_x_on_scalar(c):
+            nc.scalar.activation(
+                out=interleaved(x_bf[:, chunk_columns(c, SLOTS)]), in_=by_slot(x_in[c][:]), func=ACT.Copy
+            )
 
-        def round_x_on_scalar(n, t0, width):
-            dst, src = x_views(n, t0, width)
-            nc.scalar.activation(out=dst, in_=src, func=ACT.Copy)
+        def round_x_on_vector(c):
+            nc.vector.tensor_copy(out=interleaved(x_bf[:, chunk_columns(c, SLOTS)]), in_=by_slot(x_in[c][:]))
 
-        def round_x_on_vector(n, t0, width):
-            dst, src = x_views(n, t0, width)
-            nc.vector.tensor_copy(out=dst, in_=src)
-
-        def quantize_x(t0, width):
-            cols = slice(t0, t0 + width)
+        def quantize_x(c):
             nc.vector.quantize_mx(
-                out=x_codes[:, cols].bitcast(FP8X4),
-                scales=x_plane[:, cols],
-                in_=x_bf[:, SLOTS * t0 : SLOTS * (t0 + width)],
+                out=x_codes[:, chunk_columns(c)].bitcast(FP8X4),
+                scales=x_plane[:, chunk_columns(c)],
+                in_=x_bf[:, chunk_columns(c, SLOTS)],
             )
 
-        def w4_passes(u, banks):
-            a, t0, width = D_TILES[u]
+        def place_d(u):
+            banks = next_banks("d%d" % u, D_BANKS[u])
             per_bank = SLOTS // len(banks)
-            for n, number in enumerate(banks):
-                acc = bank("d%d_%d" % (u, n), number)
-                for s in range(per_bank):
-                    d_out[u, per_bank * n + s] = acc[:, width * s : width * (s + 1)]
-                    w4_slot(u, per_bank * n + s, s == 0)
-
-        def w4_slot(u, i, opens):
-            a, t0, width = D_TILES[u]
-            step = width if width == PASS else FP4_COLUMNS
-            for c0 in range(0, width, step):
-                cols = slice(t0 + c0, t0 + c0 + step)
-                nc.tensor.matmul_mx(
-                    out=d_out[u, i][:, c0 : c0 + step],
-                    lhsT=w4_sorted[a][:, 2 * P * i : 2 * P * (i + 1)].bitcast(FP4X4),
-                    lhsT_scale=w4_plane[a][:, P * i : P * (i + 1)],
-                    rhs=x_codes[:, cols].bitcast(FP8X4),
-                    rhs_scale=x_plane[:, cols],
-                    start=(opens and c0 == 0),
-                    stop=False,
-                )
-
-        def r8_slot(u, i, closes):
-            a, t0, width = D_TILES[u]
-            cols = slice(t0, t0 + width)
-            nc.tensor.matmul_mx(
-                out=d_out[u, i],
-                lhsT=r8_sorted[a][:, P * i : P * (i + 1)].bitcast(FP8X4),
-                lhsT_scale=r8_plane[a][:, P * i : P * (i + 1)],
-                rhs=x_codes[:, cols].bitcast(FP8X4),
-                rhs_scale=x_plane[:, cols],
-                start=False,
-                stop=closes,
-            )
-
-        def r8_passes(u, bank_count):
-            per_bank = SLOTS // bank_count
             for i in range(SLOTS):
-                r8_slot(u, i, i % per_bank == per_bank - 1)
+                d_sums[u, i] = banks[i // per_bank][:, chunk_columns(i % per_bank)]
+            return per_bank
 
-        def first_product(u, banks):
-            a, t0, width = D_TILES[u]
-            per_bank = SLOTS // len(banks)
-            for n, number in enumerate(banks):
-                acc = bank("d%d_%d" % (u, n), number)
-                for s in range(per_bank):
-                    i = per_bank * n + s
-                    d_out[u, i] = acc[:, width * s : width * (s + 1)]
-                    w4_slot(u, i, s == 0)
-                    r8_slot(u, i, s == per_bank - 1)
+        def d_pass(u, i, words, plane, start, stop):
+            c = u // J_PASSES
+            nc.tensor.matmul_mx(
+                out=d_sums[u, i],
+                lhsT=words,
+                lhsT_scale=plane[:, P * i : P * (i + 1)],
+                rhs=x_codes[:, chunk_columns(c)].bitcast(FP8X4),
+                rhs_scale=x_plane[:, chunk_columns(c)],
+                start=start,
+                stop=stop,
+            )
 
-        def square(u, t0, width, slots=range(SLOTS)):
-            a, tile_t0 = D_TILES[u][:2]
-            for i in slots:
-                col = SLOTS * a + i
+        def w4_pass(u, i, per_bank):
+            a = u % J_PASSES
+            words = w4_sorted[a][:, 2 * P * i : 2 * P * (i + 1)].bitcast(FP4X4)
+            d_pass(u, i, words, w4_plane[a], i % per_bank == 0, False)
+
+        def r8_pass(u, i, per_bank):
+            a = u % J_PASSES
+            words = r8_sorted[a][:, P * i : P * (i + 1)].bitcast(FP8X4)
+            d_pass(u, i, words, r8_plane[a], False, i % per_bank == per_bank - 1)
+
+        def first_product(u):
+            per_bank = place_d(u)
+            for i in range(SLOTS):
+                w4_pass(u, i, per_bank)
+                r8_pass(u, i, per_bank)
+
+        def square(u):
+            for i in range(SLOTS):
+                col = SLOTS * (u % J_PASSES) + i
                 nc.scalar.activation(
-                    out=squares[u][:, i, t0 - tile_t0 : t0 - tile_t0 + width],
-                    in_=d_out[u, i][:, t0 - tile_t0 : t0 - tile_t0 + width],
-                    func=ACT.Square,
-                    bias=cb_sb[:, col : col + 1],
+                    out=squares[u][:, i, :], in_=d_sums[u, i], func=ACT.Square, bias=cb_sb[:, col : col + 1]
                 )
 
-        def weigh(u, t0, width):
-            a, tile_t0 = D_TILES[u][:2]
+        def weigh(u):
+            c, a = divmod(u, J_PASSES)
             weights = cw_sb[:, SLOTS * a : SLOTS * (a + 1)].unsqueeze(1).unsqueeze(3)
             nc.vector.tensor_tensor(
-                out=interleaved(h_bf[a][:, SLOTS * t0 : SLOTS * (t0 + width)]),
-                in0=by_slot(squares[u][:, :, t0 - tile_t0 : t0 - tile_t0 + width]),
-                in1=weights.to_broadcast([P, width // 2, SLOTS, 2]),
+                out=interleaved(h_bf[a][:, chunk_columns(c, SLOTS)]),
+                in0=by_slot(squares[u][:]),
+                in1=weights.to_broadcast([P, CHUNK // RUN, SLOTS, RUN]),
                 op=ALU.mult,
             )
 
-        def quantize_h(a, t0, width):
-            cols = slice(t0, t0 + width)
+        def quantize_h(u):
+            c, a = divmod(u, J_PASSES)
             nc.vector.quantize_mx(
-                out=h_codes[a][:, cols].bitcast(FP8X4),
-                scales=h_plane[a][:, cols],
-                in_=h_bf[a][:, SLOTS * t0 : SLOTS * (t0 + width)],
+                out=h_codes[a][:, chunk_columns(c)].bitcast(FP8X4),
+                scales=h_plane[a][:, chunk_columns(c)],
+                in_=h_bf[a][:, chunk_columns(c, SLOTS)],
             )
 
-        def second_product(r, a, banks=None, halves=(0, 1)):
+        def place_y(r):
+            y_banks[r] = next_banks("y%d" % r, 2)
+
+        def y_passes(r, a, half):
             t0, width = Y_RANGES[r]
             cols = slice(t0, t0 + width)
-            if banks:
-                y_out[r] = [bank("y%d_%d" % (r, half), number) for half, number in enumerate(banks)]
-            for n in range(2 * halves[0], 2 * halves[-1] + 2):
-                first = N * a + P * n
-                half, s = divmod(n, 2)
+            for s in range(HALF_ROWS):
+                first = N * a + P * (HALF_ROWS * half + s)
                 nc.tensor.matmul_mx(
-                    out=y_out[r][half][:, width * s : width * (s + 1)],
+                    out=y_banks[r][half][:, width * s : width * (s + 1)],
                     lhsT=v8_sb[:, first : first + P].bitcast(FP8X4),
                     lhsT_scale=v8_plane[:, first : first + P],
                     rhs=h_codes[a][:, cols].bitcast(FP8X4),
                     rhs_scale=h_plane[a][:, cols],
                     start=(a == 0 and s == 0),
-                    stop=(a == J_PASSES - 1 and s == 1),
+                    stop=(a == J_PASSES - 1 and s == HALF_ROWS - 1),
                 )
 
-        def store(queue, r, half, s0=0, count=2):
+        def second_product_behind(u):
+            c, a = divmod(u, J_PASSES)
+            if u == FIRST_RANGE_TILES - 1:
+                place_y(0)
+                for half in range(2):
+                    for each_a in range(J_PASSES):
+                        y_passes(0, each_a, half)
+            elif u >= FIRST_RANGE_TILES:
+                r = [t0 for t0, width in Y_RANGES].index(CHUNK * c)
+                if a == 0:
+                    place_y(r)
+                for half in range(2):
+                    y_passes(r, a, half)
+
+        def store(queue, r, half, s0, count):
             t0, width = Y_RANGES[r]
-            rows = out.rearrange("(n p) t -> p n t", p=P)
-            n0 = 2 * half + s0
+            n0 = HALF_ROWS * half + s0
             queue.dma_start(
-                out=rows[:, n0 : n0 + count, t0 : t0 + width], in_=y_sb[2 * r + half][:, s0 : s0 + count, :]
+                out=out.rearrange("(n p) t -> p n t", p=P)[:, n0 : n0 + count, t0 : t0 + width],
+                in_=y_sb[2 * r + half][:, s0 : s0 + count, :],
             )
 
-        def finish_on_scalar(queue, r, half, singly=False):
+        def add_bias_on_scalar(r, half, s):
             width = Y_RANGES[r][1]
-            for s in range(2):
-                n = 2 * half + s
-                nc.scalar.activation(
-                    out=y_sb[2 * r + half][:, s, :],
-                    in_=y_out[r][half][:, width * s : width * (s + 1)],
-                    func=ACT.Identity,
-                    bias=b_sb[:, n : n + 1],
-                )
-                if singly:
-                    store(queue, r, half, s, 1)
-            if not singly:
-                store(queue, r, half)
+            n = HALF_ROWS * half + s
+            nc.scalar.activation(
+                out=y_sb[2 * r + half][:, s, :],
+                in_=y_banks[r][half][:, width * s : width * (s + 1)],
+                func=ACT.Identity,
+                bias=b_sb[:, n : n + 1],
+            )
 
-        def finish_on_vector(r, half):
+        def add_bias_on_vector(r, half):
             width = Y_RANGES[r][1]
-            sums = y_out[r][half][:, : 2 * width].rearrange("p (n t) -> p n t", n=2)
-            biases = b_sb[:, 2 * half : 2 * half + 2].unsqueeze(2).to_broadcast([P, 2, width])
-            nc.vector.tensor_tensor(out=y_sb[2 * r + half][:], in0=sums, in1=biases, op=ALU.add)
-            store(nc.sync, r, half)
+            sums = y_banks[r][half][:, : HALF_ROWS * width].rearrange("p (s t) -> p s t", s=HALF_ROWS)
+            biases = b_sb[:, HALF_ROWS * half : HALF_ROWS * (half + 1)].unsqueeze(2)
+            nc.vector.tensor_tensor(
+                out=y_sb[2 * r + half][:], in0=sums, in1=biases.to_broadcast([P, HALF_ROWS, width]), op=ALU.add
+            )
 
         nc.vector.memset(w4_plane_in[:].bitcast(I32), 0)
         nc.gpsimd.memset(r8_plane_in[:].bitcast(I32), 0)
         nc.gpsimd.memset(v8_plane[:].bitcast(I32), 0)
 
-        load_x(nc.sync, 0)
-        load_w4(nc.sync)
-        load_plane(nc.sync, w4_plane_in, w4_scales)
-        load_r8(nc.sync)
-        load_x(nc.sync, 1)
-        load_plane(nc.sync, r8_plane_in, r8_scales)
+        load_x(0)
+        nc.sync.dma_start(out=w4_in[:].bitcast(I32), in_=w4_words[0].bitcast(I32))
+        load_plane(w4_plane_in, w4_scales)
+        nc.sync.dma_start(out=r8_in[:], in_=r8_words[0].rearrange("p j i -> p (j i)").bitcast(I32))
+        load_x(1)
+        load_plane(r8_plane_in, r8_scales)
         load_by_slot(cb_sb, cb)
-        load_x(nc.sync, 2)
-        load_x(nc.sync, 3)
+        load_x(2)
+        load_x(3)
         load_by_slot(cw_sb, cw)
-        load_v8()
-        load_plane(nc.sync, v8_plane, v8_scales)
-        load_b()
+        nc.sync.dma_start(
+            out=v8_sb[:].rearrange("p (a n) -> p a n", a=J_PASSES),
+            in_=v8_words.rearrange("a p n i -> p a (n i)").bitcast(I32),
+        )
+        load_plane(v8_plane, v8_scales)
+        with nc.allow_non_contiguous_dma(reason="one bias value for each partition"):
+            nc.sync.dma_start(out=b_sb[:], in_=b.rearrange("(n p) -> p n", p=P))
 
-        round_x_on_scalar(0, 0, 128)
-        round_x_on_scalar(1, 128, 128)
-        sort_w4(0)
-        sort_plane(w4_plane, w4_plane_in, 0)
-        quantize_x(0, 128)
-        w4_passes(0, (0, 1, 2, 3))
-        sort_w4(1)
-        sort_plane(w4_plane, w4_plane_in, 1)
-        w4_passes(1, (4, 5))
-        sort_r8(0)
-        sort_r8(1)
-        sort_plane(r8_plane, r8_plane_in, 0)
-        r8_passes(0, 4)
+        round_x_on_scalar(0)
+        round_x_on_scalar(1)
+        slots_in_bank = {}
+        for a in range(J_PASSES):
+            sort_w4(a)
+            sort_plane(w4_plane, w4_plane_in, a)
+            if a == 0:
+                quantize_x(0)
+            slots_in_bank[a] = place_d(a)
+            for i in range(SLOTS):
+                w4_pass(a, i, slots_in_bank[a])
+        for a in range(J_PASSES):
+            sort_r8(a)
+        sort_plane(r8_plane, r8_plane_in, 0, slice(0, SLOTS // 2))
+        sort_plane(r8_plane, r8_plane_in, 0, slice(SLOTS // 2, SLOTS))
         sort_plane(r8_plane, r8_plane_in, 1)
-        r8_passes(1, 2)
-        quantize_x(128, 128)
-        first_product(2, (6, 7))
-        round_x_on_vector(2, 256, 128)
-        quantize_x(256, 128)
-        square(0, 0, 128)
-        first_product(3, (0, 1))
-        round_x_on_vector(3, 384, 128)
-        weigh(0, 0, 128)
-        quantize_x(384, 128)
-        first_product(4, (2, 3))
-        square(1, 0, 128)
-        first_product(5, (4, 5))
-        weigh(1, 0, 128)
-        quantize_h(0, 0, 128)
-        square(2, 128, 128)
-        first_product(6, (6, 7))
-        weigh(2, 128, 128)
-        quantize_h(1, 0, 128)
-        square(3, 128, 128)
-        first_product(7, (0, 1))
-        weigh(3, 128, 128)
-        quantize_h(0, 128, 128)
-        square(4, 256, 128)
-        weigh(4, 256, 128)
-        quantize_h(1, 128, 128)
-        second_product(0, 0, (2, 3), (0,))
-        second_product(0, 1, None, (0,))
-        second_product(0, 0, None, (1,))
-        second_product(0, 1, None, (1,))
-        square(5, 256, 128)
-        weigh(5, 256, 128)
-        quantize_h(0, 256, 128)
-        second_product(1, 0, (4, 5))
-        square(6, 384, 128)
-        square(7, 384, 128)
-        weigh(6, 384, 128)
-        quantize_h(1, 256, 128)
-        second_product(1, 1)
-        weigh(7, 384, 128)
-        quantize_h(0, 384, 128)
-        second_product(2, 0, (6, 7))
-        quantize_h(1, 384, 128)
-        second_product(2, 1)
-        finish_on_scalar(nc.sync, 0, 0, True)
-        finish_on_scalar(nc.sync, 0, 1)
-        finish_on_scalar(nc.sync, 1, 0)
-        finish_on_vector(1, 1)
-        finish_on_scalar(nc.scalar, 2, 0)
-        finish_on_vector(2, 1)
+        for a in range(J_PASSES):
+            for i in range(SLOTS):
+                r8_pass(a, i, slots_in_bank[a])
+        quantize_x(1)
+        first_product(2)
+        round_x_on_vector(2)
+        quantize_x(2)
+        round_x_on_vector(3)
+
+        for u in range(D_TILES):
+            square(u)
+            if u + LEAD < D_TILES:
+                first_product(u + LEAD)
+            weigh(u)
+            if u == 0:
+                quantize_x(CHUNKS - 1)
+            else:
+                quantize_h(u - 1)
+                second_product_behind(u - 1)
+        quantize_h(D_TILES - 1)
+        second_product_behind(D_TILES - 1)
+
+        for half in range(2):
+            for s in range(HALF_ROWS):
+                add_bias_on_scalar(0, half, s)
+                store(nc.sync, 0, half, s, 1)
+        for r in range(1, len(Y_RANGES)):
+            for s in range(HALF_ROWS):
+                add_bias_on_scalar(r, 0, s)
+            store(nc.scalar if r == len(Y_RANGES) - 1 else nc.sync, r, 0, 0, HALF_ROWS)
+            add_bias_on_vector(r, 1)
+            store(nc.sync, r, 1, 0, HALF_ROWS)

@@ -32,7 +32,7 @@ RUN = 2
 
 Y_RANGES = ((0, 2 * CHUNK), (2 * CHUNK, CHUNK), (3 * CHUNK, CHUNK))
 FIRST_RANGE_TILES = J_PASSES * Y_RANGES[0][1] // CHUNK
-HALF_ROWS = 2
+Y_BANK_GROUPS = (((0, 1), (2, 3)), ((0, 1), (2, 3)), ((0,), (1,), (2, 3)))
 
 
 def tile_mix_kern_resid_poly2_bias_kernel(
@@ -80,7 +80,10 @@ def tile_mix_kern_resid_poly2_bias_kernel(
         h_bf = tiles("h_bf", [[P, SLOTS * T]] * J_PASSES, BF16)
         h_codes = tiles("h_codes", [[P, T]] * J_PASSES, U32)
         h_plane = tiles("h_plane", [[P, T]] * J_PASSES, U8)
-        y_sb = tiles("y_sb", [[P, HALF_ROWS, width] for t0, width in Y_RANGES for half in range(2)], F32)
+        y_sb = [
+            tiles("y_sb%d_" % r, [[P, len(groups), width] for groups in Y_BANK_GROUPS[r]], F32)
+            for r, (t0, width) in enumerate(Y_RANGES)
+        ]
         banks_given, d_sums, y_banks = [], {}, {}
 
         def chunk_columns(c, per_column=1):
@@ -201,63 +204,63 @@ def tile_mix_kern_resid_poly2_bias_kernel(
                 in_=h_bf[a][:, chunk_columns(c, SLOTS)],
             )
 
-        def place_y(r):
-            y_banks[r] = next_banks("y%d" % r, 2)
-
-        def y_passes(r, a, half):
+        def y_passes(r, a, m):
             t0, width = Y_RANGES[r]
             cols = slice(t0, t0 + width)
-            for s in range(HALF_ROWS):
-                first = N * a + P * (HALF_ROWS * half + s)
+            groups = Y_BANK_GROUPS[r][m]
+            for s, n in enumerate(groups):
+                first = N * a + P * n
                 nc.tensor.matmul_mx(
-                    out=y_banks[r][half][:, width * s : width * (s + 1)],
+                    out=y_banks[r][m][:, width * s : width * (s + 1)],
                     lhsT=v8_sb[:, first : first + P].bitcast(FP8X4),
                     lhsT_scale=v8_plane[:, first : first + P],
                     rhs=h_codes[a][:, cols].bitcast(FP8X4),
                     rhs_scale=h_plane[a][:, cols],
                     start=(a == 0 and s == 0),
-                    stop=(a == J_PASSES - 1 and s == HALF_ROWS - 1),
+                    stop=(a == J_PASSES - 1 and s == len(groups) - 1),
                 )
 
         def second_product_behind(u):
             c, a = divmod(u, J_PASSES)
             if u == FIRST_RANGE_TILES - 1:
-                place_y(0)
-                for half in range(2):
+                y_banks[0] = next_banks("y0", len(Y_BANK_GROUPS[0]))
+                for m in range(len(y_banks[0])):
                     for each_a in range(J_PASSES):
-                        y_passes(0, each_a, half)
+                        y_passes(0, each_a, m)
             elif u >= FIRST_RANGE_TILES:
                 r = [t0 for t0, width in Y_RANGES].index(CHUNK * c)
                 if a == 0:
-                    place_y(r)
-                for half in range(2):
-                    y_passes(r, a, half)
+                    y_banks[r] = next_banks("y%d" % r, len(Y_BANK_GROUPS[r]))
+                for m in range(len(y_banks[r])):
+                    y_passes(r, a, m)
 
-        def store(queue, r, half, s0, count):
+        def store(queue, r, m, s0, count):
             t0, width = Y_RANGES[r]
-            n0 = HALF_ROWS * half + s0
+            n0 = Y_BANK_GROUPS[r][m][s0]
             queue.dma_start(
                 out=out.rearrange("(n p) t -> p n t", p=P)[:, n0 : n0 + count, t0 : t0 + width],
-                in_=y_sb[2 * r + half][:, s0 : s0 + count, :],
+                in_=y_sb[r][m][:, s0 : s0 + count, :],
             )
 
-        def add_bias_on_scalar(r, half, s):
+        def add_bias_on_scalar(r, m, s):
             width = Y_RANGES[r][1]
-            n = HALF_ROWS * half + s
+            n = Y_BANK_GROUPS[r][m][s]
             nc.scalar.activation(
-                out=y_sb[2 * r + half][:, s, :],
-                in_=y_banks[r][half][:, width * s : width * (s + 1)],
+                out=y_sb[r][m][:, s, :],
+                in_=y_banks[r][m][:, width * s : width * (s + 1)],
                 func=ACT.Identity,
                 bias=b_sb[:, n : n + 1],
             )
 
-        def add_bias_on_vector(r, half):
-            width = Y_RANGES[r][1]
-            sums = y_banks[r][half][:, : HALF_ROWS * width].rearrange("p (s t) -> p s t", s=HALF_ROWS)
-            biases = b_sb[:, HALF_ROWS * half : HALF_ROWS * (half + 1)].unsqueeze(2)
+        def finish_on_vector(r, m):
+            width, groups = Y_RANGES[r][1], Y_BANK_GROUPS[r][m]
             nc.vector.tensor_tensor(
-                out=y_sb[2 * r + half][:], in0=sums, in1=biases.to_broadcast([P, HALF_ROWS, width]), op=ALU.add
+                out=y_sb[r][m][:],
+                in0=y_banks[r][m][:, : len(groups) * width].rearrange("p (s t) -> p s t", s=len(groups)),
+                in1=b_sb[:, groups[0] : groups[-1] + 1].unsqueeze(2).to_broadcast([P, len(groups), width]),
+                op=ALU.add,
             )
+            store(nc.sync, r, m, 0, len(groups))
 
         nc.vector.memset(w4_plane_in[:].bitcast(I32), 0)
         nc.gpsimd.memset(r8_plane_in[:].bitcast(I32), 0)
@@ -319,13 +322,15 @@ def tile_mix_kern_resid_poly2_bias_kernel(
         quantize_h(D_TILES - 1)
         second_product_behind(D_TILES - 1)
 
-        for half in range(2):
-            for s in range(HALF_ROWS):
-                add_bias_on_scalar(0, half, s)
-                store(nc.sync, 0, half, s, 1)
-        for r in range(1, len(Y_RANGES)):
-            for s in range(HALF_ROWS):
-                add_bias_on_scalar(r, 0, s)
-            store(nc.scalar if r == len(Y_RANGES) - 1 else nc.sync, r, 0, 0, HALF_ROWS)
-            add_bias_on_vector(r, 1)
-            store(nc.sync, r, 1, 0, HALF_ROWS)
+        for m in range(2):
+            for s in range(2):
+                add_bias_on_scalar(0, m, s)
+                store(nc.sync, 0, m, s, 1)
+        for s in range(2):
+            add_bias_on_scalar(1, 0, s)
+        store(nc.sync, 1, 0, 0, 2)
+        finish_on_vector(1, 1)
+        for m, queue in enumerate((nc.sync, nc.scalar)):
+            add_bias_on_scalar(2, m, 0)
+            store(queue, 2, m, 0, 1)
+        finish_on_vector(2, 2)

@@ -60,9 +60,9 @@ def tile_mix_kern_resid_poly2_bias_kernel(
             return banks_given[first:]
 
         w4_plane_in = one_tile("w4_plane_in", [P, J], U8)
-        r8_plane_in = one_tile("r8_plane_in", [P, J], U8)
+        r8_plane_in = one_tile("r8_plane_in", [P, PASS], U8)
         w4_plane = tiles("w4_plane", [[P, PASS]] * J_PASSES, U8)
-        r8_plane = tiles("r8_plane", [[P, PASS]] * J_PASSES, U8)
+        r8_plane = one_tile("r8_plane", [P, PASS], U8)
         v8_plane = one_tile("v8_plane", [P, J_PASSES * N], U8)
         w4_in = one_tile("w4_in", [P, 2 * J], U8)
         w4_sorted = tiles("w4_sorted", [[P, 2 * PASS]] * J_PASSES, U8)
@@ -77,9 +77,9 @@ def tile_mix_kern_resid_poly2_bias_kernel(
         x_codes = one_tile("x_codes", [P, T], U32)
         x_plane = one_tile("x_plane", [P, T], U8)
         squares = tiles("squares", [[P, SLOTS, CHUNK]] * D_TILES, F32)
-        h_bf = tiles("h_bf", [[P, SLOTS * T]] * J_PASSES, BF16)
-        h_codes = tiles("h_codes", [[P, T]] * J_PASSES, U32)
-        h_plane = tiles("h_plane", [[P, T]] * J_PASSES, U8)
+        h_bf = one_tile("h_bf", [P, SLOTS * CHUNK * D_TILES], BF16)
+        h_codes = one_tile("h_codes", [P, CHUNK * D_TILES], U32)
+        h_plane = one_tile("h_plane", [P, CHUNK * D_TILES], U8)
         y_sb = [
             tiles("y_sb%d_" % r, [[P, len(groups), width] for groups in Y_BANK_GROUPS[r]], F32)
             for r, (t0, width) in enumerate(Y_RANGES)
@@ -100,6 +100,14 @@ def tile_mix_kern_resid_poly2_bias_kernel(
                     in_=scales[:, 4 * quadrant : 4 * quadrant + 4, :].bitcast(I32).rearrange("a r n -> r a n"),
                 )
 
+        def load_packed_plane(dst, scales):
+            for quadrant in range(QUADRANTS):
+                row = 32 * quadrant
+                nc.sync.dma_start(
+                    out=dst[row : row + 4 * J_PASSES, :].bitcast(I32),
+                    in_=scales[0, 4 * quadrant : 4 * quadrant + 4, :].bitcast(I32).rearrange("r (a n) -> a r n", a=J_PASSES),
+                )
+
         def load_by_slot(dst, vec):
             nc.sync.dma_start(
                 out=dst[:].rearrange("p (a i) -> p a i", i=SLOTS), in_=vec.rearrange("(a p i) -> p a i", p=P, i=SLOTS)
@@ -117,10 +125,10 @@ def tile_mix_kern_resid_poly2_bias_kernel(
                 in_=r8_in[:, PASS * a : PASS * (a + 1)].rearrange("p (m e i) -> p m i e", i=SLOTS, e=4),
             )
 
-        def sort_plane(dst, src, a, slots=slice(0, SLOTS)):
+        def sort_plane(dst, src, slots=slice(0, SLOTS)):
             nc.vector.tensor_copy(
-                out=dst[a][:].rearrange("p (i m) -> p i m", i=SLOTS)[:, slots, :],
-                in_=src[:, PASS * a : PASS * (a + 1)].rearrange("p (m i) -> p i m", i=SLOTS)[:, slots, :],
+                out=dst.rearrange("p (i m) -> p i m", i=SLOTS)[:, slots, :],
+                in_=src.rearrange("p (m i) -> p i m", i=SLOTS)[:, slots, :],
             )
 
         def interleaved(dst):
@@ -171,7 +179,7 @@ def tile_mix_kern_resid_poly2_bias_kernel(
         def r8_pass(u, i, per_bank):
             a = u % J_PASSES
             words = r8_sorted[a][:, P * i : P * (i + 1)].bitcast(FP8X4)
-            d_pass(u, i, words, r8_plane[a], False, i % per_bank == per_bank - 1)
+            d_pass(u, i, words, r8_plane[4 * a :, :], False, i % per_bank == per_bank - 1)
 
         def first_product(u):
             per_bank = place_d(u)
@@ -190,49 +198,41 @@ def tile_mix_kern_resid_poly2_bias_kernel(
             c, a = divmod(u, J_PASSES)
             weights = cw_sb[:, SLOTS * a : SLOTS * (a + 1)].unsqueeze(1).unsqueeze(3)
             nc.vector.tensor_tensor(
-                out=interleaved(h_bf[a][:, chunk_columns(c, SLOTS)]),
+                out=interleaved(h_bf[:, chunk_columns(u, SLOTS)]),
                 in0=by_slot(squares[u][:]),
                 in1=weights.to_broadcast([P, CHUNK // RUN, SLOTS, RUN]),
                 op=ALU.mult,
             )
 
-        def quantize_h(u):
-            c, a = divmod(u, J_PASSES)
+        def quantize_h(u, count):
+            cols = slice(CHUNK * u, CHUNK * (u + count))
             nc.vector.quantize_mx(
-                out=h_codes[a][:, chunk_columns(c)].bitcast(FP8X4),
-                scales=h_plane[a][:, chunk_columns(c)],
-                in_=h_bf[a][:, chunk_columns(c, SLOTS)],
+                out=h_codes[:, cols].bitcast(FP8X4),
+                scales=h_plane[:, cols],
+                in_=h_bf[:, SLOTS * CHUNK * u : SLOTS * CHUNK * (u + count)],
             )
 
-        def y_passes(r, a, m):
+        def y_passes(tiles_of_h):
+            r = max(n for n, (t0, width) in enumerate(Y_RANGES) if t0 <= CHUNK * (tiles_of_h[0] // J_PASSES))
             t0, width = Y_RANGES[r]
-            cols = slice(t0, t0 + width)
-            groups = Y_BANK_GROUPS[r][m]
-            for s, n in enumerate(groups):
-                first = N * a + P * n
-                nc.tensor.matmul_mx(
-                    out=y_banks[r][m][:, width * s : width * (s + 1)],
-                    lhsT=v8_sb[:, first : first + P].bitcast(FP8X4),
-                    lhsT_scale=v8_plane[:, first : first + P],
-                    rhs=h_codes[a][:, cols].bitcast(FP8X4),
-                    rhs_scale=h_plane[a][:, cols],
-                    start=(a == 0 and s == 0),
-                    stop=(a == J_PASSES - 1 and s == len(groups) - 1),
-                )
-
-        def second_product_behind(u):
-            c, a = divmod(u, J_PASSES)
-            if u == FIRST_RANGE_TILES - 1:
-                y_banks[0] = next_banks("y0", len(Y_BANK_GROUPS[0]))
-                for m in range(len(y_banks[0])):
-                    for each_a in range(J_PASSES):
-                        y_passes(0, each_a, m)
-            elif u >= FIRST_RANGE_TILES:
-                r = [t0 for t0, width in Y_RANGES].index(CHUNK * c)
-                if a == 0:
-                    y_banks[r] = next_banks("y%d" % r, len(Y_BANK_GROUPS[r]))
-                for m in range(len(y_banks[r])):
-                    y_passes(r, a, m)
+            if r not in y_banks:
+                y_banks[r] = next_banks("y%d" % r, len(Y_BANK_GROUPS[r]))
+            first_tile, last_tile = J_PASSES * t0 // CHUNK, J_PASSES * (t0 + width) // CHUNK - 1
+            for m, groups in enumerate(Y_BANK_GROUPS[r]):
+                for u in tiles_of_h:
+                    c, a = divmod(u, J_PASSES)
+                    for s, n in enumerate(groups):
+                        first = N * a + P * n
+                        column = width * s + CHUNK * c - t0
+                        nc.tensor.matmul_mx(
+                            out=y_banks[r][m][:, column : column + CHUNK],
+                            lhsT=v8_sb[:, first : first + P].bitcast(FP8X4),
+                            lhsT_scale=v8_plane[:, first : first + P],
+                            rhs=h_codes[:, chunk_columns(u)].bitcast(FP8X4),
+                            rhs_scale=h_plane[:, chunk_columns(u)],
+                            start=(u == first_tile and s == 0),
+                            stop=(u == last_tile and s == len(groups) - 1),
+                        )
 
         def store(queue, r, m, s0, count):
             t0, width = Y_RANGES[r]
@@ -271,7 +271,7 @@ def tile_mix_kern_resid_poly2_bias_kernel(
         load_plane(w4_plane_in, w4_scales)
         nc.sync.dma_start(out=r8_in[:], in_=r8_words[0].rearrange("p j i -> p (j i)").bitcast(I32))
         load_x(1)
-        load_plane(r8_plane_in, r8_scales)
+        load_packed_plane(r8_plane_in, r8_scales)
         load_by_slot(cb_sb, cb)
         load_x(2)
         load_x(3)
@@ -289,7 +289,7 @@ def tile_mix_kern_resid_poly2_bias_kernel(
         slots_in_bank = {}
         for a in range(J_PASSES):
             sort_w4(a)
-            sort_plane(w4_plane, w4_plane_in, a)
+            sort_plane(w4_plane[a][:], w4_plane_in[:, PASS * a : PASS * (a + 1)])
             if a == 0:
                 quantize_x(0)
             slots_in_bank[a] = place_d(a)
@@ -297,9 +297,8 @@ def tile_mix_kern_resid_poly2_bias_kernel(
                 w4_pass(a, i, slots_in_bank[a])
         for a in range(J_PASSES):
             sort_r8(a)
-        sort_plane(r8_plane, r8_plane_in, 0, slice(0, SLOTS // 2))
-        sort_plane(r8_plane, r8_plane_in, 0, slice(SLOTS // 2, SLOTS))
-        sort_plane(r8_plane, r8_plane_in, 1)
+        sort_plane(r8_plane[:], r8_plane_in[:], slice(0, SLOTS // 2))
+        sort_plane(r8_plane[:], r8_plane_in[:], slice(SLOTS // 2, SLOTS))
         for a in range(J_PASSES):
             for i in range(SLOTS):
                 r8_pass(a, i, slots_in_bank[a])
@@ -316,11 +315,16 @@ def tile_mix_kern_resid_poly2_bias_kernel(
             weigh(u)
             if u == 0:
                 quantize_x(CHUNKS - 1)
-            else:
-                quantize_h(u - 1)
-                second_product_behind(u - 1)
-        quantize_h(D_TILES - 1)
-        second_product_behind(D_TILES - 1)
+            elif u % 2 == 0:
+                quantize_h(u - 2, 2)
+            if u == 4:
+                y_passes((0, 1))
+                y_passes((2, 3))
+            if u == 6:
+                y_passes((4, 5))
+        for u in range(D_TILES - 2, D_TILES):
+            quantize_h(u, 1)
+            y_passes((u,))
 
         for m in range(2):
             for s in range(2):

@@ -31,6 +31,7 @@ LEAD = 3
 RUN = 2
 
 Y_RANGES = ((0, 2 * CHUNK), (2 * CHUNK, CHUNK), (3 * CHUNK, CHUNK))
+BLOCK_WORDS = 8
 FIRST_RANGE_TILES = J_PASSES * Y_RANGES[0][1] // CHUNK
 Y_BANK_GROUPS = (((0, 1), (2, 3)), ((0, 1), (2, 3)), ((0,), (1,), (2, 3)))
 
@@ -69,8 +70,8 @@ def tile_mix_kern_resid_poly2_bias_kernel(
         r8_in = one_tile("r8_in", [P, J], I32)
         r8_sorted = tiles("r8_sorted", [[P, PASS]] * J_PASSES, I32)
         v8_sb = one_tile("v8_sb", [P, J_PASSES * N], I32)
-        cw_sb = one_tile("cw_sb", [P, J_PASSES * SLOTS], F32)
-        cb_sb = one_tile("cb_sb", [P, J_PASSES * SLOTS], F32)
+        cw_sb = one_tile("cw_sb", [P, J_PASSES, BLOCK_WORDS], F32)
+        cb_sb = one_tile("cb_sb", [P, J_PASSES, BLOCK_WORDS], F32)
         b_sb = one_tile("b_sb", [P, N // P], F32)
         x_in = tiles("x_in", [[P, SLOTS, CHUNK]] * CHUNKS, F32)
         x_bf = one_tile("x_bf", [P, SLOTS * T], BF16)
@@ -110,7 +111,7 @@ def tile_mix_kern_resid_poly2_bias_kernel(
 
         def load_by_slot(dst, vec):
             nc.sync.dma_start(
-                out=dst[:].rearrange("p (a i) -> p a i", i=SLOTS), in_=vec.rearrange("(a p i) -> p a i", p=P, i=SLOTS)
+                out=dst[:, :, :SLOTS], in_=vec.rearrange("(a p i) -> p a i", p=P, i=SLOTS)
             )
 
         def sort_w4(a):
@@ -189,14 +190,13 @@ def tile_mix_kern_resid_poly2_bias_kernel(
 
         def square(u):
             for i in range(SLOTS):
-                col = SLOTS * (u % J_PASSES) + i
                 nc.scalar.activation(
-                    out=squares[u][:, i, :], in_=d_sums[u, i], func=ACT.Square, bias=cb_sb[:, col : col + 1]
+                    out=squares[u][:, i, :], in_=d_sums[u, i], func=ACT.Square, bias=cb_sb[:, u % J_PASSES, i : i + 1]
                 )
 
         def weigh(u):
             c, a = divmod(u, J_PASSES)
-            weights = cw_sb[:, SLOTS * a : SLOTS * (a + 1)].unsqueeze(1).unsqueeze(3)
+            weights = cw_sb[:, a, :SLOTS].unsqueeze(1).unsqueeze(3)
             nc.vector.tensor_tensor(
                 out=interleaved(h_bf[:, chunk_columns(u, SLOTS)]),
                 in0=by_slot(squares[u][:]),
@@ -334,7 +334,7 @@ def tile_mix_kern_resid_poly2_bias_kernel(
             add_bias_on_scalar(1, 0, s)
         store(nc.sync, 1, 0, 0, 2)
         finish_on_vector(1, 1)
-        for m, queue in enumerate((nc.sync, nc.scalar)):
+        for m, queue in enumerate((nc.sync, nc.sync)):
             add_bias_on_scalar(2, m, 0)
             store(queue, 2, m, 0, 1)
         finish_on_vector(2, 2)

@@ -25,15 +25,19 @@ BANK_COLUMNS = 512
 PSUM_BANKS = 8
 CHUNK = 128
 CHUNKS = T // CHUNK
-D_TILES = J_PASSES * CHUNKS
+TILES = ((0, 0, 1), (1, 0, 1), (0, 1, 1), (1, 1, 1), (2, 0, 1), (2, 1, 1), (3, 0, 1), (3, 1, 1))
+D_TILES = len(TILES)
+H_FIRST = [sum(tile[2] for tile in TILES[:u]) for u in range(D_TILES + 1)]
+W4_LOADS = ((0, 2),)
+R8_LOADS = ((0, 1), (1, 1))
+X_LOADS = ((0, 1), (1, 2), (3, 1))
 D_BANKS = (4, 2, 2, 2, 1, 1, 1, 1)
 LEAD = 3
 RUN = 2
 
 Y_RANGES = ((0, 2 * CHUNK), (2 * CHUNK, CHUNK), (3 * CHUNK, CHUNK))
 BLOCK_WORDS = 8
-FIRST_RANGE_TILES = J_PASSES * Y_RANGES[0][1] // CHUNK
-Y_BANK_GROUPS = (((0, 1), (2, 3)), ((0, 1), (2, 3)), ((0,), (1,), (2, 3)))
+Y_BANK_GROUPS = (((0, 1), (2, 3)), ((0, 1), (2, 3)), ((0,), (1,), (2,), (3,)))
 
 
 def tile_mix_kern_resid_poly2_bias_kernel(
@@ -61,37 +65,65 @@ def tile_mix_kern_resid_poly2_bias_kernel(
             return banks_given[first:]
 
         w4_plane_in = one_tile("w4_plane_in", [P, J], U8)
-        r8_plane_in = one_tile("r8_plane_in", [P, PASS], U8)
+        r8_plane_in = one_tile("r8_plane_in", [P, J], U8)
         w4_plane = tiles("w4_plane", [[P, PASS]] * J_PASSES, U8)
-        r8_plane = one_tile("r8_plane", [P, PASS], U8)
+        r8_plane = tiles("r8_plane", [[P, PASS]] * J_PASSES, U8)
         v8_plane = one_tile("v8_plane", [P, J_PASSES * N], U8)
-        w4_in = one_tile("w4_in", [P, 2 * J], U8)
+        w4_in = tiles("w4_in", [[P, 2 * PASS * count] for a0, count in W4_LOADS], U8)
         w4_sorted = tiles("w4_sorted", [[P, 2 * PASS]] * J_PASSES, U8)
-        r8_in = one_tile("r8_in", [P, J], I32)
-        r8_sorted = tiles("r8_sorted", [[P, PASS]] * J_PASSES, I32)
+        r8_in = tiles("r8_in", [[P, PASS * count] for a0, count in R8_LOADS], U32)
+        r8_sorted = tiles("r8_sorted", [[P, PASS]] * J_PASSES, U32)
         v8_sb = one_tile("v8_sb", [P, J_PASSES * N], I32)
         cw_sb = one_tile("cw_sb", [P, J_PASSES, BLOCK_WORDS], F32)
         cb_sb = one_tile("cb_sb", [P, J_PASSES, BLOCK_WORDS], F32)
         b_sb = one_tile("b_sb", [P, N // P], F32)
-        x_in = tiles("x_in", [[P, SLOTS, CHUNK]] * CHUNKS, F32)
+        x_in = tiles("x_in", [[P, SLOTS, CHUNK * count] for c0, count in X_LOADS], F32)
         x_bf = one_tile("x_bf", [P, SLOTS * T], BF16)
         x_codes = one_tile("x_codes", [P, T], U32)
         x_plane = one_tile("x_plane", [P, T], U8)
-        squares = tiles("squares", [[P, SLOTS, CHUNK]] * D_TILES, F32)
-        h_bf = one_tile("h_bf", [P, SLOTS * CHUNK * D_TILES], BF16)
-        h_codes = one_tile("h_codes", [P, CHUNK * D_TILES], U32)
-        h_plane = one_tile("h_plane", [P, CHUNK * D_TILES], U8)
+        squares = tiles("squares", [[P, SLOTS, CHUNK * count] for c0, a, count in TILES], F32)
+        h_bf = one_tile("h_bf", [P, SLOTS * T * J_PASSES], BF16)
+        h_codes = one_tile("h_codes", [P, T * J_PASSES], U32)
+        h_plane = one_tile("h_plane", [P, T * J_PASSES], U8)
         y_sb = [
             tiles("y_sb%d_" % r, [[P, len(groups), width] for groups in Y_BANK_GROUPS[r]], F32)
             for r, (t0, width) in enumerate(Y_RANGES)
         ]
         banks_given, d_sums, y_banks = [], {}, {}
 
-        def chunk_columns(c, per_column=1):
-            return slice(per_column * CHUNK * c, per_column * CHUNK * (c + 1))
+        def load_x(n):
+            c0, count = X_LOADS[n]
+            nc.sync.dma_start(
+                out=x_in[n][:], in_=x[:, CHUNK * c0 : CHUNK * (c0 + count)].rearrange("(p i) t -> p i t", i=SLOTS)
+            )
 
-        def load_x(c):
-            nc.sync.dma_start(out=x_in[c][:], in_=x[:, chunk_columns(c)].rearrange("(p i) t -> p i t", i=SLOTS))
+        def load_w4(n):
+            a0, count = W4_LOADS[n]
+            nc.sync.dma_start(
+                out=w4_in[n][:].bitcast(I32), in_=w4_words[0][:, 2 * PASS * a0 : 2 * PASS * (a0 + count)].bitcast(I32)
+            )
+
+        def w4_words_in(a):
+            n = max(m for m, (a0, count) in enumerate(W4_LOADS) if a0 <= a)
+            first = 2 * PASS * (a - W4_LOADS[n][0])
+            return w4_in[n][:, first : first + 2 * PASS]
+
+        def load_r8(n):
+            a0, count = R8_LOADS[n]
+            nc.sync.dma_start(
+                out=r8_in[n][:].bitcast(I32),
+                in_=r8_words[0].rearrange("p j i -> p (j i)").bitcast(I32)[:, PASS * a0 : PASS * (a0 + count)],
+            )
+
+        def r8_words_in(a):
+            n = max(m for m, (a0, count) in enumerate(R8_LOADS) if a0 <= a)
+            first = PASS * (a - R8_LOADS[n][0])
+            return r8_in[n][:, first : first + PASS]
+
+        def x_chunks(c, count):
+            n = max(m for m, (c0, chunks) in enumerate(X_LOADS) if c0 <= c)
+            first = CHUNK * (c - X_LOADS[n][0])
+            return x_in[n][:, :, first : first + CHUNK * count]
 
         def load_plane(dst, scales):
             for quadrant in range(QUADRANTS):
@@ -101,29 +133,21 @@ def tile_mix_kern_resid_poly2_bias_kernel(
                     in_=scales[:, 4 * quadrant : 4 * quadrant + 4, :].bitcast(I32).rearrange("a r n -> r a n"),
                 )
 
-        def load_packed_plane(dst, scales):
-            for quadrant in range(QUADRANTS):
-                row = 32 * quadrant
-                nc.sync.dma_start(
-                    out=dst[row : row + 4 * J_PASSES, :].bitcast(I32),
-                    in_=scales[0, 4 * quadrant : 4 * quadrant + 4, :].bitcast(I32).rearrange("r (a n) -> a r n", a=J_PASSES),
-                )
-
         def load_by_slot(dst, vec):
             nc.sync.dma_start(
                 out=dst[:, :, :SLOTS], in_=vec.rearrange("(a p i) -> p a i", p=P, i=SLOTS)
             )
 
-        def sort_w4(a):
-            nc.vector.tensor_copy(
-                out=w4_sorted[a][:].bitcast(U16).rearrange("p (i m) -> p i m", i=SLOTS),
-                in_=w4_in[:, 2 * PASS * a : 2 * PASS * (a + 1)].bitcast(U16).rearrange("p (m i) -> p i m", i=SLOTS),
+        def sort_w4(a, copy):
+            copy(
+                out=w4_sorted[a][:].bitcast(U16).rearrange("p (i m e) -> p m i e", i=SLOTS, e=8),
+                in_=w4_words_in(a).bitcast(U16).rearrange("p (m e i) -> p m i e", i=SLOTS, e=8),
             )
 
-        def sort_r8(a):
-            nc.vector.tensor_copy(
+        def sort_r8(a, copy):
+            copy(
                 out=r8_sorted[a][:].rearrange("p (i m e) -> p m i e", i=SLOTS, e=4),
-                in_=r8_in[:, PASS * a : PASS * (a + 1)].rearrange("p (m e i) -> p m i e", i=SLOTS, e=4),
+                in_=r8_words_in(a).rearrange("p (m e i) -> p m i e", i=SLOTS, e=4),
             )
 
         def sort_plane(dst, src, slots=slice(0, SLOTS)):
@@ -138,49 +162,52 @@ def tile_mix_kern_resid_poly2_bias_kernel(
         def by_slot(src):
             return src.rearrange("p i (m e) -> p m i e", e=RUN)
 
-        def round_x_on_scalar(c):
+        def columns(c, count, per_column=1):
+            return slice(per_column * CHUNK * c, per_column * CHUNK * (c + count))
+
+        def round_x_on_scalar(c, count=1):
             nc.scalar.activation(
-                out=interleaved(x_bf[:, chunk_columns(c, SLOTS)]), in_=by_slot(x_in[c][:]), func=ACT.Copy
+                out=interleaved(x_bf[:, columns(c, count, SLOTS)]), in_=by_slot(x_chunks(c, count)), func=ACT.Copy
             )
 
-        def round_x_on_vector(c):
-            nc.vector.tensor_copy(out=interleaved(x_bf[:, chunk_columns(c, SLOTS)]), in_=by_slot(x_in[c][:]))
+        def round_x_on_vector(c, count=1):
+            nc.vector.tensor_copy(out=interleaved(x_bf[:, columns(c, count, SLOTS)]), in_=by_slot(x_chunks(c, count)))
 
-        def quantize_x(c):
+        def quantize_x(c, count=1):
             nc.vector.quantize_mx(
-                out=x_codes[:, chunk_columns(c)].bitcast(FP8X4),
-                scales=x_plane[:, chunk_columns(c)],
-                in_=x_bf[:, chunk_columns(c, SLOTS)],
+                out=x_codes[:, columns(c, count)].bitcast(FP8X4),
+                scales=x_plane[:, columns(c, count)],
+                in_=x_bf[:, columns(c, count, SLOTS)],
             )
 
         def place_d(u):
             banks = next_banks("d%d" % u, D_BANKS[u])
             per_bank = SLOTS // len(banks)
             for i in range(SLOTS):
-                d_sums[u, i] = banks[i // per_bank][:, chunk_columns(i % per_bank)]
+                d_sums[u, i] = banks[i // per_bank][:, columns(TILES[u][2] * (i % per_bank), TILES[u][2])]
             return per_bank
 
         def d_pass(u, i, words, plane, start, stop):
-            c = u // J_PASSES
+            c, a, count = TILES[u]
             nc.tensor.matmul_mx(
                 out=d_sums[u, i],
                 lhsT=words,
                 lhsT_scale=plane[:, P * i : P * (i + 1)],
-                rhs=x_codes[:, chunk_columns(c)].bitcast(FP8X4),
-                rhs_scale=x_plane[:, chunk_columns(c)],
+                rhs=x_codes[:, columns(c, count)].bitcast(FP8X4),
+                rhs_scale=x_plane[:, columns(c, count)],
                 start=start,
                 stop=stop,
             )
 
         def w4_pass(u, i, per_bank):
-            a = u % J_PASSES
+            a = TILES[u][1]
             words = w4_sorted[a][:, 2 * P * i : 2 * P * (i + 1)].bitcast(FP4X4)
             d_pass(u, i, words, w4_plane[a], i % per_bank == 0, False)
 
         def r8_pass(u, i, per_bank):
-            a = u % J_PASSES
+            a = TILES[u][1]
             words = r8_sorted[a][:, P * i : P * (i + 1)].bitcast(FP8X4)
-            d_pass(u, i, words, r8_plane[4 * a :, :], False, i % per_bank == per_bank - 1)
+            d_pass(u, i, words, r8_plane[a], False, i % per_bank == per_bank - 1)
 
         def first_product(u):
             per_bank = place_d(u)
@@ -191,47 +218,47 @@ def tile_mix_kern_resid_poly2_bias_kernel(
         def square(u):
             for i in range(SLOTS):
                 nc.scalar.activation(
-                    out=squares[u][:, i, :], in_=d_sums[u, i], func=ACT.Square, bias=cb_sb[:, u % J_PASSES, i : i + 1]
+                    out=squares[u][:, i, :], in_=d_sums[u, i], func=ACT.Square, bias=cb_sb[:, TILES[u][1], i : i + 1]
                 )
 
-        def weigh(u):
-            c, a = divmod(u, J_PASSES)
+        def weigh(u, first=0, count=None, engine=nc.vector):
+            a = TILES[u][1]
+            count = count or TILES[u][2]
             weights = cw_sb[:, a, :SLOTS].unsqueeze(1).unsqueeze(3)
-            nc.vector.tensor_tensor(
-                out=interleaved(h_bf[:, chunk_columns(u, SLOTS)]),
-                in0=by_slot(squares[u][:]),
-                in1=weights.to_broadcast([P, CHUNK // RUN, SLOTS, RUN]),
+            engine.tensor_tensor(
+                out=interleaved(h_bf[:, columns(H_FIRST[u] + first, count, SLOTS)]),
+                in0=by_slot(squares[u][:, :, columns(first, count)]),
+                in1=weights.to_broadcast([P, count * CHUNK // RUN, SLOTS, RUN]),
                 op=ALU.mult,
             )
 
-        def quantize_h(u, count):
-            cols = slice(CHUNK * u, CHUNK * (u + count))
+        def quantize_h(first, count):
             nc.vector.quantize_mx(
-                out=h_codes[:, cols].bitcast(FP8X4),
-                scales=h_plane[:, cols],
-                in_=h_bf[:, SLOTS * CHUNK * u : SLOTS * CHUNK * (u + count)],
+                out=h_codes[:, columns(first, count)].bitcast(FP8X4),
+                scales=h_plane[:, columns(first, count)],
+                in_=h_bf[:, columns(first, count, SLOTS)],
             )
 
         def y_passes(tiles_of_h):
-            r = max(n for n, (t0, width) in enumerate(Y_RANGES) if t0 <= CHUNK * (tiles_of_h[0] // J_PASSES))
+            r = max(n for n, (t0, width) in enumerate(Y_RANGES) if t0 <= CHUNK * TILES[tiles_of_h[0]][0])
             t0, width = Y_RANGES[r]
             if r not in y_banks:
                 y_banks[r] = next_banks("y%d" % r, len(Y_BANK_GROUPS[r]))
-            first_tile, last_tile = J_PASSES * t0 // CHUNK, J_PASSES * (t0 + width) // CHUNK - 1
+            members = [u for u in range(D_TILES) if t0 <= CHUNK * TILES[u][0] < t0 + width]
             for m, groups in enumerate(Y_BANK_GROUPS[r]):
                 for u in tiles_of_h:
-                    c, a = divmod(u, J_PASSES)
+                    c, a, count = TILES[u]
                     for s, n in enumerate(groups):
                         first = N * a + P * n
                         column = width * s + CHUNK * c - t0
                         nc.tensor.matmul_mx(
-                            out=y_banks[r][m][:, column : column + CHUNK],
+                            out=y_banks[r][m][:, column : column + CHUNK * count],
                             lhsT=v8_sb[:, first : first + P].bitcast(FP8X4),
                             lhsT_scale=v8_plane[:, first : first + P],
-                            rhs=h_codes[:, chunk_columns(u)].bitcast(FP8X4),
-                            rhs_scale=h_plane[:, chunk_columns(u)],
-                            start=(u == first_tile and s == 0),
-                            stop=(u == last_tile and s == len(groups) - 1),
+                            rhs=h_codes[:, columns(H_FIRST[u], count)].bitcast(FP8X4),
+                            rhs_scale=h_plane[:, columns(H_FIRST[u], count)],
+                            start=(u == members[0] and s == 0),
+                            stop=(u == members[-1] and s == len(groups) - 1),
                         )
 
         def store(queue, r, m, s0, count):
@@ -252,6 +279,17 @@ def tile_mix_kern_resid_poly2_bias_kernel(
                 bias=b_sb[:, n : n + 1],
             )
 
+        def add_bias_on_vector(r, m, s):
+            width = Y_RANGES[r][1]
+            n = Y_BANK_GROUPS[r][m][s]
+            nc.vector.tensor_scalar(
+                out=y_sb[r][m][:, s, :],
+                in0=y_banks[r][m][:, width * s : width * (s + 1)],
+                scalar1=b_sb[:, n : n + 1],
+                scalar2=None,
+                op0=ALU.add,
+            )
+
         def finish_on_vector(r, m):
             width, groups = Y_RANGES[r][1], Y_BANK_GROUPS[r][m]
             nc.vector.tensor_tensor(
@@ -262,19 +300,18 @@ def tile_mix_kern_resid_poly2_bias_kernel(
             )
             store(nc.sync, r, m, 0, len(groups))
 
-        nc.vector.memset(w4_plane_in[:].bitcast(I32), 0)
-        nc.gpsimd.memset(r8_plane_in[:].bitcast(I32), 0)
+        nc.gpsimd.memset(w4_plane_in[:].bitcast(I32), 0)
+        nc.vector.memset(r8_plane_in[:].bitcast(I32), 0)
         nc.gpsimd.memset(v8_plane[:].bitcast(I32), 0)
-
         load_x(0)
-        nc.sync.dma_start(out=w4_in[:].bitcast(I32), in_=w4_words[0].bitcast(I32))
+        load_w4(0)
         load_plane(w4_plane_in, w4_scales)
-        nc.sync.dma_start(out=r8_in[:], in_=r8_words[0].rearrange("p j i -> p (j i)").bitcast(I32))
+        load_r8(0)
         load_x(1)
-        load_packed_plane(r8_plane_in, r8_scales)
+        load_plane(r8_plane_in, r8_scales)
         load_by_slot(cb_sb, cb)
+        load_r8(1)
         load_x(2)
-        load_x(3)
         load_by_slot(cw_sb, cw)
         nc.sync.dma_start(
             out=v8_sb[:].rearrange("p (a n) -> p a n", a=J_PASSES),
@@ -285,47 +322,49 @@ def tile_mix_kern_resid_poly2_bias_kernel(
             nc.sync.dma_start(out=b_sb[:], in_=b.rearrange("(n p) -> p n", p=P))
 
         round_x_on_scalar(0)
+        sort_w4(0, nc.vector.tensor_copy)
+        sort_plane(w4_plane[0][:], w4_plane_in[:, :PASS])
+        quantize_x(0)
+        sort_w4(1, nc.vector.tensor_copy)
+        sort_plane(w4_plane[1][:], w4_plane_in[:, PASS:])
+        sort_r8(0, nc.scalar.copy)
+        slots_in_bank = {u: place_d(u) for u in range(3)}
+        for u in (0, 2):
+            for i in range(SLOTS):
+                w4_pass(u, i, slots_in_bank[u])
         round_x_on_scalar(1)
-        slots_in_bank = {}
-        for a in range(J_PASSES):
-            sort_w4(a)
-            sort_plane(w4_plane[a][:], w4_plane_in[:, PASS * a : PASS * (a + 1)])
-            if a == 0:
-                quantize_x(0)
-            slots_in_bank[a] = place_d(a)
-            for i in range(SLOTS):
-                w4_pass(a, i, slots_in_bank[a])
-        for a in range(J_PASSES):
-            sort_r8(a)
-        sort_plane(r8_plane[:], r8_plane_in[:], slice(0, SLOTS // 2))
-        sort_plane(r8_plane[:], r8_plane_in[:], slice(SLOTS // 2, SLOTS))
-        for a in range(J_PASSES):
-            for i in range(SLOTS):
-                r8_pass(a, i, slots_in_bank[a])
-        quantize_x(1)
-        first_product(2)
+        sort_plane(r8_plane[0][:], r8_plane_in[:, :PASS], slice(0, SLOTS // 2))
+        sort_plane(r8_plane[0][:], r8_plane_in[:, :PASS], slice(SLOTS // 2, SLOTS))
         round_x_on_vector(2)
+        quantize_x(1)
+        for i in range(SLOTS):
+            r8_pass(0, i, slots_in_bank[0])
+        for i in range(SLOTS):
+            w4_pass(1, i, slots_in_bank[1])
+            r8_pass(1, i, slots_in_bank[1])
+        sort_plane(r8_plane[1][:], r8_plane_in[:, PASS:])
+        sort_r8(1, nc.vector.tensor_copy)
         quantize_x(2)
+        for i in range(SLOTS):
+            r8_pass(2, i, slots_in_bank[2])
         round_x_on_vector(3)
-
         for u in range(D_TILES):
             square(u)
-            if u + LEAD < D_TILES:
-                first_product(u + LEAD)
             weigh(u)
             if u == 0:
-                quantize_x(CHUNKS - 1)
-            elif u % 2 == 0:
+                quantize_x(3)
+            if u + LEAD < D_TILES:
+                first_product(u + LEAD)
+            if u in (2, 4):
                 quantize_h(u - 2, 2)
             if u == 4:
                 y_passes((0, 1))
                 y_passes((2, 3))
-            if u == 6:
-                y_passes((4, 5))
-        for u in range(D_TILES - 2, D_TILES):
-            quantize_h(u, 1)
-            y_passes((u,))
-
+            if u > 4:
+                quantize_h(u - 1, 1)
+                y_passes((u - 1,))
+        quantize_h(D_TILES - 1, 1)
+        y_passes((D_TILES - 1,))
         for m in range(2):
             for s in range(2):
                 add_bias_on_scalar(0, m, s)
@@ -334,7 +373,9 @@ def tile_mix_kern_resid_poly2_bias_kernel(
             add_bias_on_scalar(1, 0, s)
         store(nc.sync, 1, 0, 0, 2)
         finish_on_vector(1, 1)
-        for m, queue in enumerate((nc.sync, nc.sync)):
-            add_bias_on_scalar(2, m, 0)
-            store(queue, 2, m, 0, 1)
-        finish_on_vector(2, 2)
+        for m in range(4):
+            if m % 2:
+                finish_on_vector(2, m)
+            else:
+                add_bias_on_scalar(2, m, 0)
+                store(nc.sync, 2, m, 0, 1)

@@ -30,14 +30,14 @@ D_TILES = len(TILES)
 H_FIRST = [sum(tile[2] for tile in TILES[:u]) for u in range(D_TILES + 1)]
 W4_LOADS = ((0, 2),)
 R8_LOADS = ((0, 1), (1, 1))
-X_LOADS = ((0, 1), (1, 2), (3, 1))
-D_BANKS = (4, 2, 2, 2, 1, 1, 1, 1)
+X_LOADS = ((0, 1), (1, 1), (2, 1), (3, 1))
+D_BANKS = (4, 2, 2, 2, 2, 1, 1, 1)
 LEAD = 3
 RUN = 2
 
 Y_RANGES = ((0, 2 * CHUNK), (2 * CHUNK, CHUNK), (3 * CHUNK, CHUNK))
 BLOCK_WORDS = 8
-Y_BANK_GROUPS = (((0, 1), (2, 3)), ((0, 1), (2, 3)), ((0,), (1,), (2,), (3,)))
+Y_BANK_GROUPS = (((0,), (1,), (2,), (3,)), ((0, 1), (2, 3)), ((0,), (1,), (2, 3)))
 
 
 def tile_mix_kern_resid_poly2_bias_kernel(
@@ -138,10 +138,10 @@ def tile_mix_kern_resid_poly2_bias_kernel(
                 out=dst[:, :, :SLOTS], in_=vec.rearrange("(a p i) -> p a i", p=P, i=SLOTS)
             )
 
-        def sort_w4(a, copy):
+        def sort_w4(a, copy, slots=slice(0, SLOTS)):
             copy(
-                out=w4_sorted[a][:].bitcast(U16).rearrange("p (i m e) -> p m i e", i=SLOTS, e=8),
-                in_=w4_words_in(a).bitcast(U16).rearrange("p (m e i) -> p m i e", i=SLOTS, e=8),
+                out=w4_sorted[a][:].bitcast(U16).rearrange("p (i m e) -> p m i e", i=SLOTS, e=8)[:, :, slots, :],
+                in_=w4_words_in(a).bitcast(U16).rearrange("p (m e i) -> p m i e", i=SLOTS, e=8)[:, :, slots, :],
             )
 
         def sort_r8(a, copy):
@@ -165,13 +165,18 @@ def tile_mix_kern_resid_poly2_bias_kernel(
         def columns(c, count, per_column=1):
             return slice(per_column * CHUNK * c, per_column * CHUNK * (c + count))
 
-        def round_x_on_scalar(c, count=1):
-            nc.scalar.activation(
-                out=interleaved(x_bf[:, columns(c, count, SLOTS)]), in_=by_slot(x_chunks(c, count)), func=ACT.Copy
+        def round_x(copy, c, first=0, width=CHUNK):
+            column = CHUNK * c + first
+            copy(
+                out=interleaved(x_bf[:, SLOTS * column : SLOTS * (column + width)]),
+                in_=by_slot(x_chunks(c, 1)[:, :, first : first + width]),
             )
 
-        def round_x_on_vector(c, count=1):
-            nc.vector.tensor_copy(out=interleaved(x_bf[:, columns(c, count, SLOTS)]), in_=by_slot(x_chunks(c, count)))
+        def round_x_on_scalar(c, first=0, width=CHUNK):
+            round_x(lambda out, in_: nc.scalar.activation(out=out, in_=in_, func=ACT.Copy), c, first, width)
+
+        def round_x_on_vector(c, first=0, width=CHUNK):
+            round_x(nc.vector.tensor_copy, c, first, width)
 
         def quantize_x(c, count=1):
             nc.vector.quantize_mx(
@@ -187,10 +192,11 @@ def tile_mix_kern_resid_poly2_bias_kernel(
                 d_sums[u, i] = banks[i // per_bank][:, columns(TILES[u][2] * (i % per_bank), TILES[u][2])]
             return per_bank
 
-        def d_pass(u, i, words, plane, start, stop):
-            c, a, count = TILES[u]
+        def d_pass(u, i, words, plane, start, stop, first=0, count=None):
+            c = TILES[u][0] + first
+            count = count or TILES[u][2]
             nc.tensor.matmul_mx(
-                out=d_sums[u, i],
+                out=d_sums[u, i][:, columns(first, count)],
                 lhsT=words,
                 lhsT_scale=plane[:, P * i : P * (i + 1)],
                 rhs=x_codes[:, columns(c, count)].bitcast(FP8X4),
@@ -199,10 +205,10 @@ def tile_mix_kern_resid_poly2_bias_kernel(
                 stop=stop,
             )
 
-        def w4_pass(u, i, per_bank):
+        def w4_pass(u, i, per_bank, first=0, count=None):
             a = TILES[u][1]
             words = w4_sorted[a][:, 2 * P * i : 2 * P * (i + 1)].bitcast(FP4X4)
-            d_pass(u, i, words, w4_plane[a], i % per_bank == 0, False)
+            d_pass(u, i, words, w4_plane[a], i % per_bank == 0 and first == 0, False, first, count)
 
         def r8_pass(u, i, per_bank):
             a = TILES[u][1]
@@ -239,27 +245,28 @@ def tile_mix_kern_resid_poly2_bias_kernel(
                 in_=h_bf[:, columns(first, count, SLOTS)],
             )
 
-        def y_passes(tiles_of_h):
-            r = max(n for n, (t0, width) in enumerate(Y_RANGES) if t0 <= CHUNK * TILES[tiles_of_h[0]][0])
+        def y_passes(r, m, passes):
             t0, width = Y_RANGES[r]
             if r not in y_banks:
                 y_banks[r] = next_banks("y%d" % r, len(Y_BANK_GROUPS[r]))
-            members = [u for u in range(D_TILES) if t0 <= CHUNK * TILES[u][0] < t0 + width]
-            for m, groups in enumerate(Y_BANK_GROUPS[r]):
-                for u in tiles_of_h:
-                    c, a, count = TILES[u]
-                    for s, n in enumerate(groups):
-                        first = N * a + P * n
-                        column = width * s + CHUNK * c - t0
-                        nc.tensor.matmul_mx(
-                            out=y_banks[r][m][:, column : column + CHUNK * count],
-                            lhsT=v8_sb[:, first : first + P].bitcast(FP8X4),
-                            lhsT_scale=v8_plane[:, first : first + P],
-                            rhs=h_codes[:, columns(H_FIRST[u], count)].bitcast(FP8X4),
-                            rhs_scale=h_plane[:, columns(H_FIRST[u], count)],
-                            start=(u == members[0] and s == 0),
-                            stop=(u == members[-1] and s == len(groups) - 1),
-                        )
+            groups = Y_BANK_GROUPS[r][m]
+            for a in passes:
+                u = [n for n, tile in enumerate(TILES) if tile[:2] == (t0 // CHUNK, a)][0]
+                for s, n in enumerate(groups):
+                    first = N * a + P * n
+                    nc.tensor.matmul_mx(
+                        out=y_banks[r][m][:, width * s : width * (s + 1)],
+                        lhsT=v8_sb[:, first : first + P].bitcast(FP8X4),
+                        lhsT_scale=v8_plane[:, first : first + P],
+                        rhs=h_codes[:, columns(H_FIRST[u], width // CHUNK)].bitcast(FP8X4),
+                        rhs_scale=h_plane[:, columns(H_FIRST[u], width // CHUNK)],
+                        start=(a == 0 and s == 0),
+                        stop=(a == J_PASSES - 1 and s == len(groups) - 1),
+                    )
+
+        def y_pass(r, a):
+            for m in range(len(Y_BANK_GROUPS[r])):
+                y_passes(r, m, (a,))
 
         def store(queue, r, m, s0, count):
             t0, width = Y_RANGES[r]
@@ -301,18 +308,19 @@ def tile_mix_kern_resid_poly2_bias_kernel(
             store(nc.sync, r, m, 0, len(groups))
 
         nc.gpsimd.memset(w4_plane_in[:].bitcast(I32), 0)
-        nc.vector.memset(r8_plane_in[:].bitcast(I32), 0)
+        nc.gpsimd.memset(r8_plane_in[:].bitcast(I32), 0)
         nc.gpsimd.memset(v8_plane[:].bitcast(I32), 0)
         load_x(0)
-        load_w4(0)
         load_plane(w4_plane_in, w4_scales)
+        load_w4(0)
         load_r8(0)
         load_x(1)
         load_plane(r8_plane_in, r8_scales)
-        load_by_slot(cb_sb, cb)
         load_r8(1)
+        load_by_slot(cb_sb, cb)
         load_x(2)
         load_by_slot(cw_sb, cw)
+        load_x(3)
         nc.sync.dma_start(
             out=v8_sb[:].rearrange("p (a n) -> p a n", a=J_PASSES),
             in_=v8_words.rearrange("a p n i -> p a (n i)").bitcast(I32),
@@ -321,21 +329,24 @@ def tile_mix_kern_resid_poly2_bias_kernel(
         with nc.allow_non_contiguous_dma(reason="one bias value for each partition"):
             nc.sync.dma_start(out=b_sb[:], in_=b.rearrange("(n p) -> p n", p=P))
 
-        round_x_on_scalar(0)
-        sort_w4(0, nc.vector.tensor_copy)
+        round_x_on_scalar(0, 0, 48)
+        round_x_on_vector(0, 48, 80)
         sort_plane(w4_plane[0][:], w4_plane_in[:, :PASS])
         quantize_x(0)
-        sort_w4(1, nc.vector.tensor_copy)
+        sort_w4(0, nc.vector.tensor_copy, slice(0, 2))
+        sort_w4(0, nc.vector.tensor_copy, slice(2, 4))
+        sort_w4(1, nc.scalar.copy)
         sort_plane(w4_plane[1][:], w4_plane_in[:, PASS:])
         sort_r8(0, nc.scalar.copy)
         slots_in_bank = {u: place_d(u) for u in range(3)}
         for u in (0, 2):
             for i in range(SLOTS):
                 w4_pass(u, i, slots_in_bank[u])
-        round_x_on_scalar(1)
+        round_x_on_scalar(1, 0, 64)
+        round_x_on_vector(1, 64, 64)
         sort_plane(r8_plane[0][:], r8_plane_in[:, :PASS], slice(0, SLOTS // 2))
         sort_plane(r8_plane[0][:], r8_plane_in[:, :PASS], slice(SLOTS // 2, SLOTS))
-        round_x_on_vector(2)
+
         quantize_x(1)
         for i in range(SLOTS):
             r8_pass(0, i, slots_in_bank[0])
@@ -344,38 +355,38 @@ def tile_mix_kern_resid_poly2_bias_kernel(
             r8_pass(1, i, slots_in_bank[1])
         sort_plane(r8_plane[1][:], r8_plane_in[:, PASS:])
         sort_r8(1, nc.vector.tensor_copy)
-        quantize_x(2)
         for i in range(SLOTS):
             r8_pass(2, i, slots_in_bank[2])
-        round_x_on_vector(3)
+
+        round_x_on_vector(2)
         for u in range(D_TILES):
             square(u)
             weigh(u)
             if u == 0:
+                quantize_x(2)
+                round_x_on_vector(3)
+            if u == 1:
                 quantize_x(3)
             if u + LEAD < D_TILES:
                 first_product(u + LEAD)
             if u in (2, 4):
                 quantize_h(u - 2, 2)
             if u == 4:
-                y_passes((0, 1))
-                y_passes((2, 3))
+                y_pass(0, 0)
+                y_pass(0, 1)
             if u > 4:
                 quantize_h(u - 1, 1)
-                y_passes((u - 1,))
+                y_pass(1 + (u - 5) // 2, (u - 5) % 2)
         quantize_h(D_TILES - 1, 1)
-        y_passes((D_TILES - 1,))
-        for m in range(2):
-            for s in range(2):
-                add_bias_on_scalar(0, m, s)
-                store(nc.sync, 0, m, s, 1)
+        y_pass(2, 1)
+        for m in range(4):
+            add_bias_on_scalar(0, m, 0)
+            store(nc.sync, 0, m, 0, 1)
         for s in range(2):
             add_bias_on_scalar(1, 0, s)
         store(nc.sync, 1, 0, 0, 2)
         finish_on_vector(1, 1)
-        for m in range(4):
-            if m % 2:
-                finish_on_vector(2, m)
-            else:
-                add_bias_on_scalar(2, m, 0)
-                store(nc.sync, 2, m, 0, 1)
+        for m in range(2):
+            add_bias_on_scalar(2, m, 0)
+            store(nc.sync, 2, m, 0, 1)
+        finish_on_vector(2, 2)

@@ -31,13 +31,13 @@ H_FIRST = [sum(tile[2] for tile in TILES[:u]) for u in range(D_TILES + 1)]
 W4_LOADS = ((0, 2),)
 R8_LOADS = ((0, 1), (1, 1))
 X_LOADS = ((0, 1), (1, 1), (2, 1), (3, 1))
-D_BANKS = (4, 2, 2, 2, 2, 1, 1, 1)
+D_BANKS = (2, 2, 2, 2, 1, 1, 1, 1)
 LEAD = 3
 RUN = 2
 
 Y_RANGES = ((0, 2 * CHUNK), (2 * CHUNK, CHUNK), (3 * CHUNK, CHUNK))
 BLOCK_WORDS = 8
-Y_BANK_GROUPS = (((0,), (1,), (2,), (3,)), ((0, 1), (2, 3)), ((0,), (1,), (2, 3)))
+Y_BANK_GROUPS = (((0,), (1,), (2,), (3,)), ((0,), (1,), (2, 3)), ((0,), (1,), (2, 3)))
 
 
 def tile_mix_kern_resid_poly2_bias_kernel(
@@ -85,10 +85,7 @@ def tile_mix_kern_resid_poly2_bias_kernel(
         h_bf = one_tile("h_bf", [P, SLOTS * T * J_PASSES], BF16)
         h_codes = one_tile("h_codes", [P, T * J_PASSES], U32)
         h_plane = one_tile("h_plane", [P, T * J_PASSES], U8)
-        y_sb = [
-            tiles("y_sb%d_" % r, [[P, len(groups), width] for groups in Y_BANK_GROUPS[r]], F32)
-            for r, (t0, width) in enumerate(Y_RANGES)
-        ]
+        y_sb = tiles("y_sb", [[P, N // P, width] for t0, width in Y_RANGES], F32)
         banks_given, d_sums, y_banks = [], {}, {}
 
         def load_x(n):
@@ -144,10 +141,10 @@ def tile_mix_kern_resid_poly2_bias_kernel(
                 in_=w4_words_in(a).bitcast(U16).rearrange("p (m e i) -> p m i e", i=SLOTS, e=8)[:, :, slots, :],
             )
 
-        def sort_r8(a, copy):
+        def sort_r8(a, copy, slots=slice(0, SLOTS)):
             copy(
-                out=r8_sorted[a][:].rearrange("p (i m e) -> p m i e", i=SLOTS, e=4),
-                in_=r8_words_in(a).rearrange("p (m e i) -> p m i e", i=SLOTS, e=4),
+                out=r8_sorted[a][:].rearrange("p (i m e) -> p m i e", i=SLOTS, e=4)[:, :, slots, :],
+                in_=r8_words_in(a).rearrange("p (m e i) -> p m i e", i=SLOTS, e=4)[:, :, slots, :],
             )
 
         def sort_plane(dst, src, slots=slice(0, SLOTS)):
@@ -268,44 +265,27 @@ def tile_mix_kern_resid_poly2_bias_kernel(
             for m in range(len(Y_BANK_GROUPS[r])):
                 y_passes(r, m, (a,))
 
-        def store(queue, r, m, s0, count):
+        def store(r, n0, count):
             t0, width = Y_RANGES[r]
-            n0 = Y_BANK_GROUPS[r][m][s0]
-            queue.dma_start(
+            nc.sync.dma_start(
                 out=out.rearrange("(n p) t -> p n t", p=P)[:, n0 : n0 + count, t0 : t0 + width],
-                in_=y_sb[r][m][:, s0 : s0 + count, :],
+                in_=y_sb[r][:, n0 : n0 + count, :],
             )
 
-        def add_bias_on_scalar(r, m, s):
-            width = Y_RANGES[r][1]
-            n = Y_BANK_GROUPS[r][m][s]
+        def add_bias_on_scalar(r, m):
+            n = Y_BANK_GROUPS[r][m][0]
             nc.scalar.activation(
-                out=y_sb[r][m][:, s, :],
-                in_=y_banks[r][m][:, width * s : width * (s + 1)],
-                func=ACT.Identity,
-                bias=b_sb[:, n : n + 1],
+                out=y_sb[r][:, n, :], in_=y_banks[r][m][:, : Y_RANGES[r][1]], func=ACT.Identity, bias=b_sb[:, n : n + 1]
             )
 
-        def add_bias_on_vector(r, m, s):
-            width = Y_RANGES[r][1]
-            n = Y_BANK_GROUPS[r][m][s]
-            nc.vector.tensor_scalar(
-                out=y_sb[r][m][:, s, :],
-                in0=y_banks[r][m][:, width * s : width * (s + 1)],
-                scalar1=b_sb[:, n : n + 1],
-                scalar2=None,
-                op0=ALU.add,
-            )
-
-        def finish_on_vector(r, m):
+        def add_bias_on_vector(r, m):
             width, groups = Y_RANGES[r][1], Y_BANK_GROUPS[r][m]
             nc.vector.tensor_tensor(
-                out=y_sb[r][m][:],
+                out=y_sb[r][:, groups[0] : groups[-1] + 1, :],
                 in0=y_banks[r][m][:, : len(groups) * width].rearrange("p (s t) -> p s t", s=len(groups)),
                 in1=b_sb[:, groups[0] : groups[-1] + 1].unsqueeze(2).to_broadcast([P, len(groups), width]),
                 op=ALU.add,
             )
-            store(nc.sync, r, m, 0, len(groups))
 
         nc.gpsimd.memset(w4_plane_in[:].bitcast(I32), 0)
         nc.gpsimd.memset(r8_plane_in[:].bitcast(I32), 0)
@@ -316,9 +296,9 @@ def tile_mix_kern_resid_poly2_bias_kernel(
         load_r8(0)
         load_x(1)
         load_plane(r8_plane_in, r8_scales)
-        load_r8(1)
-        load_by_slot(cb_sb, cb)
         load_x(2)
+        load_by_slot(cb_sb, cb)
+        load_r8(1)
         load_by_slot(cw_sb, cw)
         load_x(3)
         nc.sync.dma_start(
@@ -338,7 +318,7 @@ def tile_mix_kern_resid_poly2_bias_kernel(
         sort_w4(1, nc.scalar.copy)
         sort_plane(w4_plane[1][:], w4_plane_in[:, PASS:])
         sort_r8(0, nc.scalar.copy)
-        slots_in_bank = {u: place_d(u) for u in range(3)}
+        slots_in_bank = {u: place_d(u) for u in range(4)}
         for u in (0, 2):
             for i in range(SLOTS):
                 w4_pass(u, i, slots_in_bank[u])
@@ -353,23 +333,28 @@ def tile_mix_kern_resid_poly2_bias_kernel(
         for i in range(SLOTS):
             w4_pass(1, i, slots_in_bank[1])
             r8_pass(1, i, slots_in_bank[1])
+        for i in range(SLOTS):
+            w4_pass(3, i, slots_in_bank[3])
         sort_plane(r8_plane[1][:], r8_plane_in[:, PASS:])
-        sort_r8(1, nc.vector.tensor_copy)
+        round_x_on_vector(2)
+        quantize_x(2)
+        sort_r8(1, nc.vector.tensor_copy, slice(0, 2))
+        sort_r8(1, nc.vector.tensor_copy, slice(2, 4))
         for i in range(SLOTS):
             r8_pass(2, i, slots_in_bank[2])
 
-        round_x_on_vector(2)
+        for i in range(SLOTS):
+            r8_pass(3, i, slots_in_bank[3])
         for u in range(D_TILES):
             square(u)
             weigh(u)
-            if u == 0:
-                quantize_x(2)
-                round_x_on_vector(3)
             if u == 1:
+                round_x_on_vector(3)
+                quantize_h(0, 2)
                 quantize_x(3)
-            if u + LEAD < D_TILES:
+            if 0 < u < D_TILES - LEAD:
                 first_product(u + LEAD)
-            if u in (2, 4):
+            if u == 4:
                 quantize_h(u - 2, 2)
             if u == 4:
                 y_pass(0, 0)
@@ -380,13 +365,15 @@ def tile_mix_kern_resid_poly2_bias_kernel(
         quantize_h(D_TILES - 1, 1)
         y_pass(2, 1)
         for m in range(4):
-            add_bias_on_scalar(0, m, 0)
-            store(nc.sync, 0, m, 0, 1)
-        for s in range(2):
-            add_bias_on_scalar(1, 0, s)
-        store(nc.sync, 1, 0, 0, 2)
-        finish_on_vector(1, 1)
+            add_bias_on_scalar(0, m)
+            store(0, m, 1)
         for m in range(2):
-            add_bias_on_scalar(2, m, 0)
-            store(nc.sync, 2, m, 0, 1)
-        finish_on_vector(2, 2)
+            add_bias_on_scalar(1, m)
+        store(1, 0, 2)
+        add_bias_on_vector(1, 2)
+        store(1, 2, 2)
+        for m in range(2):
+            add_bias_on_scalar(2, m)
+            store(2, m, 1)
+        add_bias_on_vector(2, 2)
+        store(2, 2, 2)

from contextlib import ExitStack

import concourse.mybir as mybir

K, J, N, T = 512, 1024, 512, 512
FLOPS = 2 * (2 * K * J * T + J * N * T)

F32 = mybir.dt.float32
BF16 = mybir.dt.bfloat16
I32 = mybir.dt.int32
U32 = mybir.dt.uint32
U16 = mybir.dt.uint16
U8 = mybir.dt.uint8
FP8X4 = mybir.dt.float8_e4m3fn_x4
FP4X4 = mybir.dt.float4_e2m1fn_x4
ACT = mybir.ActivationFunctionType
ALU = mybir.AluOpType

P = 128
SLOTS = 4
PASS = P * SLOTS
J_PASSES = J // PASS
QUADRANTS = 4
BANK_COLUMNS = 512
PSUM_BANKS = 8
CHUNK = 128
CHUNKS = T // CHUNK
TILES = ((0, 0, 1), (1, 0, 1), (0, 1, 1), (1, 1, 1), (2, 0, 1), (2, 1, 1), (3, 0, 1), (3, 1, 1))
D_TILES = len(TILES)
H_FIRST = [sum(tile[2] for tile in TILES[:u]) for u in range(D_TILES + 1)]
W4_LOADS = ((0, 2),)
R8_LOADS = ((0, 1), (1, 1))
X_LOADS = ((0, 1), (1, 1), (2, 1), (3, 1))
D_BANKS = (2, 2, 2, 2, 1, 1, 1, 1)
LEAD = 3
RUN = 2

Y_RANGES = ((0, 2 * CHUNK), (2 * CHUNK, CHUNK), (3 * CHUNK, CHUNK))
BLOCK_WORDS = 8
Y_BANK_GROUPS = (((0,), (1,), (2,), (3,)), ((0,), (1,), (2, 3)), ((0,), (1,), (2, 3)))


def tile_mix_kern_resid_poly2_bias_kernel(
    tc, x, w4_words, w4_scales, r8_words, r8_scales, cw, cb, v8_words, v8_scales, b, out
):
    nc = tc.nc

    with ExitStack() as ctx:
        sb = ctx.enter_context(tc.tile_pool(name="sb", bufs=1))
        ps = ctx.enter_context(tc.psum_pool(name="ps", bufs=1))
        ctx.enter_context(tc.manual_schedule())

        def one_tile(name, shape, dtype):
            return sb.tile(shape, dtype, name=name, align_bytes=64)

        def tiles(name, shapes, dtype):
            return [one_tile("%s%d" % (name, n), shape, dtype) for n, shape in enumerate(shapes)]

        def next_banks(name, count):
            first = len(banks_given)
            banks_given.extend(
                ps.tile([P, BANK_COLUMNS], F32, name="%s_%d" % (name, n), tag="bank%d" % ((first + n) % PSUM_BANKS), bufs=1)
                for n in range(count)
            )
            return banks_given[first:]

        w4_plane_in = one_tile("w4_plane_in", [P, J], U8)
        r8_plane_in = one_tile("r8_plane_in", [P, J], U8)
        w4_plane = tiles("w4_plane", [[P, PASS]] * J_PASSES, U8)
        r8_plane = tiles("r8_plane", [[P, PASS]] * J_PASSES, U8)
        v8_plane = one_tile("v8_plane", [P, J_PASSES * N], U8)
        w4_in = tiles("w4_in", [[P, 2 * PASS * count] for a0, count in W4_LOADS], U8)
        w4_sorted = tiles("w4_sorted", [[P, 2 * PASS]] * J_PASSES, U8)
        r8_in = tiles("r8_in", [[P, PASS * count] for a0, count in R8_LOADS], U32)
        r8_sorted = tiles("r8_sorted", [[P, PASS]] * J_PASSES, U32)
        v8_sb = one_tile("v8_sb", [P, J_PASSES * N], I32)
        cw_sb = one_tile("cw_sb", [P, J_PASSES, BLOCK_WORDS], F32)
        cb_sb = one_tile("cb_sb", [P, J_PASSES, BLOCK_WORDS], F32)
        b_sb = one_tile("b_sb", [P, N // P], F32)
        x_in = tiles("x_in", [[P, SLOTS, CHUNK * count] for c0, count in X_LOADS], F32)
        x_bf = one_tile("x_bf", [P, SLOTS * T], BF16)
        x_codes = one_tile("x_codes", [P, T], U32)
        x_plane = one_tile("x_plane", [P, T], U8)
        squares = tiles("squares", [[P, SLOTS, CHUNK * count] for c0, a, count in TILES], F32)
        h_bf = one_tile("h_bf", [P, SLOTS * T * J_PASSES], BF16)
        h_codes = one_tile("h_codes", [P, T * J_PASSES], U32)
        h_plane = one_tile("h_plane", [P, T * J_PASSES], U8)
        y_sb = tiles("y_sb", [[P, N // P, width] for t0, width in Y_RANGES], F32)
        banks_given, d_sums, y_banks = [], {}, {}

        def load_x(n):
            c0, count = X_LOADS[n]
            nc.sync.dma_start(
                out=x_in[n][:], in_=x[:, CHUNK * c0 : CHUNK * (c0 + count)].rearrange("(p i) t -> p i t", i=SLOTS)
            )

        def load_w4(n):
            a0, count = W4_LOADS[n]
            nc.sync.dma_start(
                out=w4_in[n][:].bitcast(I32), in_=w4_words[0][:, 2 * PASS * a0 : 2 * PASS * (a0 + count)].bitcast(I32)
            )

        def w4_words_in(a):
            n = max(m for m, (a0, count) in enumerate(W4_LOADS) if a0 <= a)
            first = 2 * PASS * (a - W4_LOADS[n][0])
            return w4_in[n][:, first : first + 2 * PASS]

        def load_r8(n):
            a0, count = R8_LOADS[n]
            nc.sync.dma_start(
                out=r8_in[n][:].bitcast(I32),
                in_=r8_words[0].rearrange("p j i -> p (j i)").bitcast(I32)[:, PASS * a0 : PASS * (a0 + count)],
            )

        def r8_words_in(a):
            n = max(m for m, (a0, count) in enumerate(R8_LOADS) if a0 <= a)
            first = PASS * (a - R8_LOADS[n][0])
            return r8_in[n][:, first : first + PASS]

        def x_chunks(c, count):
            n = max(m for m, (c0, chunks) in enumerate(X_LOADS) if c0 <= c)
            first = CHUNK * (c - X_LOADS[n][0])
            return x_in[n][:, :, first : first + CHUNK * count]

        def load_plane(dst, scales):
            for quadrant in range(QUADRANTS):
                row = 32 * quadrant
                nc.sync.dma_start(
                    out=dst[row : row + 4, :].bitcast(I32).rearrange("r (a n) -> r a n", a=scales.shape[0]),
                    in_=scales[:, 4 * quadrant : 4 * quadrant + 4, :].bitcast(I32).rearrange("a r n -> r a n"),
                )

        def load_by_slot(dst, vec):
            nc.sync.dma_start(
                out=dst[:, :, :SLOTS], in_=vec.rearrange("(a p i) -> p a i", p=P, i=SLOTS)
            )

        def sort_w4(a, copy, slots=slice(0, SLOTS)):
            copy(
                out=w4_sorted[a][:].bitcast(U16).rearrange("p (i m e) -> p m i e", i=SLOTS, e=8)[:, :, slots, :],
                in_=w4_words_in(a).bitcast(U16).rearrange("p (m e i) -> p m i e", i=SLOTS, e=8)[:, :, slots, :],
            )

        def sort_r8(a, copy, slots=slice(0, SLOTS)):
            copy(
                out=r8_sorted[a][:].rearrange("p (i m e) -> p m i e", i=SLOTS, e=4)[:, :, slots, :],
                in_=r8_words_in(a).rearrange("p (m e i) -> p m i e", i=SLOTS, e=4)[:, :, slots, :],
            )

        def sort_plane(dst, src, slots=slice(0, SLOTS)):
            nc.vector.tensor_copy(
                out=dst.rearrange("p (i m) -> p i m", i=SLOTS)[:, slots, :],
                in_=src.rearrange("p (m i) -> p i m", i=SLOTS)[:, slots, :],
            )

        def interleaved(dst):
            return dst.rearrange("p (m e i) -> p m i e", i=SLOTS, e=RUN)

        def by_slot(src):
            return src.rearrange("p i (m e) -> p m i e", e=RUN)

        def columns(c, count, per_column=1):
            return slice(per_column * CHUNK * c, per_column * CHUNK * (c + count))

        def round_x(copy, c, first=0, width=CHUNK):
            column = CHUNK * c + first
            copy(
                out=interleaved(x_bf[:, SLOTS * column : SLOTS * (column + width)]),
                in_=by_slot(x_chunks(c, 1)[:, :, first : first + width]),
            )

        def round_x_on_scalar(c, first=0, width=CHUNK):
            round_x(lambda out, in_: nc.scalar.activation(out=out, in_=in_, func=ACT.Copy), c, first, width)

        def round_x_on_vector(c, first=0, width=CHUNK):
            round_x(nc.vector.tensor_copy, c, first, width)

        def quantize_x(c, count=1):
            nc.vector.quantize_mx(
                out=x_codes[:, columns(c, count)].bitcast(FP8X4),
                scales=x_plane[:, columns(c, count)],
                in_=x_bf[:, columns(c, count, SLOTS)],
            )

        def place_d(u):
            banks = next_banks("d%d" % u, D_BANKS[u])
            per_bank = SLOTS // len(banks)
            for i in range(SLOTS):
                d_sums[u, i] = banks[i // per_bank][:, columns(TILES[u][2] * (i % per_bank), TILES[u][2])]
            return per_bank

        def d_pass(u, i, words, plane, start, stop, first=0, count=None):
            c = TILES[u][0] + first
            count = count or TILES[u][2]
            nc.tensor.matmul_mx(
                out=d_sums[u, i][:, columns(first, count)],
                lhsT=words,
                lhsT_scale=plane[:, P * i : P * (i + 1)],
                rhs=x_codes[:, columns(c, count)].bitcast(FP8X4),
                rhs_scale=x_plane[:, columns(c, count)],
                start=start,
                stop=stop,
            )

        def w4_pass(u, i, per_bank, first=0, count=None):
            a = TILES[u][1]
            words = w4_sorted[a][:, 2 * P * i : 2 * P * (i + 1)].bitcast(FP4X4)
            d_pass(u, i, words, w4_plane[a], i % per_bank == 0 and first == 0, False, first, count)

        def r8_pass(u, i, per_bank):
            a = TILES[u][1]
            words = r8_sorted[a][:, P * i : P * (i + 1)].bitcast(FP8X4)
            d_pass(u, i, words, r8_plane[a], False, i % per_bank == per_bank - 1)

        def first_product(u):
            per_bank = place_d(u)
            for i in range(SLOTS):
                w4_pass(u, i, per_bank)
                r8_pass(u, i, per_bank)

        def square(u):
            for i in range(SLOTS):
                nc.scalar.activation(
                    out=squares[u][:, i, :], in_=d_sums[u, i], func=ACT.Square, bias=cb_sb[:, TILES[u][1], i : i + 1]
                )

        def weigh(u, first=0, count=None, engine=nc.vector):
            a = TILES[u][1]
            count = count or TILES[u][2]
            weights = cw_sb[:, a, :SLOTS].unsqueeze(1).unsqueeze(3)
            engine.tensor_tensor(
                out=interleaved(h_bf[:, columns(H_FIRST[u] + first, count, SLOTS)]),
                in0=by_slot(squares[u][:, :, columns(first, count)]),
                in1=weights.to_broadcast([P, count * CHUNK // RUN, SLOTS, RUN]),
                op=ALU.mult,
            )

        def quantize_h(first, count):
            nc.vector.quantize_mx(
                out=h_codes[:, columns(first, count)].bitcast(FP8X4),
                scales=h_plane[:, columns(first, count)],
                in_=h_bf[:, columns(first, count, SLOTS)],
            )

        def y_passes(r, m, passes):
            t0, width = Y_RANGES[r]
            if r not in y_banks:
                y_banks[r] = next_banks("y%d" % r, len(Y_BANK_GROUPS[r]))
            groups = Y_BANK_GROUPS[r][m]
            for a in passes:
                u = [n for n, tile in enumerate(TILES) if tile[:2] == (t0 // CHUNK, a)][0]
                for s, n in enumerate(groups):
                    first = N * a + P * n
                    nc.tensor.matmul_mx(
                        out=y_banks[r][m][:, width * s : width * (s + 1)],
                        lhsT=v8_sb[:, first : first + P].bitcast(FP8X4),
                        lhsT_scale=v8_plane[:, first : first + P],
                        rhs=h_codes[:, columns(H_FIRST[u], width // CHUNK)].bitcast(FP8X4),
                        rhs_scale=h_plane[:, columns(H_FIRST[u], width // CHUNK)],
                        start=(a == 0 and s == 0),
                        stop=(a == J_PASSES - 1 and s == len(groups) - 1),
                    )

        def y_pass(r, a):
            for m in range(len(Y_BANK_GROUPS[r])):
                y_passes(r, m, (a,))

        def store(r, n0, count):
            t0, width = Y_RANGES[r]
            nc.sync.dma_start(
                out=out.rearrange("(n p) t -> p n t", p=P)[:, n0 : n0 + count, t0 : t0 + width],
                in_=y_sb[r][:, n0 : n0 + count, :],
            )

        def add_bias_on_scalar(r, m):
            n = Y_BANK_GROUPS[r][m][0]
            nc.scalar.activation(
                out=y_sb[r][:, n, :], in_=y_banks[r][m][:, : Y_RANGES[r][1]], func=ACT.Identity, bias=b_sb[:, n : n + 1]
            )

        def add_bias_on_vector(r, m):
            width, groups = Y_RANGES[r][1], Y_BANK_GROUPS[r][m]
            nc.vector.tensor_tensor(
                out=y_sb[r][:, groups[0] : groups[-1] + 1, :],
                in0=y_banks[r][m][:, : len(groups) * width].rearrange("p (s t) -> p s t", s=len(groups)),
                in1=b_sb[:, groups[0] : groups[-1] + 1].unsqueeze(2).to_broadcast([P, len(groups), width]),
                op=ALU.add,
            )

        nc.gpsimd.memset(w4_plane_in[:].bitcast(I32), 0)
        nc.gpsimd.memset(r8_plane_in[:].bitcast(I32), 0)
        nc.gpsimd.memset(v8_plane[:].bitcast(I32), 0)
        load_x(0)
        load_plane(w4_plane_in, w4_scales)
        load_w4(0)
        load_r8(0)
        load_x(1)
        load_plane(r8_plane_in, r8_scales)
        load_x(2)
        load_by_slot(cb_sb, cb)
        load_r8(1)
        load_by_slot(cw_sb, cw)
        load_x(3)
        nc.sync.dma_start(
            out=v8_sb[:].rearrange("p (a n) -> p a n", a=J_PASSES),
            in_=v8_words.rearrange("a p n i -> p a (n i)").bitcast(I32),
        )
        load_plane(v8_plane, v8_scales)
        with nc.allow_non_contiguous_dma(reason="one bias value for each partition"):
            nc.sync.dma_start(out=b_sb[:], in_=b.rearrange("(n p) -> p n", p=P))

        round_x_on_scalar(0, 0, 48)
        round_x_on_vector(0, 48, 80)
        sort_plane(w4_plane[0][:], w4_plane_in[:, :PASS])
        quantize_x(0)
        sort_w4(0, nc.vector.tensor_copy, slice(0, 2))
        sort_w4(0, nc.vector.tensor_copy, slice(2, 4))
        sort_w4(1, nc.scalar.copy)
        sort_plane(w4_plane[1][:], w4_plane_in[:, PASS:])
        sort_r8(0, nc.scalar.copy)
        slots_in_bank = {u: place_d(u) for u in range(4)}
        for u in (0, 2):
            for i in range(SLOTS):
                w4_pass(u, i, slots_in_bank[u])
        round_x_on_scalar(1, 0, 64)
        round_x_on_vector(1, 64, 64)
        sort_plane(r8_plane[0][:], r8_plane_in[:, :PASS], slice(0, SLOTS // 2))
        sort_plane(r8_plane[0][:], r8_plane_in[:, :PASS], slice(SLOTS // 2, SLOTS))

        quantize_x(1)
        for i in range(SLOTS):
            r8_pass(0, i, slots_in_bank[0])
        for i in range(SLOTS):
            w4_pass(1, i, slots_in_bank[1])
            r8_pass(1, i, slots_in_bank[1])
        for i in range(SLOTS):
            w4_pass(3, i, slots_in_bank[3])
        sort_plane(r8_plane[1][:], r8_plane_in[:, PASS:])
        round_x_on_vector(2)
        quantize_x(2)
        sort_r8(1, nc.vector.tensor_copy, slice(0, 2))
        sort_r8(1, nc.vector.tensor_copy, slice(2, 4))
        for i in range(SLOTS):
            r8_pass(2, i, slots_in_bank[2])

        for i in range(SLOTS):
            r8_pass(3, i, slots_in_bank[3])
        for u in range(D_TILES):
            square(u)
            weigh(u)
            if u == 1:
                round_x_on_vector(3)
                quantize_h(0, 2)
                quantize_x(3)
            if 0 < u < D_TILES - LEAD:
                first_product(u + LEAD)
            if u == 4:
                quantize_h(u - 2, 2)
            if u == 4:
                y_pass(0, 0)
                y_pass(0, 1)
            if u > 4:
                quantize_h(u - 1, 1)
                y_pass(1 + (u - 5) // 2, (u - 5) % 2)
        quantize_h(D_TILES - 1, 1)
        y_pass(2, 1)
        for m in range(4):
            add_bias_on_scalar(0, m)
            store(0, m, 1)
        for m in range(2):
            add_bias_on_scalar(1, m)
        store(1, 0, 2)
        add_bias_on_vector(1, 2)
        store(1, 2, 2)
        for m in range(2):
            add_bias_on_scalar(2, m)
            store(2, m, 1)
        add_bias_on_vector(2, 2)
        store(2, 2, 2)
